import numpy as np, ml_dtypes
CORES = [16,18,20,22]
N = 4
import mx_ref
BF = ml_dtypes.bfloat16
def gcols(t, e):
    v = np.concatenate([t.reshape(8, 16, -1, 4), np.zeros((8, 16, 1, 4), BF)], axis=2)
    return np.ascontiguousarray(np.stack([v[g][:, e[g]] for g in range(8)])).reshape(128, -1)
def tile(rs):
    return np.stack(rs, axis=2).reshape(128, -1).astype(BF)
def pick(q, e):
    c = np.concatenate([q[0].reshape(128, -1, 4), np.zeros((128, 1, 4), np.uint8)], axis=1); s = np.concatenate([q[1], np.ones((16, 1), np.uint8)], axis=1)
    return (np.ascontiguousarray(c[:, e].reshape(128, -1)), np.ascontiguousarray(s[:, e]))
def join(*qs):
    return (np.concatenate([q[0] for q in qs], axis=1), np.concatenate([q[1] for q in qs], axis=1))
def put(q, e, v):
    c, s = q[0].reshape(128, -1, 4).copy(), q[1].copy(); c[:, e] = v[0].reshape(128, -1, 4); s[:, e] = v[1]
    return (c.reshape(128, -1), s)
def pk(c, s):
    return (np.ascontiguousarray(c), mx_ref.live(s))
def emit(q):
    return q[0], q[1]
def packed(v, rng):
    q = [mx_ref.quantize(np.ascontiguousarray(v[r])) for r in range(N)]
    return np.stack([a for a, b in q]), np.stack([mx_ref.plane(b, rng) for a, b in q])
def values_of_codes():
    e, c = np.zeros((128, 128, 4), np.float32), np.zeros((128, 2, 4), np.uint8)
    e[np.arange(128), np.arange(128), 0] = 1
    c[:127, :, 0] = np.arange(256).reshape(2, 128).T[:127]
    return mx_ref.matmul(mx_ref.quantize(e.reshape(128, 512).astype(BF)), (c.reshape(128, 8), np.full((16, 2), 127, np.uint8))).T.reshape(-1).astype(np.float64)
CODE_VALUE, SCALE_VALUE = values_of_codes(), 2.0 ** (np.arange(256) - 127.0)
def decode(q):
    return (CODE_VALUE[q[0]].reshape(16, 8, -1, 4) * SCALE_VALUE[q[1]][:, None, :, None] + 0.0).reshape(128, -1).astype(np.float32)
def f(rng, *shape):
    return mx_ref.flush((rng.standard_normal(shape, dtype=np.float32) * np.exp2(rng.integers(-2, 3, shape[:-1] + (1,)))).astype(BF))
def wide(rng, *shape, cols=0):
    v = rng.standard_normal(shape, dtype=np.float32) * np.exp2(rng.integers(-12, 13, shape)).astype(np.float32)
    if cols: v *= np.repeat(np.exp2(rng.integers(-cols, cols + 1, shape[:-2] + (1, shape[-1] // 4))) * (rng.random(shape[:-2] + (1, shape[-1] // 4)) > 0.0625), 4, axis=-1).astype(np.float32)
    return mx_ref.flush(v.astype(BF))
C, M, R = 448, 192, 3
def meet(n):
    i = np.arange(n)
    q = np.stack([i] * 4 + [n - 1 - i] * 4)
    for h in range(1, 8):
        k = n // 2 if h < 4 else n // 2 - 1
        q[h, [h - 1, k]] = q[h, [k, h - 1]]
    q[4, [0, 1, 2, n - 1, n - 2, n - 3]] = q[4, [n - 1, n - 2, n - 3, 0, 1, 2]]
    return q
def big(v):
    v = v.astype(np.float32)
    v[np.abs(v) < np.float32(2.0 ** -16)] = 0
    return v.astype(BF)
def numbers_of(rng):
    return {"x": big(f(rng, N, 128, 4 * C)), "u": np.array(f(rng, N, 128, 512)), "v": np.array(f(rng, N, 128, 512))}
def layers(rng, still=[]):
    w = (rng.random((N, 128, 2048)) * 2.0 - 1.0) * 0.054 * np.exp2(-rng.integers(0, 2, (N, 128, 1)))
    w = big(w).reshape(N, 8, 16, 4, 8, 16, 4)
    for i in still:
        w[:, :, i] = 0
        w[:, :, :, :, :, i] = 0
    return w
def weights(rng, w):
    c, p = packed(np.ascontiguousarray(w).reshape(N, 128, 2048), rng)
    return {"wc": c, "ws": p}
def setup_inputs(rng):
    return {**numbers_of(rng), **weights(rng, layers(rng))}
def setup_inputs_ties(rng):
    d = numbers_of(rng)
    x = d["x"].reshape(N, 8, 16, C, 4)
    x[:, :, 0] = 0
    x[:, :, 0, :, 0] = rng.integers(1, 4, (N, 8, C)).astype(np.float32).astype(BF)
    u = d["u"].reshape(N, 128, 128, 4)
    one = u[:, :, :1].copy()
    one[:, :8] = 0
    u[:, :, ::16] = 0
    o = rng.permutation(N)
    for r in range(N):
        if o[r] == 2:
            u[r, :, ::16] = one[r]
            s = mx_ref.matmul(mx_ref.quantize(np.ascontiguousarray(u[r].reshape(128, 512))), mx_ref.quantize(np.ascontiguousarray(x[r].reshape(128, 4 * C))))[0]
            x[r, 0, 0] = 0
            x[r, 0, 0, np.argsort(-s, kind="stable")[C // 2], 0] = 2.0
            u[r, 0, 0, 0] = -2.0 ** 20
        else:
            for h in range(0, 128, 16): u[r, h, h, 0] = 0.0 if o[r] == 0 else -1.0 if o[r] == 1 else 1.0
    return {"x": x.reshape(N, 128, 4 * C), "u": u.reshape(N, 128, 512), "v": d["v"], **weights(rng, layers(rng, [0]))}
def setup_inputs_near(rng):
    d = numbers_of(rng)
    x = d["x"].astype(np.float32).reshape(N, 8, 16, C, 4)
    u = d["u"].reshape(N, 128, 128, 4)
    x[:, :, 0] = 0
    x[:, :, 8:] = 0
    u[:, :, ::16] = 0
    o = rng.permutation(N) % 4
    for r in range(N):
        k = 1.0 if o[r] == 0 else 2.0 ** -30
        if o[r] < 2:
            x[r, :, 0, :, 0] = rng.integers(0, 2, (8, C)) * 2.0 - 1.0
            x[r, :, 11, :, 0] = 2.0 ** -10
        if o[r] == 2:
            e = np.argsort(rng.random((8, C)), axis=1)
            x[r, :, 0, :, 0] = np.where(e < C // 16, 1.0, np.where(e < C // 8, -1.0, 0.0))
        if o[r] < 3:
            s = rng.integers(0, 16, (8, C))
            x[r, :, 8] = ((s[:, :, None] >> np.arange(4)) & 1) * np.exp2(np.arange(4) - 23.0)
        else:
            a = rng.integers(0, 4, (8, C))
            x[r, :, 10, :, 0] = np.array([1.0, 0.0, -1.0, 0.0])[a] * 2.0 ** -27
            x[r, :, 10, :, 1] = np.array([0.0, 1.125, 1.125, 0.0])[a] * 2.0 ** -27
        for h in range(0, 128, 16):
            if o[r] < 2:
                u[r, h, h, 0] = k
                u[r, h + 11, h, 0] = k
            if o[r] == 2: u[r, h, h, 0] = 1.0
            if o[r] < 3: u[r, h + 8, h] = k
            else:
                u[r, h + 10, h, 0] = 1.25 * k
                u[r, h + 10, h, 1] = 1.125 * k
    return {"x": x.reshape(N, 128, 4 * C).astype(BF), "u": u.reshape(N, 128, 512), "v": d["v"], **weights(rng, layers(rng, [0, 8, 9, 10, 11, 12, 13, 14, 15]))}
def setup_inputs_odd(rng):
    d = numbers_of(rng)
    a = (1.0 + (2 * rng.integers(0, 64, (N, 8, 2, C, 32)) + 1) * 2.0 ** -7) * np.exp2(-rng.integers(8, 15, (N, 8, 2, C, 32))) * (rng.integers(0, 2, (N, 8, 2, C, 32)) * 2.0 - 1.0)
    e = rng.integers(0, 32, (N, 8, 2, C, 1))
    np.put_along_axis(a, e, 1.96875 * (rng.integers(0, 2, (N, 8, 2, C, 1)) * 2.0 - 1.0), axis=4)
    a *= np.exp2(rng.integers(-1, 3, (N, 8, 2, C, 1)))
    d["x"] = np.ascontiguousarray(a.reshape(N, 8, 2, C, 8, 4).transpose(0, 1, 2, 4, 3, 5)).reshape(N, 128, 4 * C).astype(np.float32).astype(BF)
    return {**d, **weights(rng, layers(rng))}
def setup_inputs_ends(rng):
    d = numbers_of(rng)
    e = rng.permutation(N)
    o = e % 4
    x = (0.9 + 0.1 * rng.random((N, 8, 16, C, 4))) * 2.0 ** 30
    x[:, :, 8:] = 2.0 ** -27 * (rng.integers(0, 2, (N, 8, 8, C, 4)) * 2.0 - 1.0)
    u, v = d["u"].reshape(N, 128, 128, 4), d["v"]
    w = np.zeros((N, 8, 16, 4, 8, 16, 4), np.float32)
    for r in range(N):
        a = np.zeros((8, 16, 8, 4))
        if o[r] == 0: x[r] = -2.0 ** 30 * (0.9 + 0.1 * rng.random((8, 16, C, 4)))
        if o[r] == 1: x[r, :, :8] *= rng.integers(0, 2, (1, 1, C, 1)) * 2.0 - 1.0
        if o[r] == 2: x[r, :, :8] *= rng.integers(0, 2, (8, 8, C, 4)) * 2.0 - 1.0
        if o[r] == 3:
            q = meet(C)[rng.permutation(8)] if e[r] == 3 else np.stack([C - 1 - np.arange(C)] * 8)
            x[r, :, :8] *= rng.integers(0, 2, (8, 1, C, 1)) * 2.0 - 1.0
            x[r, :, 0] = 0
            x[r, :, 0, :, :3] = (((C - 1 - q)[:, :, None] >> np.array([0, 3, 6])) & 7) * 2.0 ** 27
            for g in range(0 if e[r] == 3 else 4, 8): a[g, 0, g, :3] = 2.0 ** 20 * np.array([1.0, 8.0, 64.0])
        if o[r] == 0: a = 2.0 ** 30 * (1.0 - 0.1 * rng.random((8, 16, 8, 4)))
        if o[r] == 1:
            a[:, :8] = 2.0 ** 30 * (1.0 - 0.1 * rng.random((8, 8, 8, 4)))
            a *= (rng.permutation(8) % 2 * 2.0 - 1.0)[None, None, :, None]
        if o[r] == 2: a[:, 8:] = 2.0 ** -30 * (rng.integers(0, 2, (8, 8, 8, 4)) * 2.0 - 1.0)
        u[r, :, ::16] = a.reshape(128, 8, 4).astype(np.float32).astype(BF)
        if o[r] == 0: w[r, :, :8, :, :, :8] = 0.0546875
        if o[r] in (1, 3): w[r, :, :8, :, :, :8] = 0.0546875 * (rng.integers(0, 2, (8, 8, 4, 8, 8, 4)) * 2.0 - 1.0)
        if o[r] == 0: v[r] = 2.0 ** 30
        if o[r] == 1: v[r] = (2.0 ** 30 * (rng.integers(0, 2, (128, 512)) * 2.0 - 1.0)).astype(np.float32).astype(BF)
        if o[r] == 2: v[r] = (2.0 ** -30 * (rng.integers(0, 2, (128, 512)) * 2.0 - 1.0)).astype(np.float32).astype(BF)
    return {"x": x.astype(np.float32).reshape(N, 128, 4 * C).astype(BF), "u": u.reshape(N, 128, 512), "v": v, **weights(rng, w.astype(BF))}
def setup_inputs_spread(rng):
    d = setup_inputs(rng)
    d["x"] = big(wide(rng, N, 128, 4 * C, cols=6))
    return d
def check_inputs(d):
    b = []
    for k, low in (("x", 2.0 ** -27), ("u", 2.0 ** -30), ("v", 2.0 ** -30)):
        a = np.abs(d[k].astype(np.float32))
        if not (np.isfinite(a).all() and ((a == 0) | (a >= low) & (a <= 2.0 ** 30)).all()): b.append("a value of " + k)
    none, least, most = [emit(mx_ref.quantize(np.full((128, 16), k, np.float32).astype(BF)))[1][0, 0] for k in (0.0, 2.0 ** -16, 2.0 ** -5)]
    for r in range(N):
        if ((d["wc"][r] == 0x7F) | (d["wc"][r] == 0xFF)).any(): b.append("wc: a code that is no number")
        s = mx_ref.live(d["ws"][r])
        if ((s != none) & ((s < least) | (s > most))).any(): b.append("ws: a scale out of range")
        if not (np.abs(decode(pk(d["wc"][r], d["ws"][r]))) < 2.0 ** -4).all(): b.append("wc, ws: a number of W that isn't below 2**-4 in size")
    return b
def reference(x, u, v, wc, ws):
    qu = [mx_ref.quantize(u[r]) for r in range(N)]
    lay = [pk(wc[r], ws[r]) for r in range(N)]
    now = [x[r] for r in range(N)]
    l, own = [None] * N, [None] * N
    for t in range(R):
        y, z = [], []
        for r in range(N):
            q = mx_ref.quantize(now[r])
            d = decode(q).astype(BF)
            s = mx_ref.matmul(qu[r], q)[::16] + np.float32(0.0)
            o = np.argsort(-s, axis=1, kind="stable")
            place = np.argsort(o, axis=1, kind="stable")
            m = np.sort(place, axis=0)
            l[r] = np.where(place <= m[3], o[:, m[4]], o[:, m[3]])
            c = np.argsort(m[0] - m[7], kind="stable")[:M]
            own[r] = l[r][:, c]
            z.append(mx_ref.quantize(gcols(d, own[r])))
            y.append(((now[r].astype(np.float32) + gcols(d, l[r]).astype(np.float32)) * np.float32(0.5)).astype(BF))
        for r in range(N):
            came = z[(r - 1 - t) % N]
            h = tile([mx_ref.matmul(pick(lay[r], np.arange(128 * b, 128 * b + 128)), came) * np.float32(0.03125) for b in range(4)])
            first = np.full((8, C), M)
            np.minimum.at(first, (np.arange(8)[:, None], own[r]), np.arange(M)[None])
            now[r] = gcols(np.concatenate([y[r], h], axis=1), np.where(first < M, C + first, np.arange(C)[None]))
    y, ol = np.zeros((N, 128, C), np.float32), np.zeros((N, 8, C), np.float32)
    oc, osc = np.zeros((N, 128, 4 * C), np.uint8), np.zeros((N, 16, C), np.uint8)
    for r in range(N):
        q = mx_ref.quantize(now[r])
        y[r] = mx_ref.matmul(mx_ref.quantize(v[r]), q)
        ol[r] = l[r]
        oc[r], osc[r] = emit(q)
    return {"y": y, "ol": ol, "oc": oc, "osc": osc}

@@ -1,0 +1,521 @@
+from concourse.mybir import dt, AluOpType, ActivationFunctionType
+
+C, M, R, NS, MS = 448, 192, 3, 28, 12
+MAGIC = 12582912.0
+QN = [128, 128, 176, 240, 304, 368, 448]
+BYSIGN = (24, 20, 19, 16, 12)
+OP = AluOpType
+AF = ActivationFunctionType
+
+SCRATCH = {}
+ALIAS = {}
+
+
+def _sb(name, n, d):
+    SCRATCH[name] = ("sbuf", [128, n], d)
+
+
+def _mx(name, n):
+    _sb("q" + name, n, "float8_e4m3fn_x4")
+    _sb("s" + name, n, "uint8")
+
+
+def _pack(buf, d, parts):
+    at = 0
+    for n, w in parts:
+        ALIAS[n] = (buf, at, w)
+        at += (w + 15) // 16 * 16
+    _sb(buf, at, d)
+
+
+def _packmx(buf, parts):
+    at = 0
+    for n, w in parts:
+        ALIAS["q" + n] = ("q" + buf, at, w)
+        ALIAS["s" + n] = ("s" + buf, at, w)
+        at += w
+    _mx(buf, at)
+
+
+for _n in ("xa", "xb", "ft", "cr", "tl"):
+    _sb(_n, 4 * C, "bfloat16")
+_sb("ut", 512, "bfloat16")
+_sb("vt", 512, "bfloat16")
+_pack("kt", "bfloat16", [(n, 512) for n in ("ctile", "cneg", "fb", "sgt", "fst", "mst", "ont", "et0", "et1", "et2", "et3")])
+_pack("tb", "bfloat16", [("t%d" % b, C) for b in range(4)])
+_pack("yh", "bfloat16", [("yh%d" % b, C + M) for b in range(4)])
+_pack("ctb", "bfloat16", [("ct%d" % q, 4 * QN[q]) for q in range(7)])
+_pack("kb", "bfloat16", [("mk", C), ("rst", C), ("iotaj", C), ("mlt", M), ("kv", M), ("i16", C), ("jwm", C), ("jwf", C)])
+_pack("sgn", "bfloat16", [("sgn%d" % k, 16 * k) for k in BYSIGN])
+_packmx("k", [(n, 128) for n in ("e0", "e1", "e2", "e3", "sg", "fs", "ms", "on")])
+_packmx("c", [("c%d" % q, QN[q]) for q in range(7)])
+for _n, _w in (("u", 128), ("ux", 128), ("v", 128), ("w", 512), ("x", C), ("f", C), ("mv", 224), ("cr", C)):
+    _mx(_n, _w)
+for _t in range(R):
+    _mx("tl%d" % _t, C)
+    _mx("z%d" % _t, M)
+    _mx("a%d" % _t, M)
+for _n, _w in (("junk0", C), ("junk1", C), ("junk2", C), ("ot", C), ("la", C), ("lm", C), ("lf", C), ("ctab", C), ("cm", M), ("cf", M), ("lk", M), ("lkm", M),
+               ("lkf", M), ("rep2", M), ("eqd", M), ("eqm", M), ("df", M), ("eqo", 12 * 192), ("st", C + M), ("stm", C), ("stf", C), ("rfb", C), ("em2", C),
+               ("rf", C), ("dg", 112), ("mv", 896), ("m8", 112), ("lo", 112), ("hi", 112), ("gx", 56), ("gy", 56), ("gg", 224)):
+    _sb(_n, _w, "bfloat16")
+for _n in ("sm", "swf", "rep", "em", "ef", "iot512", "kca", "ka", "yo", "olf"):
+    _sb(_n, C, "float32")
+_pack("fk", "float32", [("cst", NS), ("onef", 32), ("gm", 8), ("mb", 32), ("rst8", 32), ("kc", NS), ("j448", NS), ("nt", MS)])
+_pack("fw", "float32", [("rs", NS), ("rsc", NS), ("z", NS), ("x1", NS), ("kw", NS), ("km", 32), ("kf", 32), ("aa", 112), ("bb", 112), ("a2", 56), ("b2", 56),
+                        ("av", NS), ("bv", NS), ("mn", NS), ("mxv", NS), ("spr", NS), ("sp5", NS), ("ab", NS), ("c1", NS), ("c2", NS), ("tg", NS),
+                        ("dc", MS), ("dup", MS), ("dp1", MS), ("ntf", MS), ("lk2", MS), ("offf", MS), ("sx2", NS)])
+_pack("ki", "int32", [("ia", C), ("ib", C), ("if1", NS), ("if2", 8)])
+for _n, _w in (("offrep", NS), ("offu", 8), ("offq", NS), ("offt", NS), ("offs", NS), ("offr", NS), ("offc", MS), ("offl", NS), ("offd", MS), ("offx", NS)):
+    _sb(_n, _w, "uint16")
+for _n in ("pss", "psa", "psm", "psr", "pd0", "pd1", "pd2", "pd3"):
+    SCRATCH[_n] = ("psum", [128, 512], "float32")
+
+SEMAPHORES = ["sv", "ss", "sg", "st"] + ["arr%d" % t for t in range(R)] + ["snd%d" % t for t in range(R)] + ["d%d" % i for i in range(24)]
+
+
+def make_queues(g, T):
+    eng = {"v": g.vector, "s": g.scalar, "g": g, "t": g.tensor, "y": g.sync}
+    sem = {"v": "sv", "s": "ss", "g": "sg", "t": "st"}
+    count = {k: 0 for k in sem}
+    known = {k: {} for k in eng}
+    snap = {}
+    log = {}
+    ndma = [0]
+
+    def psum(v):
+        return SCRATCH[v[0]][0] == "psum"
+
+    def region(v):
+        return (0, 512, 1) if psum(v) else (v[1], v[2], v[3])
+
+    def hit(p, q):
+        if p[0] >= q[1] or q[0] >= p[1]:
+            return False
+        return not (p[2] == q[2] and p[2] > 1 and (p[0] - q[0]) % p[2])
+
+    def wait(e, src, n):
+        if known[e].get(src, 0) >= n:
+            return
+        eng[e].wait_ge(T.sem[sem.get(src, src)], n)
+        known[e][src] = n
+        for k, m in snap.get((src, n), {}).items():
+            if known[e].get(k, 0) < m:
+                known[e][k] = m
+
+    def deps(e, outs, ins):
+        need = {}
+        for write, vs in ((True, outs), (False, ins)):
+            for v in vs:
+                r = region(v)
+                for w2, r2, src, n in log.get(v[0], []):
+                    if not hit(r, r2) or (e == "t" and src == "t"):
+                        continue
+                    if write or w2 or (psum(v) and src != e):
+                        need[src] = max(need.get(src, 0), n)
+        for src in sorted(need):
+            wait(e, src, need[src])
+
+    def record(outs, ins, src, n):
+        for write, vs in ((True, outs), (False, ins)):
+            for v in vs:
+                r = region(v)
+                L = log.setdefault(v[0], [])
+                if write and not psum(v) and r[2] == 1:
+                    L[:] = [x for x in L if not (r[0] <= x[1][0] and x[1][1] <= r[1])]
+                L[:] = [x for x in L if not (x[0] == write and x[1] == r and x[2] == src)]
+                L.append((write, r, src, n))
+
+    def ap(v):
+        x = T[v[0]][:, v[1]:v[2]:v[3]] if v[3] > 1 else T[v[0]][:, v[1]:v[2]]
+        if len(v) > 4:
+            if v[5] == "codes":
+                x = x.bitcast(dt.uint32)
+            if v[4] is not None:
+                o = v[4]
+                x = x.indirect(T[o[0]][:, o[1]:o[2]])
+        return x
+
+    def issue(e, outs, ins, call):
+        deps(e, outs, ins)
+        count[e] += 1
+        call().then_inc(T.sem[sem[e]], 1)
+        snap[(e, count[e])] = dict(known[e])
+        record(outs, ins, e, count[e])
+
+    def dma(e, out, in_, outs, ins, **kw):
+        deps(e, outs, ins)
+        name = "d%d" % ndma[0]
+        ndma[0] += 1
+        snap[(name, 16)] = dict(known[e])
+        eng[e].dma_start(out, in_, **kw).then_inc(T.sem[name], 16)
+        record(outs, ins, name, 16)
+
+    def finish():
+        for i in range(ndma[0]):
+            wait("g", "d%d" % i, 16)
+        for k in ("v", "s", "t", "g"):
+            wait("g", k, count[k])
+
+    return issue, dma, ap, wait, deps, finish
+
+
+def rank_program(g, core, T, topo):
+    rank = T.rank_of(core)
+    if rank is None:
+        return
+    issue, dma, ap, wait, deps, finish = make_queues(g, T)
+
+    def B(name, a=0, b=None, s=1):
+        if name in ALIAS:
+            buf, at, w = ALIAS[name]
+        else:
+            buf, at, w = name, 0, SCRATCH[name][1][1]
+        return (buf, at + a, at + (w if b is None else b), s)
+
+    def I(v, off, kind=""):
+        return v + (off, kind)
+
+    def srcs(*vs):
+        r = []
+        for v in vs:
+            r.append(v)
+            if len(v) > 4 and v[4] is not None:
+                r.append(v[4])
+        return r
+
+    def tt(out, a, b, op):
+        issue("v", [out], srcs(a, b), lambda: g.vector.tensor_tensor(ap(out), ap(a), ap(b), op))
+
+    def sc(out, a, s1, op0, s2=None, op1=None):
+        ins = srcs(a) + ([s1] if isinstance(s1, tuple) else [])
+        x1 = ap(s1) if isinstance(s1, tuple) else s1
+        if op1 is None:
+            issue("v", [out], ins, lambda: g.vector.tensor_scalar(ap(out), ap(a), x1, None, op0))
+        else:
+            issue("v", [out], ins, lambda: g.vector.tensor_scalar(ap(out), ap(a), x1, s2, op0, op1))
+
+    def scan(out, d0, d1, op0, op1):
+        issue("v", [out], [d0, d1], lambda: g.vector.tensor_tensor_scan(ap(out), ap(d0), ap(d1), 0.0, op0, op1))
+
+    def vcopy(out, a):
+        ins = srcs(a) + ([out[4]] if len(out) > 4 and out[4] is not None else [])
+        issue("v", [out], ins, lambda: g.vector.tensor_copy(ap(out), ap(a)))
+
+    def act(out, a, func=AF.Copy, scale=None, bias=None, acc=None):
+        kw = {}
+        ins, outs = srcs(a), [out]
+        for k, v in (("scale", scale), ("bias", bias)):
+            if v is not None:
+                kw[k] = ap(v) if isinstance(v, tuple) else v
+                if isinstance(v, tuple):
+                    ins.append(v)
+        if acc is not None:
+            kw["accum_out"] = ap(acc)
+            outs.append(acc)
+        issue("s", outs, ins, lambda: g.scalar.activation(ap(out), ap(a), func, **kw))
+
+    nj = [0]
+
+    def count_ones(acc, v, n):
+        nj[0] = (nj[0] + 1) % 3
+        act(B("junk%d" % nj[0], 0, n), v, acc=acc)
+
+    def fill(v, c):
+        issue("v", [v], [], lambda: g.vector.memset(ap(v), c))
+
+    def quant(name, n, tile):
+        src, o, s = B(tile, 0, 4 * n), B("q" + name, 0, n), B("s" + name, 0, n)
+        issue("v", [o, s], [src], lambda: g.vector.quantize_mx(ap(o), ap(s), ap(src)))
+
+    def mm(out, n, l, r, start=True, stop=True, la=0):
+        o = B(out, 0, n)
+        a, asc, b, bsc = B("q" + l, la, la + 128), B("s" + l, la, la + 128), B("q" + r, 0, n), B("s" + r, 0, n)
+        issue("t", [o], [a, asc, b, bsc], lambda: g.tensor.matmul_mx(ap(o), ap(a), ap(asc), ap(b), ap(bsc), start, stop))
+
+    def iota(v, pattern, base, cm):
+        kw = {} if SCRATCH[v[0]][2] == "int32" else {"allow_small_or_imprecise_dtypes": True}
+        issue("g", [v], [], lambda: g.iota(ap(v), pattern, base, cm, **kw))
+
+    def sel(out, in_, pattern, op, base, cm):
+        issue("g", [out], [in_], lambda: g.affine_select(ap(out), ap(in_), pattern, op, 0.0, base, cm))
+
+    def last16(name, n=C):
+        return B(name, 15, n, 16)
+
+    def mask(out, v, n=C):
+        scan(B(out, 0, n), v, B("mk", 0, n), OP.add, OP.mult)
+
+    def hold(out, m, n=C):
+        scan(B(out, 0, n), B("rst", 0, n), B(m, 0, n), OP.mult, OP.add)
+
+    dma("y", T["xa"][:, :], T.x[:, :], [B("xa")], [])
+    dma("s", T["ut"][:, :], T.u[:, :], [B("ut")], [])
+    dma("y", T["qw"][:, 0:512].bitcast(dt.uint8), T.wc[:, :], [B("qw")], [])
+    dma("s", T["sw"][:, :], T.ws[:, :], [B("sw")], [])
+    dma("y", T["vt"][:, :], T.v[:, :], [B("vt")], [])
+
+    def zeros(n):
+        w = ALIAS[n][2]
+        for a in range(0, w, 512):
+            act(B(n, a, min(a + 512, w)), B("ctile", 0, min(512, w - a)), scale=0.0)
+
+    iota(B("if2"), [[16, 8]], 0, 0)
+    iota(B("ia"), [[0, NS], [-1, 16]], 1024, 1)
+    iota(B("i16"), [[0, NS], [1, 16]], 0, 0)
+    iota(B("if1"), [[16, NS]], 15, 0)
+    fill(B("ctile"), 1.0)
+    zeros("ct6")
+    fill(B("ft"), 0.0)
+    for a, b in (("ct4", "ct4"), ("ct3", "ct3"), ("ct0", "ct2")):
+        n = ALIAS[b][1] + ALIAS[b][2] - ALIAS[a][1]
+        o, i = B(a, 0, n), B("ft", 0, n)
+        dma("y", ap(o), ap(i), [o], [i])
+    fill(B("cneg"), -1.0)
+    vcopy(B("offu"), B("if2"))
+    fill(B("fst"), 0.0)
+    sc(B("ib"), B("ia"), 15, OP.bitwise_and)
+    sc(B("mk"), B("ib"), 0.0, OP.is_equal)
+    sc(B("rst"), B("i16"), 1.0, OP.min)
+    vcopy(B("offrep"), B("if1"))
+    quant("u", 128, "ut")
+    vcopy(I(B("qux"), None, "codes"), I(B("qu"), B("offu"), "codes"))
+    act(B("sux"), I(B("su"), B("offu")))
+    quant("x", C, "xa")
+    zeros("ct5")
+
+    sel(B("fb"), B("cneg"), [[-16, 8], [0, 16], [0, 4]], OP.is_ge, 0, 1)
+    sel(B("sgt"), B("fb"), [[16, 8], [0, 16], [0, 4]], OP.is_ge, 15, -1)
+    l0, l1, one = B("fst", 0, 512, 4), B("fst", 1, 512, 4), B("ctile", 0, 128)
+    sel(l0, one, [[16, 8], [1, 16]], OP.is_gt, 0, -1)
+    sel(l0, l0, [[-16, 8], [0, 16]], OP.is_ge, 0, 1)
+    sel(l1, one, [[-16, 8], [-1, 16]], OP.is_gt, 0, 1)
+    sel(l1, l1, [[16, 8], [0, 16]], OP.is_ge, 15, -1)
+    iota(B("rs", 0, 1), [[0, 1]], 0, 0)
+    iota(B("dc", 0, 1), [[0, 1]], 0, 0)
+    iota(B("cst"), [[-16, NS]], 208, 0)
+    iota(B("iotaj"), [[1, C]], -224, 0)
+    iota(B("dg"), [[0, 112]], 0, 0)
+    iota(B("onef"), [[0, 32]], 1, 0)
+    sel(B("gm"), B("onef", 0, 8), [[-16, 8]], OP.is_ge, 0, 1)
+    sel(B("gm"), B("gm"), [[16, 8]], OP.is_ge, 15, -1)
+    sel(B("mb"), B("onef"), [[0, 4], [-16, 8]], OP.is_ge, 0, 1)
+    sel(B("mb"), B("mb"), [[0, 4], [16, 8]], OP.is_ge, 15, -1)
+    sel(B("rst8"), B("onef"), [[0, 4], [1, 8]], OP.is_gt, 0, 0)
+    for b in range(4):
+        sel(B("et%d" % b), B("ctile"), [[-4, 128], [-1, 4]], OP.is_equal, b, 4)
+    sel(B("ont"), B("ctile"), [[0, 128], [-1000, 4]], OP.is_ge, 2936, 1)
+    iota(B("iot512"), [[512, C]], 0, 0)
+    iota(B("kca"), [[-1, C]], C - 1, 0)
+    iota(B("kv"), [[1, M]], 0, 0)
+
+    def consts_last():
+        for e in range(4):
+            act(B("mst", e, 512, 4), B("mk", 0, 128))
+        mask("jwm", B("iotaj"))
+        hold("jwf", "jwm")
+        sc(B("j448"), last16("jwf"), -224.0, OP.add)
+        sc(B("kc"), last16("jwf"), -1.0, OP.mult, 223.0, OP.add)
+        sc(B("nt"), last16("jwf", M), 672.0, OP.add)
+        quant("ms", 128, "mst")
+        for b in range(4):
+            quant("e%d" % b, 128, "et%d" % b)
+        quant("on", 128, "ont")
+        hold("jwm", "mk", M)
+        sc(B("mlt"), B("jwm", 0, M), -1.0, OP.mult, 1.0, OP.add)
+        quant("v", 128, "vt")
+
+    X = ["xa", "xb"]
+    for t in range(R):
+        x, xn = X[t % 2], X[(t + 1) % 2]
+        first = t == 0
+        mm("pss", C, "ux", "x")
+        mm("psm", C, "ux", "x")
+        if not first:
+            for b in range(4):
+                mm("pd%d" % b, C, "e%d" % b, "x")
+        tt(B("sm"), B("pss", 0, C), B("mk"), OP.mult)
+        hold("swf", "sm")
+        if not first:
+            act(B("t0"), B("pd0", 0, C))
+
+        def signs(q):
+            for k in range(4 * q + 3, 4 * q - 1, -1):
+                if k in BYSIGN:
+                    act(B("sgn%d" % k), B("psm", 0, 16 * k), AF.Sign, scale=-1.0, bias=B("swf", 16 * k + 15, 16 * k + 16))
+
+        signs(6)
+        for q in (6, 5, 4, 3, 2, 1, 0):
+            for k in range(4 * q + 3, max(4 * q - 1, 0), -1):
+                c = B("ct%d" % q, k % 4, 64 * k, 4)
+                if k in BYSIGN:
+                    sc(c, B("sgn%d" % k), 0.0, OP.is_le)
+                else:
+                    sc(c, B("pss", 0, 16 * k), B("swf", 16 * k + 15, 16 * k + 16), OP.is_ge)
+                if k == 4 * q + 3:
+                    signs(q - 1)
+                count_ones(B("rs", k, k + 1), c, 16 * k)
+                if k == 23:
+                    act(B("rep"), I(B("swf"), B("offrep")))
+            if first and q == 6:
+                quant("sg", 128, "sgt")
+            quant("c%d" % q, QN[q], "ct%d" % q)
+            mm("psa", QN[q], "sg", "c%d" % q, q == 6, q == 0)
+            if q == 4:
+                if first:
+                    quant("fs", 128, "fst")
+                tt(B("ft", 0, 4 * C, 4), B("pss", 0, C), B("rep"), OP.is_le)
+                tt(B("ft", 1, 4 * C, 4), B("pss", 0, C), B("rep"), OP.is_lt)
+                quant("f", C, "ft")
+                mm("psa", C, "fs", "f", False, False)
+            if q == 1 and first:
+                consts_last()
+        if first:
+            for b in range(4):
+                mm("pd%d" % b, C, "e%d" % b, "x")
+            act(B("t0"), B("pd0", 0, C))
+        act(B("t1"), B("pd1", 0, C))
+        tt(B("em"), B("psa", 0, C), B("mk"), OP.mult)
+        tt(B("rsc"), B("rs"), B("cst"), OP.add)
+        hold("ef", "em")
+        tt(B("z"), last16("ef"), B("rsc"), OP.add)
+        sc(B("x1"), B("z"), 0.0625, OP.mult, MAGIC, OP.add)
+        sc(B("offq"), B("z"), 224.0, OP.add)
+        sc(B("dg", 0, 112, 4), B("x1"), -MAGIC, OP.add, 16.0, OP.mult)
+        tt(B("dg", 1, 112, 4), B("z"), B("dg", 0, 112, 4), OP.subtract)
+        for gr in range(4):
+            act(B("mv", 112 * (gr + 4), 112 * (gr + 5)), B("dg"), scale=B("gm", gr + 4, gr + 5))
+            sc(B("mv", 112 * gr, 112 * (gr + 1)), B("dg"), B("gm", gr, gr + 1), OP.mult)
+        quant("mv", 224, "mv")
+        mm("psm", 224, "ms", "mv")
+        act(B("t2"), B("pd2", 0, C))
+        act(B("t3"), B("pd3", 0, C))
+        vcopy(I(B("ot"), B("offq")), B("iotaj"))
+        vcopy(B("m8"), B("psm", 112, 224))
+        tt(B("lo"), B("psm", 0, 112), B("m8"), OP.min)
+        tt(B("hi"), B("psm", 0, 112), B("m8"), OP.max)
+        tt(B("gg", 0, 56), B("lo", 0, 56), B("lo", 56, 112), OP.min)
+        tt(B("gg", 168, 224), B("hi", 0, 56), B("hi", 56, 112), OP.max)
+        tt(B("mn"), B("gg", 0, 28), B("gg", 28, 56), OP.min)
+        tt(B("mxv"), B("gg", 168, 196), B("gg", 196, 224), OP.max)
+        tt(B("gx"), B("lo", 0, 56), B("lo", 56, 112), OP.max)
+        tt(B("spr"), B("mxv"), B("mn"), OP.subtract)
+        tt(B("gy"), B("hi", 0, 56), B("hi", 56, 112), OP.min)
+        sc(B("offs"), B("spr"), 0.0, OP.add)
+        sc(B("sp5"), B("spr"), 512.0, OP.mult)
+        tt(B("ka"), I(B("iot512"), B("offs")), B("kca"), OP.add)
+        tt(B("kw"), B("sp5"), B("kc"), OP.add)
+        tt(B("gg", 56, 112), B("gx"), B("gy"), OP.min)
+        tt(B("km", 0, 24), B("kw", 0, 24), B("mb", 0, 24), OP.mult)
+        tt(B("km", 24, 32), B("kw", 20, 28), B("mb", 24, 32), OP.mult)
+        tt(B("gg", 112, 168), B("gx"), B("gy"), OP.max)
+        scan(B("kf"), B("rst8"), B("km"), OP.mult, OP.add)
+        for e in range(4):
+            act(B("cr", e, 4 * C, 4), B("ka"), AF.Sign, scale=-1.0, bias=B("kf", 8 * e + 7, 8 * e + 8))
+        for r in range(4):
+            p, o = B("gg", 56 * r, 56 * r + 28), B("gg", 56 * (3 - r) + 28, 56 * (3 - r) + 56)
+            tt(B("aa", 28 * r, 28 * r + 28), p, o, OP.min)
+            tt(B("bb", 28 * r, 28 * r + 28), p, o, OP.max)
+        tt(B("a2"), B("aa", 0, 56), B("aa", 56, 112), OP.max)
+        tt(B("b2"), B("bb", 0, 56), B("bb", 56, 112), OP.min)
+        tt(B("av"), B("a2", 0, 28), B("a2", 28, 56), OP.max)
+        tt(B("bv"), B("b2", 0, 28), B("b2", 28, 56), OP.min)
+        tt(B("c1"), B("z"), B("av"), OP.max)
+        tt(B("ab"), B("av"), B("bv"), OP.add)
+        tt(B("c2"), B("c1"), B("bv"), OP.min)
+        tt(B("tg"), B("ab"), B("c2"), OP.subtract)
+        sc(B("offt"), B("tg"), 224.0, OP.add)
+        quant("cr", C, "cr")
+        mm("psr", C, "on", "cr")
+        act(B("rfb"), B("psr", 0, C), AF.Identity, scale=0.5, bias=-0.5)
+        vcopy(B("la"), I(B("ot"), B("offt")))
+        mask("lm", B("la"))
+        hold("lf", "lm")
+        mask("em2", B("rfb"))
+        sc(B("offl"), last16("lf"), 224.0, OP.add)
+        for b in range(4):
+            act(B("tl", b, 4 * C, 4), I(B("t%d" % b), B("offl")))
+        hold("rf", "em2")
+        sc(B("offr"), last16("rf"), 224.0, OP.add)
+        vcopy(I(B("ctab"), B("offr")), B("iotaj"))
+        mask("cm", B("ctab", 0, M), M)
+        hold("cf", "cm", M)
+        sc(B("offc"), last16("cf", M), 224.0, OP.add)
+        n_tl, n_z, n_a = "tl%d" % t, "z%d" % t, "a%d" % t
+        act(B("lk"), I(B("la"), B("offc")))
+        quant(n_tl, C, "tl")
+        act(B("s" + n_z), I(B("s" + n_tl), B("offc")))
+        vcopy(I(B("q" + n_z), None, "codes"), I(B("q" + n_tl), B("offc"), "codes"))
+        to = T.cores[(rank + 1 + t) % len(T.cores)]
+        rid, pid, _se = topo.addr(to)
+        en = topo.engines(core, to)
+        wide, thin = en[0::2], en[1::4]
+        got = len(wide) + len(thin)
+        for nm, view, es in (("s", lambda n: T["s" + n][:, 0:M], thin), ("q", lambda n: T["q" + n][:, 0:M].bitcast(dt.uint8), wide)):
+            deps("g", [], [B(nm + n_z)])
+            g.remote_dma(view(n_a), view(n_z), T.sem["arr%d" % t], T.sem["snd%d" % t], pid, rid, sum(1 << e for e in es))
+        dma("g", T[x][:, :], T["tl"][:, :], [B(x)], [B("tl")], accum_op=OP.add)
+        iota(B("st", 0, C), [[0, C]], -512, 0)
+        mask("lkm", B("lk"), M)
+        hold("lkf", "lkm", M)
+        act(B("rep2"), I(B("lkf"), B("offrep", 0, MS)))
+        for k in range(MS - 1, 0, -1):
+            e = B("eqo", 192 * k, 192 * k + 16 * k)
+            sc(e, B("lk", 0, 16 * k), B("lkf", 16 * k + 15, 16 * k + 16), OP.is_equal)
+            count_ones(B("dc", k, k + 1), e, 16 * k)
+        if t == R - 1:
+            act(B("olf"), B("la"), AF.Identity, bias=224.0)
+            dma("y", T.ol[:, :], T["olf"][0:128:16, :], [], [B("olf")])
+        tt(B("eqd"), B("lk"), B("rep2"), OP.is_equal)
+        scan(B("eqm"), B("eqd"), B("mlt"), OP.max, OP.mult)
+        sc(B("lk2"), last16("lkf", M), 224.0, OP.add)
+        scan(B("df"), B("rst", 0, M), B("eqm"), OP.mult, OP.max)
+        tt(B("dup"), B("dc"), last16("df", M), OP.max)
+        sc(B("dp1"), B("dup"), 1.0, OP.min)
+        tt(B("ntf"), B("dp1"), B("nt"), OP.mult)
+        tt(B("offf"), B("ntf"), B("lk2"), OP.max)
+        sc(B("offd"), B("offf"), 0.0, OP.add)
+        vcopy(I(B("st"), B("offd")), B("kv"))
+
+        def halve(b):
+            o, i = B("yh%d" % b, 0, C), B(x, b, 4 * C, 4)
+            if b % 2:
+                act(o, i, scale=0.5)
+            else:
+                sc(o, i, 0.5, OP.mult)
+
+        halve(1)
+        halve(3)
+        mask("stm", B("st", 0, C))
+        halve(0)
+        hold("stf", "stm")
+        halve(2)
+        tt(B("sx2"), last16("stf"), B("j448"), OP.max)
+        wait("t", "arr%d" % t, got)
+        for b in range(4):
+            mm("pd%d" % b, M, "w", n_a, la=128 * b)
+        for b in range(4):
+            h, pd = B("yh%d" % b, C, C + M), B("pd%d" % b, 0, M)
+            if b % 2:
+                act(h, pd, scale=0.03125)
+            else:
+                sc(h, pd, 0.03125, OP.mult)
+            if b == 0:
+                sc(B("offx"), B("sx2"), 448.0, OP.add)
+        for b in range(4):
+            o, w = B(xn, b, 4 * C, 4), I(B("yh%d" % b), B("offx"))
+            if b % 2:
+                act(o, w)
+            else:
+                vcopy(o, w)
+        quant("x", C, xn)
+    mm("pss", C, "v", "x")
+    act(B("yo"), B("pss", 0, C))
+    dma("y", T.oc[:, :], T["qx"][:, 0:C].bitcast(dt.uint8), [], [B("qx")])
+    for k in range(4):
+        dma("y", T.osc[4 * k:4 * k + 4, :], T["sx"][32 * k:32 * k + 4, 0:C], [], [B("sx")])
+    dma("s", T.y[:, :], T["yo"][:, :], [], [B("yo")])
+    for t in range(R):
+        wait("g", "arr%d" % t, got)
+        wait("g", "snd%d" % t, got)
+    finish()

@@ -1,9 +1,11 @@
 from concourse.mybir import dt, AluOpType, ActivationFunctionType
 
 C, M, R, NS, MS = 448, 192, 3, 28, 12
-MAGIC = 12582912.0
-QN = [128, 128, 176, 240, 304, 368, 448]
-BYSIGN = (24, 20, 19, 16, 12)
+ROUND16 = 201326592.0
+TILES = [(448, ("d", "d", 26, 27)), (400, (22, 23, 24, 25)), (336, (18, 19, 20, 21)), (272, (14, 15, 16, 17)),
+         (208, (10, 11, 12, 13)), (144, (6, 7, 8, 9)), (256, (2, 3, 4, 5))]
+LAST = len(TILES) - 1
+BYSIGN = (26, 24, 22, 20, 18, 14, 10)
 OP = AluOpType
 AF = ActivationFunctionType
 
@@ -37,36 +39,33 @@ def _packmx(buf, parts):
     _mx(buf, at)
 
 
-for _n in ("xa", "xb", "ft", "cr", "tl"):
-    _sb(_n, 4 * C, "bfloat16")
-_sb("ut", 512, "bfloat16")
-_sb("vt", 512, "bfloat16")
-_pack("kt", "bfloat16", [(n, 512) for n in ("ctile", "cneg", "fb", "sgt", "fst", "mst", "ont", "et0", "et1", "et2", "et3")])
+for _n in ("xa", "xb"):
+    _sb(_n, 4 * (C + M), "bfloat16")
+for _n, _w in (("cr", 4 * C), ("tl", 4 * C), ("zt", 4 * M), ("ut", 512), ("vt", 512), ("dg", 512)):
+    _sb(_n, _w, "bfloat16")
+_pack("kt", "bfloat16", [("ones", 528), ("grp", 128), ("grp0", 128), ("unit", 256), ("sgt", 512), ("fst", 512), ("rtt", 4 * 176), ("ont", 512), ("et", 528)])
 _pack("tb", "bfloat16", [("t%d" % b, C) for b in range(4)])
-_pack("yh", "bfloat16", [("yh%d" % b, C + M) for b in range(4)])
-_pack("ctb", "bfloat16", [("ct%d" % q, 4 * QN[q]) for q in range(7)])
-_pack("kb", "bfloat16", [("mk", C), ("rst", C), ("iotaj", C), ("mlt", M), ("kv", M), ("i16", C), ("jwm", C), ("jwf", C)])
+_pack("ctb", "bfloat16", [("ct%d" % q, 4 * TILES[q][0]) for q in range(len(TILES))])
+_pack("kb", "bfloat16", [("mk", C + 16), ("nmk", C + 16), ("i16", C + 16), ("iotaj", C), ("rst", M), ("amp", M), ("cc", M), ("kv", M)])
 _pack("sgn", "bfloat16", [("sgn%d" % k, 16 * k) for k in BYSIGN])
-_packmx("k", [(n, 128) for n in ("e0", "e1", "e2", "e3", "sg", "fs", "ms", "on")])
-_packmx("c", [("c%d" % q, QN[q]) for q in range(7)])
-for _n, _w in (("u", 128), ("ux", 128), ("v", 128), ("w", 512), ("x", C), ("f", C), ("mv", 224), ("cr", C)):
+_packmx("k", [("e0", 128), ("e1", 128), ("e2", 128), ("e3", 128), ("sg", 128), ("fs", 128), ("on", 128), ("rt", 176)])
+_packmx("c", [("c%d" % q, TILES[q][0]) for q in range(len(TILES))])
+for _n, _w in (("u", 128), ("ux", 128), ("v", 128), ("w", 512), ("x", C), ("dg", 128), ("cr", C)):
     _mx(_n, _w)
 for _t in range(R):
-    _mx("tl%d" % _t, C)
     _mx("z%d" % _t, M)
     _mx("a%d" % _t, M)
-for _n, _w in (("junk0", C), ("junk1", C), ("junk2", C), ("ot", C), ("la", C), ("lm", C), ("lf", C), ("ctab", C), ("cm", M), ("cf", M), ("lk", M), ("lkm", M),
-               ("lkf", M), ("rep2", M), ("eqd", M), ("eqm", M), ("df", M), ("eqo", 12 * 192), ("st", C + M), ("stm", C), ("stf", C), ("rfb", C), ("em2", C),
-               ("rf", C), ("dg", 112), ("mv", 896), ("m8", 112), ("lo", 112), ("hi", 112), ("gx", 56), ("gy", 56), ("gg", 224)):
+for _n, _w in (("junk0", C), ("junk1", C), ("junk2", C), ("ot", C), ("la", C), ("lm", C), ("lf", C), ("lk", C), ("lkm", M + 16), ("lkf", M + 16),
+               ("eqd", M), ("df", M), ("eqo", 12 * 192), ("st", C + M), ("stm", C), ("stf", C), ("em", C), ("ef", C), ("rm", C), ("rf", C)):
     _sb(_n, _w, "bfloat16")
-for _n in ("sm", "swf", "rep", "em", "ef", "iot512", "kca", "ka", "yo", "olf"):
-    _sb(_n, C, "float32")
-_pack("fk", "float32", [("cst", NS), ("onef", 32), ("gm", 8), ("mb", 32), ("rst8", 32), ("kc", NS), ("j448", NS), ("nt", MS)])
-_pack("fw", "float32", [("rs", NS), ("rsc", NS), ("z", NS), ("x1", NS), ("kw", NS), ("km", 32), ("kf", 32), ("aa", 112), ("bb", 112), ("a2", 56), ("b2", 56),
-                        ("av", NS), ("bv", NS), ("mn", NS), ("mxv", NS), ("spr", NS), ("sp5", NS), ("ab", NS), ("c1", NS), ("c2", NS), ("tg", NS),
-                        ("dc", MS), ("dup", MS), ("dp1", MS), ("ntf", MS), ("lk2", MS), ("offf", MS), ("sx2", NS)])
-_pack("ki", "int32", [("ia", C), ("ib", C), ("if1", NS), ("if2", 8)])
-for _n, _w in (("offrep", NS), ("offu", 8), ("offq", NS), ("offt", NS), ("offs", NS), ("offr", NS), ("offc", MS), ("offl", NS), ("offd", MS), ("offx", NS)):
+for _n, _w in (("sm", C + 16), ("swf", C + 16), ("iot512", C), ("kca", C), ("ka", C), ("yo", C), ("olf", C)):
+    _sb(_n, _w, "float32")
+_pack("fk", "float32", [("pm", 1), ("pg", 1), ("p3", 1), ("k16", NS), ("kc", NS), ("j448", NS), ("nt", MS)])
+_pack("fw", "float32", [("rs", NS), ("z", NS), ("kw", NS), ("kf", 16), ("qs", 56), ("lo", 56), ("hi", 56), ("l2", 56), ("h2", 56), ("s1", 56), ("s4", 56),
+                        ("gy", 56), ("s3", 56), ("b2", NS), ("n1", NS), ("n2", NS), ("mn", NS), ("mxv", NS), ("spr", NS), ("m1", NS), ("m2", NS), ("m3", NS),
+                        ("m4", NS), ("m5", NS), ("med", NS), ("dc", MS), ("lk2", MS), ("d1", MS), ("d2", MS), ("d3", MS), ("sxw", NS)])
+_pack("ki", "int32", [("ip", 1), ("ia", 1), ("ib", 1), ("ic", 1), ("if2", 8)])
+for _n, _w in (("offu", 8), ("offe", 2), ("offq", NS), ("offt", NS), ("offs", NS), ("offr", NS), ("offk", MS), ("offl", NS), ("offd", MS), ("offx", 4 * NS)):
     _sb(_n, _w, "uint16")
 for _n in ("pss", "psa", "psm", "psr", "pd0", "pd1", "pd2", "pd3"):
     SCRATCH[_n] = ("psum", [128, 512], "float32")
@@ -217,20 +216,20 @@ def rank_program(g, core, T, topo):
 
     nj = [0]
 
-    def count_ones(acc, v, n):
+    def row_sum(acc, v, n, scale=None):
         nj[0] = (nj[0] + 1) % 3
-        act(B("junk%d" % nj[0], 0, n), v, acc=acc)
+        act(B("junk%d" % nj[0], 0, n), v, acc=acc, scale=scale)
 
     def fill(v, c):
         issue("v", [v], [], lambda: g.vector.memset(ap(v), c))
 
-    def quant(name, n, tile):
-        src, o, s = B(tile, 0, 4 * n), B("q" + name, 0, n), B("s" + name, 0, n)
+    def quant(name, n, tile, at=0):
+        src, o, s = B(tile, at, at + 4 * n), B("q" + name, 0, n), B("s" + name, 0, n)
         issue("v", [o, s], [src], lambda: g.vector.quantize_mx(ap(o), ap(s), ap(src)))
 
-    def mm(out, n, l, r, start=True, stop=True, la=0):
+    def mm(out, n, l, r, start=True, stop=True, la=0, ra=0):
         o = B(out, 0, n)
-        a, asc, b, bsc = B("q" + l, la, la + 128), B("s" + l, la, la + 128), B("q" + r, 0, n), B("s" + r, 0, n)
+        a, asc, b, bsc = B("q" + l, la, la + 128), B("s" + l, la, la + 128), B("q" + r, ra, ra + n), B("s" + r, ra, ra + n)
         issue("t", [o], [a, asc, b, bsc], lambda: g.tensor.matmul_mx(ap(o), ap(a), ap(asc), ap(b), ap(bsc), start, stop))
 
     def iota(v, pattern, base, cm):
@@ -247,83 +246,79 @@ def rank_program(g, core, T, topo):
         scan(B(out, 0, n), v, B("mk", 0, n), OP.add, OP.mult)
 
     def hold(out, m, n=C):
-        scan(B(out, 0, n), B("rst", 0, n), B(m, 0, n), OP.mult, OP.add)
+        scan(B(out, 0, n), B("nmk", 0, n), B(m, 0, n), OP.mult, OP.add)
 
-    dma("y", T["xa"][:, :], T.x[:, :], [B("xa")], [])
+    def zeros(n, a, b):
+        for c in range(a, b, 512):
+            act(B(n, c, min(c + 512, b)), B("ones", 0, min(512, b - c)), scale=0.0)
+
+    dma("y", T["xa"][:, 0:4 * C], T.x[:, :], [B("xa", 0, 4 * C)], [])
     dma("s", T["ut"][:, :], T.u[:, :], [B("ut")], [])
+    deps("y", [], [B("xa", 0, 4 * C)])
     dma("y", T["qw"][:, 0:512].bitcast(dt.uint8), T.wc[:, :], [B("qw")], [])
-    dma("s", T["sw"][:, :], T.ws[:, :], [B("sw")], [])
+    dma("y", T["sw"][:, :], T.ws[:, :], [B("sw")], [])
     dma("y", T["vt"][:, :], T.v[:, :], [B("vt")], [])
 
-    def zeros(n):
-        w = ALIAS[n][2]
-        for a in range(0, w, 512):
-            act(B(n, a, min(a + 512, w)), B("ctile", 0, min(512, w - a)), scale=0.0)
-
     iota(B("if2"), [[16, 8]], 0, 0)
-    iota(B("ia"), [[0, NS], [-1, 16]], 1024, 1)
-    iota(B("i16"), [[0, NS], [1, 16]], 0, 0)
-    iota(B("if1"), [[16, NS]], 15, 0)
-    fill(B("ctile"), 1.0)
-    zeros("ct6")
-    fill(B("ft"), 0.0)
-    for a, b in (("ct4", "ct4"), ("ct3", "ct3"), ("ct0", "ct2")):
-        n = ALIAS[b][1] + ALIAS[b][2] - ALIAS[a][1]
-        o, i = B(a, 0, n), B("ft", 0, n)
-        dma("y", ap(o), ap(i), [o], [i])
-    fill(B("cneg"), -1.0)
+    iota(B("ip"), [[0, 1]], 0, 1)
+    fill(B("ones"), 1.0)
+    iota(B("i16"), [[0, NS + 1], [1, 16]], 0, 0)
+    one = B("ones", 0, 128)
+    sel(B("grp0"), one, [[-16, 8], [0, 16]], OP.is_ge, 0, 1)
+    sel(B("grp"), B("grp0"), [[16, 8], [0, 16]], OP.is_ge, 15, -1)
+    sel(B("fst", 0, 512, 4), B("grp"), [[1, 128]], OP.is_gt, 0, -1)
+    sel(B("fst", 1, 512, 4), B("grp"), [[-1, 128]], OP.is_gt, 0, 1)
+    zeros("ct%d" % LAST, 0, 1024)
+    zeros("dg", 0, 512)
+    for q, (w, slots) in enumerate(TILES[:LAST]):
+        fill(B("ct%d" % q, 4 * w - 192, 4 * w), 0.0)
+    fill(B("sm", C, C + 16), 0.0)
+    fill(B("rs", 0, 1), 0.0)
+    fill(B("dc", 0, 1), 0.0)
     vcopy(B("offu"), B("if2"))
-    fill(B("fst"), 0.0)
-    sc(B("ib"), B("ia"), 15, OP.bitwise_and)
-    sc(B("mk"), B("ib"), 0.0, OP.is_equal)
-    sc(B("rst"), B("i16"), 1.0, OP.min)
-    vcopy(B("offrep"), B("if1"))
+    sc(B("ia"), B("ip"), 15, OP.bitwise_and)
+    sc(B("ib"), B("ip"), 4, OP.arith_shift_right)
+    sc(B("ic"), B("ip"), 3, OP.bitwise_and)
+    vcopy(B("pm"), B("ia"))
+    vcopy(B("pg"), B("ib"))
+    sc(B("p3"), B("ic"), 8.0, OP.mult)
+    sc(B("mk"), B("i16"), B("pm"), OP.is_equal)
+    sc(B("nmk"), B("i16"), B("pm"), OP.not_equal)
+    sc(B("offe", 0, 1), B("p3"), B("pg"), OP.add, float(NS - 1), OP.min)
     quant("u", 128, "ut")
+    quant("c%d" % LAST, 256, "ct%d" % LAST)
     vcopy(I(B("qux"), None, "codes"), I(B("qu"), B("offu"), "codes"))
     act(B("sux"), I(B("su"), B("offu")))
+    for e in (2, 3):
+        act(B("fst", e, 512, 4), B("grp"), scale=-1.0)
+    for e in range(4):
+        act(B("sgt", e, 512, 4), B("grp"), scale=-1.0)
     quant("x", C, "xa")
-    zeros("ct5")
+    quant("fs", 128, "fst")
+    quant("sg", 128, "sgt")
 
-    sel(B("fb"), B("cneg"), [[-16, 8], [0, 16], [0, 4]], OP.is_ge, 0, 1)
-    sel(B("sgt"), B("fb"), [[16, 8], [0, 16], [0, 4]], OP.is_ge, 15, -1)
-    l0, l1, one = B("fst", 0, 512, 4), B("fst", 1, 512, 4), B("ctile", 0, 128)
-    sel(l0, one, [[16, 8], [1, 16]], OP.is_gt, 0, -1)
-    sel(l0, l0, [[-16, 8], [0, 16]], OP.is_ge, 0, 1)
-    sel(l1, one, [[-16, 8], [-1, 16]], OP.is_gt, 0, 1)
-    sel(l1, l1, [[16, 8], [0, 16]], OP.is_ge, 15, -1)
-    iota(B("rs", 0, 1), [[0, 1]], 0, 0)
-    iota(B("dc", 0, 1), [[0, 1]], 0, 0)
-    iota(B("cst"), [[-16, NS]], 208, 0)
+    sel(B("unit"), B("ones", 0, 256), [[0, 2], [-1, 128]], OP.is_equal, 0, 1)
+    sel(B("et", 0, 516), B("ones", 0, 516), [[-1, 516]], OP.is_equal, 3, 4)
     iota(B("iotaj"), [[1, C]], -224, 0)
-    iota(B("dg"), [[0, 112]], 0, 0)
-    iota(B("onef"), [[0, 32]], 1, 0)
-    sel(B("gm"), B("onef", 0, 8), [[-16, 8]], OP.is_ge, 0, 1)
-    sel(B("gm"), B("gm"), [[16, 8]], OP.is_ge, 15, -1)
-    sel(B("mb"), B("onef"), [[0, 4], [-16, 8]], OP.is_ge, 0, 1)
-    sel(B("mb"), B("mb"), [[0, 4], [16, 8]], OP.is_ge, 15, -1)
-    sel(B("rst8"), B("onef"), [[0, 4], [1, 8]], OP.is_gt, 0, 0)
-    for b in range(4):
-        sel(B("et%d" % b), B("ctile"), [[-4, 128], [-1, 4]], OP.is_equal, b, 4)
-    sel(B("ont"), B("ctile"), [[0, 128], [-1000, 4]], OP.is_ge, 2936, 1)
+    iota(B("k16"), [[16, NS]], 0, 0)
     iota(B("iot512"), [[512, C]], 0, 0)
-    iota(B("kca"), [[-1, C]], C - 1, 0)
+    iota(B("kca"), [[-1, C]], 0, 0)
+    sel(B("ont"), B("ones", 0, 512), [[0, 128], [-1000, 4]], OP.is_gt, 3064, -1)
     iota(B("kv"), [[1, M]], 0, 0)
 
-    def consts_last():
+    def consts_later():
         for e in range(4):
-            act(B("mst", e, 512, 4), B("mk", 0, 128))
-        mask("jwm", B("iotaj"))
-        hold("jwf", "jwm")
-        sc(B("j448"), last16("jwf"), -224.0, OP.add)
-        sc(B("kc"), last16("jwf"), -1.0, OP.mult, 223.0, OP.add)
-        sc(B("nt"), last16("jwf", M), 672.0, OP.add)
-        quant("ms", 128, "mst")
+            a = 16 + 48 * (e // 2)
+            vcopy(B("rtt", e, 4 * 176, 4), B("unit", a, a + 176))
+        quant("rt", 176, "rtt")
         for b in range(4):
-            quant("e%d" % b, 128, "et%d" % b)
+            quant("e%d" % b, 128, "et", 3 - b)
+
+    def consts_last():
+        sc(B("j448"), B("k16"), B("pm"), OP.add, -448.0, OP.add)
+        sc(B("nt"), B("k16", 0, MS), B("pm"), OP.add, 450.0, OP.add)
+        sc(B("kc"), B("j448"), 447.5, OP.add, -1.0 / 512, OP.mult)
         quant("on", 128, "ont")
-        hold("jwm", "mk", M)
-        sc(B("mlt"), B("jwm", 0, M), -1.0, OP.mult, 1.0, OP.add)
-        quant("v", 128, "vt")
 
     X = ["xa", "xb"]
     for t in range(R):
@@ -334,187 +329,192 @@ def rank_program(g, core, T, topo):
         if not first:
             for b in range(4):
                 mm("pd%d" % b, C, "e%d" % b, "x")
-        tt(B("sm"), B("pss", 0, C), B("mk"), OP.mult)
-        hold("swf", "sm")
+        tt(B("sm", 0, C), B("pss", 0, C), B("mk", 0, C), OP.mult)
+        hold("swf", "sm", C + 16)
         if not first:
             act(B("t0"), B("pd0", 0, C))
+        iota(B("st", 0, C), [[0, C]], -512, 0)
 
         def signs(q):
-            for k in range(4 * q + 3, 4 * q - 1, -1):
+            for k in reversed(TILES[q][1]):
                 if k in BYSIGN:
                     act(B("sgn%d" % k), B("psm", 0, 16 * k), AF.Sign, scale=-1.0, bias=B("swf", 16 * k + 15, 16 * k + 16))
 
-        signs(6)
-        for q in (6, 5, 4, 3, 2, 1, 0):
-            for k in range(4 * q + 3, max(4 * q - 1, 0), -1):
-                c = B("ct%d" % q, k % 4, 64 * k, 4)
-                if k in BYSIGN:
-                    sc(c, B("sgn%d" % k), 0.0, OP.is_le)
+        def compare(k, c):
+            if k in BYSIGN:
+                sc(c, B("sgn%d" % k), 0.0, OP.is_le, -0.5, OP.add)
+            else:
+                sc(c, B("pss", 0, 16 * k), B("swf", 16 * k + 15, 16 * k + 16), OP.is_ge, -0.5, OP.add)
+
+        signs(0)
+        for q, (w, slots) in enumerate(TILES):
+            ct = "ct%d" % q
+            order = [e for e in (3, 2, 1, 0) if slots[e] not in BYSIGN] + [e for e in (3, 2, 1, 0) if slots[e] in BYSIGN]
+            if q < LAST:
+                signs(q + 1)
+            for e in order:
+                k = slots[e]
+                if k == "d":
+                    a = 16 * e
+                    tt(B(ct, e, 4 * C, 4), B("pss", 0, C), B("swf", a, a + C), (OP.is_le, OP.is_lt)[e])
                 else:
-                    sc(c, B("pss", 0, 16 * k), B("swf", 16 * k + 15, 16 * k + 16), OP.is_ge)
-                if k == 4 * q + 3:
-                    signs(q - 1)
-                count_ones(B("rs", k, k + 1), c, 16 * k)
-                if k == 23:
-                    act(B("rep"), I(B("swf"), B("offrep")))
-            if first and q == 6:
-                quant("sg", 128, "sgt")
-            quant("c%d" % q, QN[q], "ct%d" % q)
-            mm("psa", QN[q], "sg", "c%d" % q, q == 6, q == 0)
-            if q == 4:
-                if first:
-                    quant("fs", 128, "fst")
-                tt(B("ft", 0, 4 * C, 4), B("pss", 0, C), B("rep"), OP.is_le)
-                tt(B("ft", 1, 4 * C, 4), B("pss", 0, C), B("rep"), OP.is_lt)
-                quant("f", C, "ft")
-                mm("psa", C, "fs", "f", False, False)
-            if q == 1 and first:
-                consts_last()
+                    c = B(ct, e, 64 * k, 4)
+                    compare(k, c)
+                    row_sum(B("rs", k, k + 1), c, 16 * k)
+            if q < LAST:
+                quant("c%d" % q, w, ct)
+                mm("psa", w, "sg" if q else "fs", "c%d" % q, q == 0, False)
+            else:
+                c = B(ct, 512, 576, 4)
+                compare(1, c)
+                row_sum(B("rs", 1, 2), c, 16)
+                quant("c%d" % q, 144, ct)
+                mm("psa", 128, "sg", "c%d" % q, False, False)
+                mm("psa", 128, "sg", "c%d" % q, False, True, ra=128)
         if first:
+            consts_later()
             for b in range(4):
                 mm("pd%d" % b, C, "e%d" % b, "x")
             act(B("t0"), B("pd0", 0, C))
         act(B("t1"), B("pd1", 0, C))
-        tt(B("em"), B("psa", 0, C), B("mk"), OP.mult)
-        tt(B("rsc"), B("rs"), B("cst"), OP.add)
+        tt(B("em"), B("psa", 0, C), B("mk", 0, C), OP.mult)
         hold("ef", "em")
-        tt(B("z"), last16("ef"), B("rsc"), OP.add)
-        sc(B("x1"), B("z"), 0.0625, OP.mult, MAGIC, OP.add)
-        sc(B("offq"), B("z"), 224.0, OP.add)
-        sc(B("dg", 0, 112, 4), B("x1"), -MAGIC, OP.add, 16.0, OP.mult)
+        tt(B("z"), last16("ef"), B("rs"), OP.add)
+        sc(B("dg", 0, 112, 4), B("z"), ROUND16, OP.add, -ROUND16, OP.add)
+        sc(B("dg", 114, 224, 4), B("z"), ROUND16, OP.add, -ROUND16, OP.add)
         tt(B("dg", 1, 112, 4), B("z"), B("dg", 0, 112, 4), OP.subtract)
-        for gr in range(4):
-            act(B("mv", 112 * (gr + 4), 112 * (gr + 5)), B("dg"), scale=B("gm", gr + 4, gr + 5))
-            sc(B("mv", 112 * gr, 112 * (gr + 1)), B("dg"), B("gm", gr, gr + 1), OP.mult)
-        quant("mv", 224, "mv")
-        mm("psm", 224, "ms", "mv")
+        tt(B("dg", 115, 224, 4), B("z"), B("dg", 0, 112, 4), OP.subtract)
+        sc(B("offq"), B("z"), 216.0, OP.add)
+        quant("dg", 128, "dg")
+        for n, bank in ((1, "psm"), (2, "psr"), (0, "pss"), (3, "psa")):
+            mm(bank, 128, "rt", "dg", la=16 * n)
+        vcopy(I(B("ot"), B("offq")), B("iotaj"))
+        if first:
+            consts_last()
+        act(B("qs"), B("psm", 0, 56))
+        act(B("l2"), B("psr", 0, 56))
+        act(B("h2", 0, NS), B("psr", 0, NS))
         act(B("t2"), B("pd2", 0, C))
         act(B("t3"), B("pd3", 0, C))
-        vcopy(I(B("ot"), B("offq")), B("iotaj"))
-        vcopy(B("m8"), B("psm", 112, 224))
-        tt(B("lo"), B("psm", 0, 112), B("m8"), OP.min)
-        tt(B("hi"), B("psm", 0, 112), B("m8"), OP.max)
-        tt(B("gg", 0, 56), B("lo", 0, 56), B("lo", 56, 112), OP.min)
-        tt(B("gg", 168, 224), B("hi", 0, 56), B("hi", 56, 112), OP.max)
-        tt(B("mn"), B("gg", 0, 28), B("gg", 28, 56), OP.min)
-        tt(B("mxv"), B("gg", 168, 196), B("gg", 196, 224), OP.max)
-        tt(B("gx"), B("lo", 0, 56), B("lo", 56, 112), OP.max)
+
+        def lo(n):
+            return B(n, 0, NS)
+
+        def hi(n):
+            return B(n, NS, 2 * NS)
+
+        tt(B("lo"), B("pss", 0, 56), B("qs"), OP.min)
+        tt(B("hi"), B("pss", 0, 56), B("qs"), OP.max)
+        tt(hi("h2"), hi("psa"), hi("l2"), OP.max)
+        tt(hi("l2"), hi("psa"), hi("l2"), OP.min)
+        tt(B("s4"), B("hi"), B("h2"), OP.max)
+        tt(B("s1"), B("lo"), B("l2"), OP.min)
+        tt(B("n2"), lo("s4"), hi("s4"), OP.max)
+        tt(B("n1"), lo("s1"), hi("s1"), OP.min)
+        tt(B("mxv"), B("n2"), B("z"), OP.max)
+        tt(B("mn"), B("n1"), B("z"), OP.min)
+        tt(hi("lo"), hi("lo"), hi("l2"), OP.max)
         tt(B("spr"), B("mxv"), B("mn"), OP.subtract)
-        tt(B("gy"), B("hi", 0, 56), B("hi", 56, 112), OP.min)
+        tt(B("gy"), B("hi"), B("h2"), OP.min)
         sc(B("offs"), B("spr"), 0.0, OP.add)
-        sc(B("sp5"), B("spr"), 512.0, OP.mult)
+        tt(B("kw"), B("spr"), B("kc"), OP.add)
         tt(B("ka"), I(B("iot512"), B("offs")), B("kca"), OP.add)
-        tt(B("kw"), B("sp5"), B("kc"), OP.add)
-        tt(B("gg", 56, 112), B("gx"), B("gy"), OP.min)
-        tt(B("km", 0, 24), B("kw", 0, 24), B("mb", 0, 24), OP.mult)
-        tt(B("km", 24, 32), B("kw", 20, 28), B("mb", 24, 32), OP.mult)
-        tt(B("gg", 112, 168), B("gx"), B("gy"), OP.max)
-        scan(B("kf"), B("rst8"), B("km"), OP.mult, OP.add)
+        act(B("kf"), I(B("kw"), B("offe", 0, 1)), scale=512.0)
         for e in range(4):
-            act(B("cr", e, 4 * C, 4), B("ka"), AF.Sign, scale=-1.0, bias=B("kf", 8 * e + 7, 8 * e + 8))
-        for r in range(4):
-            p, o = B("gg", 56 * r, 56 * r + 28), B("gg", 56 * (3 - r) + 28, 56 * (3 - r) + 56)
-            tt(B("aa", 28 * r, 28 * r + 28), p, o, OP.min)
-            tt(B("bb", 28 * r, 28 * r + 28), p, o, OP.max)
-        tt(B("a2"), B("aa", 0, 56), B("aa", 56, 112), OP.max)
-        tt(B("b2"), B("bb", 0, 56), B("bb", 56, 112), OP.min)
-        tt(B("av"), B("a2", 0, 28), B("a2", 28, 56), OP.max)
-        tt(B("bv"), B("b2", 0, 28), B("b2", 28, 56), OP.min)
-        tt(B("c1"), B("z"), B("av"), OP.max)
-        tt(B("ab"), B("av"), B("bv"), OP.add)
-        tt(B("c2"), B("c1"), B("bv"), OP.min)
-        tt(B("tg"), B("ab"), B("c2"), OP.subtract)
-        sc(B("offt"), B("tg"), 224.0, OP.add)
-        quant("cr", C, "cr")
-        mm("psr", C, "on", "cr")
-        act(B("rfb"), B("psr", 0, C), AF.Identity, scale=0.5, bias=-0.5)
+            act(B("cr", e, 4 * C, 4), B("ka"), AF.Sign, scale=-1.0, bias=B("kf", e, e + 1))
+        tt(B("s3"), B("lo"), B("gy"), OP.max)
+        tt(B("b2"), hi("lo"), hi("gy"), OP.min)
+        tt(B("m1"), lo("s4"), hi("s1"), OP.max)
+        tt(B("m3"), lo("s1"), hi("s3"), OP.max)
+        tt(B("m2"), lo("s3"), B("b2"), OP.max)
+        tt(B("m4"), B("m1"), hi("s4"), OP.min)
+        tt(B("m5"), B("m2"), B("m3"), OP.min)
+        tt(B("med"), B("m4"), B("m5"), OP.min)
+        sc(B("offt"), B("med"), 216.0, OP.add)
         vcopy(B("la"), I(B("ot"), B("offt")))
         mask("lm", B("la"))
+        quant("cr", C, "cr")
+        mm("psr", C, "on", "cr")
         hold("lf", "lm")
-        mask("em2", B("rfb"))
         sc(B("offl"), last16("lf"), 224.0, OP.add)
         for b in range(4):
             act(B("tl", b, 4 * C, 4), I(B("t%d" % b), B("offl")))
-        hold("rf", "em2")
-        sc(B("offr"), last16("rf"), 224.0, OP.add)
-        vcopy(I(B("ctab"), B("offr")), B("iotaj"))
-        mask("cm", B("ctab", 0, M), M)
-        hold("cf", "cm", M)
-        sc(B("offc"), last16("cf", M), 224.0, OP.add)
-        n_tl, n_z, n_a = "tl%d" % t, "z%d" % t, "a%d" % t
-        act(B("lk"), I(B("la"), B("offc")))
-        quant(n_tl, C, "tl")
-        act(B("s" + n_z), I(B("s" + n_tl), B("offc")))
-        vcopy(I(B("q" + n_z), None, "codes"), I(B("q" + n_tl), B("offc"), "codes"))
+        dma("g", T[x][:, 0:4 * C], T["tl"][:, :], [B(x, 0, 4 * C)], [B("tl")], accum_op=OP.add)
+        tt(B("rm"), B("psr", 0, C), B("mk", 0, C), OP.mult)
+        hold("rf", "rm")
+        sc(B("offr"), last16("rf"), 0.5, OP.mult, 223.0, OP.add)
+        vcopy(I(B("lk"), B("offr")), B("la"))
+        mask("lkm", B("lk", 0, M + 16), M + 16)
+        if first:
+            sc(B("rst"), B("i16", 0, M), 1.0, OP.min)
+        hold("lkf", "lkm", M + 16)
+        if first:
+            sc(B("amp"), B("mk", 0, M), 1023.0, OP.mult, 1.0, OP.add)
+        sc(B("offk"), last16("lkf", M), 224.0, OP.add)
+        n_z, n_a = "z%d" % t, "a%d" % t
+        for b in range(4):
+            o, w = B("zt", b, 4 * M, 4), I(B("t%d" % b), B("offk"))
+            if b % 2:
+                act(o, w)
+            else:
+                vcopy(o, w)
+        tt(B("eqd"), B("lk", 0, M), B("lkf", 16, M + 16), OP.is_equal)
+        quant(n_z, M, "zt")
         to = T.cores[(rank + 1 + t) % len(T.cores)]
         rid, pid, _se = topo.addr(to)
         en = topo.engines(core, to)
         wide, thin = en[0::2], en[1::4]
         got = len(wide) + len(thin)
-        for nm, view, es in (("s", lambda n: T["s" + n][:, 0:M], thin), ("q", lambda n: T["q" + n][:, 0:M].bitcast(dt.uint8), wide)):
-            deps("g", [], [B(nm + n_z)])
+        deps("g", [], [B("q" + n_z), B("s" + n_z)])
+        for view, es in ((lambda n: T["q" + n][:, 0:M].bitcast(dt.uint8), wide), (lambda n: T["s" + n][:, 0:M], thin)):
             g.remote_dma(view(n_a), view(n_z), T.sem["arr%d" % t], T.sem["snd%d" % t], pid, rid, sum(1 << e for e in es))
-        dma("g", T[x][:, :], T["tl"][:, :], [B(x)], [B("tl")], accum_op=OP.add)
-        iota(B("st", 0, C), [[0, C]], -512, 0)
-        mask("lkm", B("lk"), M)
-        hold("lkf", "lkm", M)
-        act(B("rep2"), I(B("lkf"), B("offrep", 0, MS)))
         for k in range(MS - 1, 0, -1):
             e = B("eqo", 192 * k, 192 * k + 16 * k)
             sc(e, B("lk", 0, 16 * k), B("lkf", 16 * k + 15, 16 * k + 16), OP.is_equal)
-            count_ones(B("dc", k, k + 1), e, 16 * k)
+            row_sum(B("dc", k, k + 1), e, 16 * k, 1024.0)
+        if first:
+            tt(B("cc"), B("amp"), B("rst"), OP.mult)
+            quant("v", 128, "vt")
+        sc(B("lk2"), last16("lkf", M), 226.0, OP.add)
+        scan(B("df"), B("cc"), B("eqd"), OP.mult, OP.max)
         if t == R - 1:
             act(B("olf"), B("la"), AF.Identity, bias=224.0)
             dma("y", T.ol[:, :], T["olf"][0:128:16, :], [], [B("olf")])
-        tt(B("eqd"), B("lk"), B("rep2"), OP.is_equal)
-        scan(B("eqm"), B("eqd"), B("mlt"), OP.max, OP.mult)
-        sc(B("lk2"), last16("lkf", M), 224.0, OP.add)
-        scan(B("df"), B("rst", 0, M), B("eqm"), OP.mult, OP.max)
-        tt(B("dup"), B("dc"), last16("df", M), OP.max)
-        sc(B("dp1"), B("dup"), 1.0, OP.min)
-        tt(B("ntf"), B("dp1"), B("nt"), OP.mult)
-        tt(B("offf"), B("ntf"), B("lk2"), OP.max)
-        sc(B("offd"), B("offf"), 0.0, OP.add)
+        tt(B("d1"), last16("df", M), B("lk2"), OP.max)
+        tt(B("d2"), B("d1"), B("dc"), OP.max)
+        tt(B("d3"), B("d2"), B("nt"), OP.min)
+        sc(B("offd"), B("d3"), -2.0, OP.add)
         vcopy(I(B("st"), B("offd")), B("kv"))
-
-        def halve(b):
-            o, i = B("yh%d" % b, 0, C), B(x, b, 4 * C, 4)
-            if b % 2:
-                act(o, i, scale=0.5)
-            else:
-                sc(o, i, 0.5, OP.mult)
-
-        halve(1)
-        halve(3)
         mask("stm", B("st", 0, C))
-        halve(0)
         hold("stf", "stm")
-        halve(2)
-        tt(B("sx2"), last16("stf"), B("j448"), OP.max)
+        tt(B("sxw"), last16("stf"), B("j448"), OP.max)
+        for b in (1, 0, 3, 2):
+            sc(B("offx", NS * b, NS * b + NS), B("sxw"), 4.0, OP.mult, 4.0 * C + b, OP.add)
         wait("t", "arr%d" % t, got)
         for b in range(4):
             mm("pd%d" % b, M, "w", n_a, la=128 * b)
         for b in range(4):
-            h, pd = B("yh%d" % b, C, C + M), B("pd%d" % b, 0, M)
-            if b % 2:
-                act(h, pd, scale=0.03125)
+            h, pd = B(x, 4 * C + b, 4 * (C + M), 4), B("pd%d" % b, 0, M)
+            if b < 3:
+                act(h, pd, scale=0.0625)
             else:
-                sc(h, pd, 0.03125, OP.mult)
-            if b == 0:
-                sc(B("offx"), B("sx2"), 448.0, OP.add)
+                sc(h, pd, 0.0625, OP.mult)
         for b in range(4):
-            o, w = B(xn, b, 4 * C, 4), I(B("yh%d" % b), B("offx"))
+            o, w = B(xn, b, 4 * C, 4), I(B(x), B("offx", NS * b, NS * b + NS))
             if b % 2:
-                act(o, w)
+                act(o, w, scale=0.5)
             else:
-                vcopy(o, w)
+                sc(o, w, 0.5, OP.mult)
         quant("x", C, xn)
-    mm("pss", C, "v", "x")
-    act(B("yo"), B("pss", 0, C))
+    half = C // 2
+    mm("pss", half, "v", "x")
+    mm("psm", half, "v", "x", ra=half)
     dma("y", T.oc[:, :], T["qx"][:, 0:C].bitcast(dt.uint8), [], [B("qx")])
+    vcopy(B("yo", 0, half), B("pss", 0, half))
+    act(B("yo", half, C), B("psm", 0, half))
+    dma("s", T.y[:, :], T["yo"][:, :], [], [B("yo")])
     for k in range(4):
         dma("y", T.osc[4 * k:4 * k + 4, :], T["sx"][32 * k:32 * k + 4, 0:C], [], [B("sx")])
-    dma("s", T.y[:, :], T["yo"][:, :], [], [B("yo")])
     for t in range(R):
         wait("g", "arr%d" % t, got)
         wait("g", "snd%d" % t, got)

@@ -1,11 +1,15 @@
 from concourse.mybir import dt, AluOpType, ActivationFunctionType
 
 C, M, R, NS, MS = 448, 192, 3, 28, 12
+H, HS = C // 2, NS // 2
 ROUND16 = 201326592.0
 TILES = [(448, ("d", "d", 26, 27)), (400, (22, 23, 24, 25)), (336, (18, 19, 20, 21)), (272, (14, 15, 16, 17)),
          (208, (10, 11, 12, 13)), (144, (6, 7, 8, 9)), (256, (2, 3, 4, 5))]
 LAST = len(TILES) - 1
-BYSIGN = (26, 24, 22, 20, 18, 14, 10)
+LOW = 144
+BYSIGN = (27, 26, 24, 22, 18, 14)
+EQ = [96 * k for k in range(6)] + [576 + 192 * k for k in range(7)]
+EARLY = 18
 OP = AluOpType
 AF = ActivationFunctionType
 
@@ -46,7 +50,7 @@ for _n, _w in (("cr", 4 * C), ("tl", 4 * C), ("zt", 4 * M), ("ut", 512), ("vt", 
 _pack("kt", "bfloat16", [("ones", 528), ("grp", 128), ("grp0", 128), ("unit", 256), ("sgt", 512), ("fst", 512), ("rtt", 4 * 176), ("ont", 512), ("et", 528)])
 _pack("tb", "bfloat16", [("t%d" % b, C) for b in range(4)])
 _pack("ctb", "bfloat16", [("ct%d" % q, 4 * TILES[q][0]) for q in range(len(TILES))])
-_pack("kb", "bfloat16", [("mk", C + 16), ("nmk", C + 16), ("i16", C + 16), ("iotaj", C), ("rst", M), ("amp", M), ("cc", M), ("kv", M)])
+_pack("kb", "bfloat16", [("mk", C + 16), ("nmk", C + 16), ("i16", C + 16), ("iotaj", C), ("amp", 16), ("cc", EQ[MS]), ("kv", M)])
 _pack("sgn", "bfloat16", [("sgn%d" % k, 16 * k) for k in BYSIGN])
 _packmx("k", [("e0", 128), ("e1", 128), ("e2", 128), ("e3", 128), ("sg", 128), ("fs", 128), ("on", 128), ("rt", 176)])
 _packmx("c", [("c%d" % q, TILES[q][0]) for q in range(len(TILES))])
@@ -55,15 +59,15 @@ for _n, _w in (("u", 128), ("ux", 128), ("v", 128), ("w", 512), ("x", C), ("dg",
 for _t in range(R):
     _mx("z%d" % _t, M)
     _mx("a%d" % _t, M)
-for _n, _w in (("junk0", C), ("junk1", C), ("junk2", C), ("ot", C), ("la", C), ("lm", C), ("lf", C), ("lk", C), ("lkm", M + 16), ("lkf", M + 16),
-               ("eqd", M), ("df", M), ("eqo", 12 * 192), ("st", C + M), ("stm", C), ("stf", C), ("em", C), ("ef", C), ("rm", C), ("rf", C)):
+for _n, _w in (("junk0", C), ("junk1", C), ("junk2", C), ("ot", C), ("la", C), ("lm", C), ("lf", C), ("lk", C), ("lkm", M), ("lkf", M),
+               ("df", EQ[MS]), ("eqo", EQ[MS]), ("st", C + M), ("stm", C), ("stf", C), ("em", C), ("ef", C), ("em2", LOW), ("ef2", LOW), ("rm", C), ("rf", C)):
     _sb(_n, _w, "bfloat16")
 for _n, _w in (("sm", C + 16), ("swf", C + 16), ("iot512", C), ("kca", C), ("ka", C), ("yo", C), ("olf", C)):
     _sb(_n, _w, "float32")
 _pack("fk", "float32", [("pm", 1), ("pg", 1), ("p3", 1), ("k16", NS), ("kc", NS), ("j448", NS), ("nt", MS)])
 _pack("fw", "float32", [("rs", NS), ("z", NS), ("kw", NS), ("kf", 16), ("qs", 56), ("lo", 56), ("hi", 56), ("l2", 56), ("h2", 56), ("s1", 56), ("s4", 56),
-                        ("gy", 56), ("s3", 56), ("b2", NS), ("n1", NS), ("n2", NS), ("mn", NS), ("mxv", NS), ("spr", NS), ("m1", NS), ("m2", NS), ("m3", NS),
-                        ("m4", NS), ("m5", NS), ("med", NS), ("dc", MS), ("lk2", MS), ("d1", MS), ("d2", MS), ("d3", MS), ("sxw", NS)])
+                        ("gy", 56), ("s3", 56), ("l3", NS), ("gx", NS), ("b2", NS), ("n1", NS), ("n2", NS), ("mn", NS), ("mxv", NS), ("spr", NS),
+                        ("m1", NS), ("m2", NS), ("m3", NS), ("m4", NS), ("m5", NS), ("med", NS), ("lk2", MS), ("d1", MS), ("d3", MS), ("sxw", NS)])
 _pack("ki", "int32", [("ip", 1), ("ia", 1), ("ib", 1), ("ic", 1), ("if2", 8)])
 for _n, _w in (("offu", 8), ("offe", 2), ("offq", NS), ("offt", NS), ("offs", NS), ("offr", NS), ("offk", MS), ("offl", NS), ("offd", MS), ("offx", 4 * NS)):
     _sb(_n, _w, "uint16")
@@ -216,15 +220,15 @@ def rank_program(g, core, T, topo):
 
     nj = [0]
 
-    def row_sum(acc, v, n, scale=None):
+    def row_sum(acc, v, n):
         nj[0] = (nj[0] + 1) % 3
-        act(B("junk%d" % nj[0], 0, n), v, acc=acc, scale=scale)
+        act(B("junk%d" % nj[0], 0, n), v, acc=acc)
 
     def fill(v, c):
         issue("v", [v], [], lambda: g.vector.memset(ap(v), c))
 
-    def quant(name, n, tile, at=0):
-        src, o, s = B(tile, at, at + 4 * n), B("q" + name, 0, n), B("s" + name, 0, n)
+    def quant(name, n, tile, a=0, shift=0):
+        src, o, s = B(tile, 4 * a + shift, 4 * (a + n) + shift), B("q" + name, a, a + n), B("s" + name, a, a + n)
         issue("v", [o, s], [src], lambda: g.vector.quantize_mx(ap(o), ap(s), ap(src)))
 
     def mm(out, n, l, r, start=True, stop=True, la=0, ra=0):
@@ -245,12 +249,21 @@ def rank_program(g, core, T, topo):
     def mask(out, v, n=C):
         scan(B(out, 0, n), v, B("mk", 0, n), OP.add, OP.mult)
 
+    def mask_psum(out, bank, a, n):
+        tt(B(out, a, a + n), B(bank, 0, n), B("mk", 0, n), OP.mult)
+
     def hold(out, m, n=C):
         scan(B(out, 0, n), B("nmk", 0, n), B(m, 0, n), OP.mult, OP.add)
 
     def zeros(n, a, b):
         for c in range(a, b, 512):
             act(B(n, c, min(c + 512, b)), B("ones", 0, min(512, b - c)), scale=0.0)
+
+    def lo(n):
+        return B(n, 0, NS)
+
+    def hi(n):
+        return B(n, NS, 2 * NS)
 
     dma("y", T["xa"][:, 0:4 * C], T.x[:, :], [B("xa", 0, 4 * C)], [])
     dma("s", T["ut"][:, :], T.u[:, :], [B("ut")], [])
@@ -263,6 +276,7 @@ def rank_program(g, core, T, topo):
     iota(B("ip"), [[0, 1]], 0, 1)
     fill(B("ones"), 1.0)
     iota(B("i16"), [[0, NS + 1], [1, 16]], 0, 0)
+    iota(B("k16"), [[16, NS]], 0, 0)
     one = B("ones", 0, 128)
     sel(B("grp0"), one, [[-16, 8], [0, 16]], OP.is_ge, 0, 1)
     sel(B("grp"), B("grp0"), [[16, 8], [0, 16]], OP.is_ge, 15, -1)
@@ -271,10 +285,9 @@ def rank_program(g, core, T, topo):
     zeros("ct%d" % LAST, 0, 1024)
     zeros("dg", 0, 512)
     for q, (w, slots) in enumerate(TILES[:LAST]):
-        fill(B("ct%d" % q, 4 * w - 192, 4 * w), 0.0)
+        iota(B("ct%d" % q, 4 * w - 192, 4 * w), [[0, 192]], 0, 0)
     fill(B("sm", C, C + 16), 0.0)
     fill(B("rs", 0, 1), 0.0)
-    fill(B("dc", 0, 1), 0.0)
     vcopy(B("offu"), B("if2"))
     sc(B("ia"), B("ip"), 15, OP.bitwise_and)
     sc(B("ib"), B("ip"), 4, OP.arith_shift_right)
@@ -286,53 +299,58 @@ def rank_program(g, core, T, topo):
     sc(B("nmk"), B("i16"), B("pm"), OP.not_equal)
     sc(B("offe", 0, 1), B("p3"), B("pg"), OP.add, float(NS - 1), OP.min)
     quant("u", 128, "ut")
-    quant("c%d" % LAST, 256, "ct%d" % LAST)
+    sc(B("j448"), B("k16"), B("pm"), OP.add, -448.0, OP.add)
     vcopy(I(B("qux"), None, "codes"), I(B("qu"), B("offu"), "codes"))
     act(B("sux"), I(B("su"), B("offu")))
+    sc(B("nt"), B("k16", 0, MS), B("pm"), OP.add, 450.0, OP.add)
+    sc(B("kc"), B("j448"), 447.5, OP.add, -1.0 / 512, OP.mult)
+    sc(B("amp"), B("mk", 0, 16), 1023.0, OP.mult, 1.0, OP.add)
+    quant("c%d" % LAST, 256, "ct%d" % LAST)
     for e in (2, 3):
         act(B("fst", e, 512, 4), B("grp"), scale=-1.0)
     for e in range(4):
         act(B("sgt", e, 512, 4), B("grp"), scale=-1.0)
-    quant("x", C, "xa")
-    quant("fs", 128, "fst")
-    quant("sg", 128, "sgt")
+    for h in range(2):
+        quant("x", H, "xa", H * h)
 
     sel(B("unit"), B("ones", 0, 256), [[0, 2], [-1, 128]], OP.is_equal, 0, 1)
     sel(B("et", 0, 516), B("ones", 0, 516), [[-1, 516]], OP.is_equal, 3, 4)
     iota(B("iotaj"), [[1, C]], -224, 0)
-    iota(B("k16"), [[16, NS]], 0, 0)
     iota(B("iot512"), [[512, C]], 0, 0)
     iota(B("kca"), [[-1, C]], 0, 0)
     sel(B("ont"), B("ones", 0, 512), [[0, 128], [-1000, 4]], OP.is_gt, 3064, -1)
+    iota(B("cc"), [[0, EQ[MS]]], 1, 0)
+    for k in range(MS):
+        sel(B("cc", EQ[k] + 16 * k, EQ[k] + 16 * k + 16), B("amp"), [[0, 16]], OP.is_ge, 0, 0)
+    iota(B("cc", 0, EQ[6], 96), [[0, 6]], 0, 0)
+    iota(B("cc", EQ[6], EQ[MS], 192), [[0, 6]], 0, 0)
+    iota(B("eqo"), [[0, EQ[MS]]], 0, 0)
     iota(B("kv"), [[1, M]], 0, 0)
-
-    def consts_later():
-        for e in range(4):
-            a = 16 + 48 * (e // 2)
-            vcopy(B("rtt", e, 4 * 176, 4), B("unit", a, a + 176))
-        quant("rt", 176, "rtt")
-        for b in range(4):
-            quant("e%d" % b, 128, "et", 3 - b)
-
-    def consts_last():
-        sc(B("j448"), B("k16"), B("pm"), OP.add, -448.0, OP.add)
-        sc(B("nt"), B("k16", 0, MS), B("pm"), OP.add, 450.0, OP.add)
-        sc(B("kc"), B("j448"), 447.5, OP.add, -1.0 / 512, OP.mult)
-        quant("on", 128, "ont")
 
     X = ["xa", "xb"]
     for t in range(R):
         x, xn = X[t % 2], X[(t + 1) % 2]
         first = t == 0
+
+        def unit_tile(b):
+            if first:
+                quant("e%d" % b, 128, "et", shift=3 - b)
+                mm("pd%d" % b, C, "e%d" % b, "x")
+
+        mm("psr", H, "ux", "x")
+        mm("psa", H, "ux", "x", ra=H)
         mm("pss", C, "ux", "x")
         mm("psm", C, "ux", "x")
         if not first:
             for b in range(4):
                 mm("pd%d" % b, C, "e%d" % b, "x")
-        tt(B("sm", 0, C), B("pss", 0, C), B("mk", 0, C), OP.mult)
+        mask_psum("sm", "psr", 0, H)
+        mask_psum("sm", "psa", H, H)
+        if first:
+            quant("fs", 128, "fst")
         hold("swf", "sm", C + 16)
-        if not first:
-            act(B("t0"), B("pd0", 0, C))
+        if first:
+            quant("sg", 128, "sgt")
         iota(B("st", 0, C), [[0, C]], -512, 0)
 
         def signs(q):
@@ -345,6 +363,19 @@ def rank_program(g, core, T, topo):
                 sc(c, B("sgn%d" % k), 0.0, OP.is_le, -0.5, OP.add)
             else:
                 sc(c, B("pss", 0, 16 * k), B("swf", 16 * k + 15, 16 * k + 16), OP.is_ge, -0.5, OP.add)
+            row_sum(B("rs", k, k + 1), c, 16 * k)
+
+        def summed(q):
+            if q < LAST - 1:
+                quant("c%d" % q, TILES[q][0], "ct%d" % q)
+                mm("psa", TILES[q][0], "sg" if q else "fs", "c%d" % q, q == 0, q == LAST - 2)
+            elif q < LAST:
+                quant("c%d" % q, LOW, "ct%d" % q)
+                mm("psr", LOW, "sg", "c%d" % q, True, False)
+            else:
+                quant("c%d" % q, LOW, "ct%d" % q)
+                mm("psr", 128, "sg", "c%d" % q, False, False)
+                mm("psr", 128, "sg", "c%d" % q, False, True, ra=128)
 
         signs(0)
         for q, (w, slots) in enumerate(TILES):
@@ -355,110 +386,119 @@ def rank_program(g, core, T, topo):
             for e in order:
                 k = slots[e]
                 if k == "d":
-                    a = 16 * e
-                    tt(B(ct, e, 4 * C, 4), B("pss", 0, C), B("swf", a, a + C), (OP.is_le, OP.is_lt)[e])
+                    tt(B(ct, e, 4 * C, 4), B("pss", 0, C), B("swf", 16 * e, 16 * e + C), (OP.is_le, OP.is_lt)[e])
                 else:
-                    c = B(ct, e, 64 * k, 4)
-                    compare(k, c)
-                    row_sum(B("rs", k, k + 1), c, 16 * k)
-            if q < LAST:
-                quant("c%d" % q, w, ct)
-                mm("psa", w, "sg" if q else "fs", "c%d" % q, q == 0, False)
-            else:
-                c = B(ct, 512, 576, 4)
-                compare(1, c)
-                row_sum(B("rs", 1, 2), c, 16)
-                quant("c%d" % q, 144, ct)
-                mm("psa", 128, "sg", "c%d" % q, False, False)
-                mm("psa", 128, "sg", "c%d" % q, False, True, ra=128)
-        if first:
-            consts_later()
-            for b in range(4):
-                mm("pd%d" % b, C, "e%d" % b, "x")
-            act(B("t0"), B("pd0", 0, C))
-        act(B("t1"), B("pd1", 0, C))
-        tt(B("em"), B("psa", 0, C), B("mk", 0, C), OP.mult)
+                    compare(k, B(ct, e, 64 * k, 4))
+                if q and e == order[0]:
+                    summed(q - 1)
+        compare(1, B("ct%d" % LAST, 512, 576, 4))
+        mask_psum("em", "psa", 0, C)
+        summed(LAST)
         hold("ef", "em")
+        if first:
+            for e in range(4):
+                a = 16 + 48 * (e // 2)
+                act(B("rtt", e, 4 * 176, 4), B("unit", a, a + 176))
+        unit_tile(0)
+        mask_psum("em2", "psr", 0, LOW)
         tt(B("z"), last16("ef"), B("rs"), OP.add)
+        hold("ef2", "em2", LOW)
+        unit_tile(1)
+        tt(B("z", 0, LOW // 16), last16("ef2", LOW), B("z", 0, LOW // 16), OP.add)
+        for b in (0, 1):
+            act(B("t%d" % b), B("pd%d" % b, 0, C))
+        if first:
+            quant("rt", 176, "rtt")
         sc(B("dg", 0, 112, 4), B("z"), ROUND16, OP.add, -ROUND16, OP.add)
         sc(B("dg", 114, 224, 4), B("z"), ROUND16, OP.add, -ROUND16, OP.add)
+        sc(B("offq"), B("z"), 216.0, OP.add)
         tt(B("dg", 1, 112, 4), B("z"), B("dg", 0, 112, 4), OP.subtract)
         tt(B("dg", 115, 224, 4), B("z"), B("dg", 0, 112, 4), OP.subtract)
-        sc(B("offq"), B("z"), 216.0, OP.add)
+        if first:
+            quant("on", 128, "ont")
         quant("dg", 128, "dg")
         for n, bank in ((1, "psm"), (2, "psr"), (0, "pss"), (3, "psa")):
             mm(bank, 128, "rt", "dg", la=16 * n)
-        vcopy(I(B("ot"), B("offq")), B("iotaj"))
-        if first:
-            consts_last()
+
+        def by_place(h):
+            vcopy(I(B("ot"), B("offq", HS * h, HS * h + HS)), B("iotaj", H * h, H * h + H))
+
+        by_place(0)
         act(B("qs"), B("psm", 0, 56))
         act(B("l2"), B("psr", 0, 56))
-        act(B("h2", 0, NS), B("psr", 0, NS))
-        act(B("t2"), B("pd2", 0, C))
-        act(B("t3"), B("pd3", 0, C))
-
-        def lo(n):
-            return B(n, 0, NS)
-
-        def hi(n):
-            return B(n, NS, 2 * NS)
-
+        act(lo("h2"), lo("psr"))
         tt(B("lo"), B("pss", 0, 56), B("qs"), OP.min)
         tt(B("hi"), B("pss", 0, 56), B("qs"), OP.max)
         tt(hi("h2"), hi("psa"), hi("l2"), OP.max)
-        tt(hi("l2"), hi("psa"), hi("l2"), OP.min)
+        tt(B("l3"), hi("psa"), hi("l2"), OP.min)
+        unit_tile(2)
         tt(B("s4"), B("hi"), B("h2"), OP.max)
-        tt(B("s1"), B("lo"), B("l2"), OP.min)
+        tt(lo("s1"), lo("lo"), lo("l2"), OP.min)
+        tt(hi("s1"), hi("lo"), B("l3"), OP.min)
         tt(B("n2"), lo("s4"), hi("s4"), OP.max)
+        unit_tile(3)
         tt(B("n1"), lo("s1"), hi("s1"), OP.min)
         tt(B("mxv"), B("n2"), B("z"), OP.max)
-        tt(B("mn"), B("n1"), B("z"), OP.min)
-        tt(hi("lo"), hi("lo"), hi("l2"), OP.max)
-        tt(B("spr"), B("mxv"), B("mn"), OP.subtract)
         tt(B("gy"), B("hi"), B("h2"), OP.min)
+        tt(B("mn"), B("n1"), B("z"), OP.min)
+        tt(B("gx"), hi("lo"), B("l3"), OP.max)
+        tt(B("m1"), lo("s4"), hi("s1"), OP.max)
+        tt(B("spr"), B("mxv"), B("mn"), OP.subtract)
+        tt(lo("s3"), lo("lo"), lo("gy"), OP.max)
+        tt(hi("s3"), B("gx"), hi("gy"), OP.max)
         sc(B("offs"), B("spr"), 0.0, OP.add)
         tt(B("kw"), B("spr"), B("kc"), OP.add)
-        tt(B("ka"), I(B("iot512"), B("offs")), B("kca"), OP.add)
+        tt(B("b2"), B("gx"), hi("gy"), OP.min)
+        for b in (2, 3):
+            act(B("t%d" % b), B("pd%d" % b, 0, C))
+        for h in range(2):
+            tt(B("ka", H * h, H * h + H), I(B("iot512"), B("offs", HS * h, HS * h + HS)), B("kca", H * h, H * h + H), OP.add)
         act(B("kf"), I(B("kw"), B("offe", 0, 1)), scale=512.0)
-        for e in range(4):
-            act(B("cr", e, 4 * C, 4), B("ka"), AF.Sign, scale=-1.0, bias=B("kf", e, e + 1))
-        tt(B("s3"), B("lo"), B("gy"), OP.max)
-        tt(B("b2"), hi("lo"), hi("gy"), OP.min)
-        tt(B("m1"), lo("s4"), hi("s1"), OP.max)
+        for h in range(2):
+            for e in range(4):
+                act(B("cr", 4 * H * h + e, 4 * H * (h + 1), 4), B("ka", H * h, H * h + H), AF.Sign, scale=-1.0, bias=B("kf", e, e + 1))
         tt(B("m3"), lo("s1"), hi("s3"), OP.max)
         tt(B("m2"), lo("s3"), B("b2"), OP.max)
         tt(B("m4"), B("m1"), hi("s4"), OP.min)
         tt(B("m5"), B("m2"), B("m3"), OP.min)
+        by_place(1)
         tt(B("med"), B("m4"), B("m5"), OP.min)
+        quant("cr", H, "cr")
+        mm("psr", H, "on", "cr")
         sc(B("offt"), B("med"), 216.0, OP.add)
-        vcopy(B("la"), I(B("ot"), B("offt")))
+        act(B("la"), I(B("ot"), B("offt")))
+        quant("cr", H, "cr", H)
+        mm("psa", H, "on", "cr", ra=H)
+        mask_psum("rm", "psr", 0, H)
+        mask_psum("rm", "psa", H, H)
         mask("lm", B("la"))
-        quant("cr", C, "cr")
-        mm("psr", C, "on", "cr")
-        hold("lf", "lm")
-        sc(B("offl"), last16("lf"), 224.0, OP.add)
-        for b in range(4):
-            act(B("tl", b, 4 * C, 4), I(B("t%d" % b), B("offl")))
-        dma("g", T[x][:, 0:4 * C], T["tl"][:, :], [B(x, 0, 4 * C)], [B("tl")], accum_op=OP.add)
-        tt(B("rm"), B("psr", 0, C), B("mk", 0, C), OP.mult)
         hold("rf", "rm")
+        hold("lf", "lm")
         sc(B("offr"), last16("rf"), 0.5, OP.mult, 223.0, OP.add)
+        sc(B("offl"), last16("lf"), 224.0, OP.add)
+
+        def picked(k0, k1):
+            for b in range(4):
+                act(B("tl", 64 * k0 + b, 64 * k1, 4), I(B("t%d" % b), B("offl", k0, k1)))
+
+        def add(k0, k1):
+            o, i = B(x, 64 * k0, 64 * k1), B("tl", 64 * k0, 64 * k1)
+            dma("g", ap(o), ap(i), [o], [i], accum_op=OP.add)
+
+        picked(0, EARLY)
+        add(0, EARLY)
         vcopy(I(B("lk"), B("offr")), B("la"))
-        mask("lkm", B("lk", 0, M + 16), M + 16)
-        if first:
-            sc(B("rst"), B("i16", 0, M), 1.0, OP.min)
-        hold("lkf", "lkm", M + 16)
-        if first:
-            sc(B("amp"), B("mk", 0, M), 1023.0, OP.mult, 1.0, OP.add)
+        mask("lkm", B("lk", 0, M), M)
+        hold("lkf", "lkm", M)
         sc(B("offk"), last16("lkf", M), 224.0, OP.add)
+        sc(B("lk2"), last16("lkf", M), 226.0, OP.add)
         n_z, n_a = "z%d" % t, "a%d" % t
         for b in range(4):
-            o, w = B("zt", b, 4 * M, 4), I(B("t%d" % b), B("offk"))
-            if b % 2:
-                act(o, w)
-            else:
-                vcopy(o, w)
-        tt(B("eqd"), B("lk", 0, M), B("lkf", 16, M + 16), OP.is_equal)
+            act(B("zt", b, 4 * M, 4), I(B("t%d" % b), B("offk")))
+        picked(EARLY, NS)
+        for k in range(MS):
+            sc(B("eqo", EQ[k], EQ[k] + 16 * k + 16), B("lk", 0, 16 * k + 16), B("lkf", 16 * k + 15, 16 * k + 16), OP.is_equal)
+        scan(B("df", 0, EQ[6]), B("cc", 0, EQ[6]), B("eqo", 0, EQ[6]), OP.mult, OP.max)
         quant(n_z, M, "zt")
         to = T.cores[(rank + 1 + t) % len(T.cores)]
         rid, pid, _se = topo.addr(to)
@@ -468,21 +508,16 @@ def rank_program(g, core, T, topo):
         deps("g", [], [B("q" + n_z), B("s" + n_z)])
         for view, es in ((lambda n: T["q" + n][:, 0:M].bitcast(dt.uint8), wide), (lambda n: T["s" + n][:, 0:M], thin)):
             g.remote_dma(view(n_a), view(n_z), T.sem["arr%d" % t], T.sem["snd%d" % t], pid, rid, sum(1 << e for e in es))
-        for k in range(MS - 1, 0, -1):
-            e = B("eqo", 192 * k, 192 * k + 16 * k)
-            sc(e, B("lk", 0, 16 * k), B("lkf", 16 * k + 15, 16 * k + 16), OP.is_equal)
-            row_sum(B("dc", k, k + 1), e, 16 * k, 1024.0)
-        if first:
-            tt(B("cc"), B("amp"), B("rst"), OP.mult)
-            quant("v", 128, "vt")
-        sc(B("lk2"), last16("lkf", M), 226.0, OP.add)
-        scan(B("df"), B("cc"), B("eqd"), OP.mult, OP.max)
+        add(EARLY, NS)
+        scan(B("df", EQ[6]), B("cc", EQ[6]), B("eqo", EQ[6]), OP.mult, OP.max)
         if t == R - 1:
             act(B("olf"), B("la"), AF.Identity, bias=224.0)
             dma("y", T.ol[:, :], T["olf"][0:128:16, :], [], [B("olf")])
-        tt(B("d1"), last16("df", M), B("lk2"), OP.max)
-        tt(B("d2"), B("d1"), B("dc"), OP.max)
-        tt(B("d3"), B("d2"), B("nt"), OP.min)
+        tt(B("d1", 0, 6), B("df", 95, EQ[6], 96), B("lk2", 0, 6), OP.max)
+        tt(B("d1", 6, MS), B("df", EQ[6] + 191, EQ[MS], 192), B("lk2", 6, MS), OP.max)
+        if first:
+            quant("v", 128, "vt")
+        tt(B("d3"), B("d1"), B("nt"), OP.min)
         sc(B("offd"), B("d3"), -2.0, OP.add)
         vcopy(I(B("st"), B("offd")), B("kv"))
         mask("stm", B("st", 0, C))
@@ -495,23 +530,28 @@ def rank_program(g, core, T, topo):
             mm("pd%d" % b, M, "w", n_a, la=128 * b)
         for b in range(4):
             h, pd = B(x, 4 * C + b, 4 * (C + M), 4), B("pd%d" % b, 0, M)
-            if b < 3:
+            if b % 2 == 0:
                 act(h, pd, scale=0.0625)
             else:
                 sc(h, pd, 0.0625, OP.mult)
-        for b in range(4):
-            o, w = B(xn, b, 4 * C, 4), I(B(x), B("offx", NS * b, NS * b + NS))
+
+        def pick(b, h):
+            o, w = B(xn, 4 * H * h + b, 4 * H * (h + 1), 4), I(B(x), B("offx", NS * b + HS * h, NS * b + HS * h + HS))
             if b % 2:
                 act(o, w, scale=0.5)
             else:
                 sc(o, w, 0.5, OP.mult)
-        quant("x", C, xn)
-    half = C // 2
-    mm("pss", half, "v", "x")
-    mm("psm", half, "v", "x", ra=half)
+
+        for b, h in ((0, 0), (1, 0), (2, 0), (3, 0), (0, 1), (1, 1), (3, 1)):
+            pick(b, h)
+        quant("x", H, xn)
+        pick(2, 1)
+        quant("x", H, xn, H)
+    mm("pss", H, "v", "x")
+    mm("psm", H, "v", "x", ra=H)
     dma("y", T.oc[:, :], T["qx"][:, 0:C].bitcast(dt.uint8), [], [B("qx")])
-    vcopy(B("yo", 0, half), B("pss", 0, half))
-    act(B("yo", half, C), B("psm", 0, half))
+    act(B("yo", 0, H), B("pss", 0, H))
+    vcopy(B("yo", H, C), B("psm", 0, H))
     dma("s", T.y[:, :], T["yo"][:, :], [], [B("yo")])
     for k in range(4):
         dma("y", T.osc[4 * k:4 * k + 4, :], T["sx"][32 * k:32 * k + 4, 0:C], [], [B("sx")])

@@ -3,12 +3,15 @@ from concourse.mybir import dt, AluOpType, ActivationFunctionType
 C, M, R, NS, MS = 448, 192, 3, 28, 12
 H, HS = C // 2, NS // 2
 ROUND16 = 201326592.0
-TILES = [(448, ("d", "d", 26, 27)), (400, (22, 23, 24, 25)), (336, (18, 19, 20, 21)), (272, (14, 15, 16, 17)),
-         (208, (10, 11, 12, 13)), (144, (6, 7, 8, 9)), (256, (2, 3, 4, 5))]
+TILES = [(448, ("d", 25, 26, 27)), (384, (21, 22, 23, 24)), (320, (17, 18, 19, 20)), (256, (13, 14, 15, 16)),
+         (192, (9, 10, 11, 12)), (128, (5, 6, 7, 8)), (128, (1, 2, 3, 4))]
 LAST = len(TILES) - 1
-LOW = 144
-BYSIGN = (27, 26, 24, 22, 18, 14)
+LATE, LOW = 4, 192
+DENSE = 65
+WIDE = C + DENSE + 2 * (M - DENSE)
+BYSIGN = (27, 26, 23, 21, 17)
 EQ = [96 * k for k in range(6)] + [576 + 192 * k for k in range(7)]
+HS_ = 3
 EARLY = 18
 OP = AluOpType
 AF = ActivationFunctionType
@@ -44,13 +47,13 @@ def _packmx(buf, parts):
 
 
 for _n in ("xa", "xb"):
-    _sb(_n, 4 * (C + M), "bfloat16")
+    _sb(_n, 4 * WIDE, "bfloat16")
 for _n, _w in (("cr", 4 * C), ("tl", 4 * C), ("zt", 4 * M), ("ut", 512), ("vt", 512), ("dg", 512)):
     _sb(_n, _w, "bfloat16")
 _pack("kt", "bfloat16", [("ones", 528), ("grp", 128), ("grp0", 128), ("unit", 256), ("sgt", 512), ("fst", 512), ("rtt", 4 * 176), ("ont", 512), ("et", 528)])
 _pack("tb", "bfloat16", [("t%d" % b, C) for b in range(4)])
 _pack("ctb", "bfloat16", [("ct%d" % q, 4 * TILES[q][0]) for q in range(len(TILES))])
-_pack("kb", "bfloat16", [("mk", C + 16), ("nmk", C + 16), ("i16", C + 16), ("iotaj", C), ("amp", 16), ("cc", EQ[MS]), ("kv", M)])
+_pack("kb", "bfloat16", [("mk", C), ("nmk", C), ("i16", C), ("iotaj", C), ("far", M), ("farm", M), ("amp", M), ("cc", EQ[MS]), ("kv", M)])
 _pack("sgn", "bfloat16", [("sgn%d" % k, 16 * k) for k in BYSIGN])
 _packmx("k", [("e0", 128), ("e1", 128), ("e2", 128), ("e3", 128), ("sg", 128), ("fs", 128), ("on", 128), ("rt", 176)])
 _packmx("c", [("c%d" % q, TILES[q][0]) for q in range(len(TILES))])
@@ -60,14 +63,14 @@ for _t in range(R):
     _mx("z%d" % _t, M)
     _mx("a%d" % _t, M)
 for _n, _w in (("junk0", C), ("junk1", C), ("junk2", C), ("ot", C), ("la", C), ("lm", C), ("lf", C), ("lk", C), ("lkm", M), ("lkf", M),
-               ("df", EQ[MS]), ("eqo", EQ[MS]), ("st", C + M), ("stm", C), ("stf", C), ("em", C), ("ef", C), ("em2", LOW), ("ef2", LOW), ("rm", C), ("rf", C)):
+               ("df", EQ[MS]), ("eqo", EQ[MS]), ("st", 2048), ("stm", C), ("stf", C), ("em", C), ("fsum", C), ("ef", C), ("em2", LOW), ("ef2", LOW), ("rm", C), ("rf", C)):
     _sb(_n, _w, "bfloat16")
-for _n, _w in (("sm", C + 16), ("swf", C + 16), ("iot512", C), ("kca", C), ("ka", C), ("yo", C), ("olf", C)):
+for _n, _w in (("sm", C), ("swf", C), ("iot512", C), ("kca", C), ("ka", C), ("yo", C), ("olf", C)):
     _sb(_n, _w, "float32")
-_pack("fk", "float32", [("pm", 1), ("pg", 1), ("p3", 1), ("k16", NS), ("kc", NS), ("j448", NS), ("nt", MS)])
-_pack("fw", "float32", [("rs", NS), ("z", NS), ("kw", NS), ("kf", 16), ("qs", 56), ("lo", 56), ("hi", 56), ("l2", 56), ("h2", 56), ("s1", 56), ("s4", 56),
-                        ("gy", 56), ("s3", 56), ("l3", NS), ("gx", NS), ("b2", NS), ("n1", NS), ("n2", NS), ("mn", NS), ("mxv", NS), ("spr", NS),
-                        ("m1", NS), ("m2", NS), ("m3", NS), ("m4", NS), ("m5", NS), ("med", NS), ("lk2", MS), ("d1", MS), ("d3", MS), ("sxw", NS)])
+_pack("fk", "float32", [("pm", 1), ("pg", 1), ("p3", 1), ("base", 1), ("k16", NS), ("kc", NS), ("jw", NS)])
+_pack("fw", "float32", [("rs", NS), ("z", NS), ("zd", NS), ("kw", NS), ("kf", 16), ("qs", 56), ("lo", 56), ("hi", 56), ("l2", 56), ("h2", 56), ("s1", 56), ("s4", 56),
+                        ("gy", 56), ("s3", 56), ("l3", 56), ("gx", NS), ("b2", NS), ("n1", NS), ("n2", NS), ("mn", NS), ("mxv", NS), ("spr", NS),
+                        ("m1", NS), ("m2", NS), ("m3", NS), ("m4", NS), ("m5", NS), ("med", NS), ("lk2", MS), ("d1", MS)])
 _pack("ki", "int32", [("ip", 1), ("ia", 1), ("ib", 1), ("ic", 1), ("if2", 8)])
 for _n, _w in (("offu", 8), ("offe", 2), ("offq", NS), ("offt", NS), ("offs", NS), ("offr", NS), ("offk", MS), ("offl", NS), ("offd", MS), ("offx", 4 * NS)):
     _sb(_n, _w, "uint16")
@@ -198,8 +201,9 @@ def rank_program(g, core, T, topo):
         else:
             issue("v", [out], ins, lambda: g.vector.tensor_scalar(ap(out), ap(a), x1, s2, op0, op1))
 
-    def scan(out, d0, d1, op0, op1):
-        issue("v", [out], [d0, d1], lambda: g.vector.tensor_tensor_scan(ap(out), ap(d0), ap(d1), 0.0, op0, op1))
+    def scan(out, d0, d1, op0, op1, init=None):
+        issue("v", [out], [d0, d1] + ([init] if init else []),
+              lambda: g.vector.tensor_tensor_scan(ap(out), ap(d0), ap(d1), ap(init) if init else 0.0, op0, op1))
 
     def vcopy(out, a):
         ins = srcs(a) + ([out[4]] if len(out) > 4 and out[4] is not None else [])
@@ -265,28 +269,28 @@ def rank_program(g, core, T, topo):
     def hi(n):
         return B(n, NS, 2 * NS)
 
-    dma("y", T["xa"][:, 0:4 * C], T.x[:, :], [B("xa", 0, 4 * C)], [])
     dma("s", T["ut"][:, :], T.u[:, :], [B("ut")], [])
+    for h in range(2):
+        a, b = 4 * H * h, 4 * H * (h + 1)
+        dma("y", T["xa"][:, a:b], T.x[:, a:b], [B("xa", a, b)], [])
     deps("y", [], [B("xa", 0, 4 * C)])
     dma("y", T["qw"][:, 0:512].bitcast(dt.uint8), T.wc[:, :], [B("qw")], [])
     dma("y", T["sw"][:, :], T.ws[:, :], [B("sw")], [])
-    dma("y", T["vt"][:, :], T.v[:, :], [B("vt")], [])
 
     iota(B("if2"), [[16, 8]], 0, 0)
     iota(B("ip"), [[0, 1]], 0, 1)
     fill(B("ones"), 1.0)
-    iota(B("i16"), [[0, NS + 1], [1, 16]], 0, 0)
-    iota(B("k16"), [[16, NS]], 0, 0)
+    iota(B("i16"), [[0, NS], [1, 16]], 0, 0)
+    iota(B("ct5", 320, 512), [[0, 192]], 0, 0)
     one = B("ones", 0, 128)
     sel(B("grp0"), one, [[-16, 8], [0, 16]], OP.is_ge, 0, 1)
     sel(B("grp"), B("grp0"), [[16, 8], [0, 16]], OP.is_ge, 15, -1)
     sel(B("fst", 0, 512, 4), B("grp"), [[1, 128]], OP.is_gt, 0, -1)
-    sel(B("fst", 1, 512, 4), B("grp"), [[-1, 128]], OP.is_gt, 0, 1)
-    zeros("ct%d" % LAST, 0, 1024)
+    zeros("ct%d" % LAST, 0, 512)
     zeros("dg", 0, 512)
-    for q, (w, slots) in enumerate(TILES[:LAST]):
+    for q in range(5):
+        w = TILES[q][0]
         iota(B("ct%d" % q, 4 * w - 192, 4 * w), [[0, 192]], 0, 0)
-    fill(B("sm", C, C + 16), 0.0)
     fill(B("rs", 0, 1), 0.0)
     vcopy(B("offu"), B("if2"))
     sc(B("ia"), B("ip"), 15, OP.bitwise_and)
@@ -295,23 +299,21 @@ def rank_program(g, core, T, topo):
     vcopy(B("pm"), B("ia"))
     vcopy(B("pg"), B("ib"))
     sc(B("p3"), B("ic"), 8.0, OP.mult)
-    sc(B("mk"), B("i16"), B("pm"), OP.is_equal)
-    sc(B("nmk"), B("i16"), B("pm"), OP.not_equal)
     sc(B("offe", 0, 1), B("p3"), B("pg"), OP.add, float(NS - 1), OP.min)
+    sc(B("mk"), B("i16"), B("pm"), OP.is_equal)
     quant("u", 128, "ut")
-    sc(B("j448"), B("k16"), B("pm"), OP.add, -448.0, OP.add)
+    sc(B("nmk"), B("i16"), B("pm"), OP.not_equal)
     vcopy(I(B("qux"), None, "codes"), I(B("qu"), B("offu"), "codes"))
     act(B("sux"), I(B("su"), B("offu")))
-    sc(B("nt"), B("k16", 0, MS), B("pm"), OP.add, 450.0, OP.add)
-    sc(B("kc"), B("j448"), 447.5, OP.add, -1.0 / 512, OP.mult)
-    sc(B("amp"), B("mk", 0, 16), 1023.0, OP.mult, 1.0, OP.add)
-    quant("c%d" % LAST, 256, "ct%d" % LAST)
-    for e in (2, 3):
+    for e in (1, 2, 3):
         act(B("fst", e, 512, 4), B("grp"), scale=-1.0)
     for e in range(4):
         act(B("sgt", e, 512, 4), B("grp"), scale=-1.0)
     for h in range(2):
         quant("x", H, "xa", H * h)
+    sc(B("base"), B("pm"), -1.0, OP.mult, 232.0, OP.add)
+    iota(B("k16"), [[16, NS]], 0, 0)
+    iota(B("far"), [[8, M]], 512, 0)
 
     sel(B("unit"), B("ones", 0, 256), [[0, 2], [-1, 128]], OP.is_equal, 0, 1)
     sel(B("et", 0, 516), B("ones", 0, 516), [[-1, 516]], OP.is_equal, 3, 4)
@@ -320,12 +322,9 @@ def rank_program(g, core, T, topo):
     iota(B("kca"), [[-1, C]], 0, 0)
     sel(B("ont"), B("ones", 0, 512), [[0, 128], [-1000, 4]], OP.is_gt, 3064, -1)
     iota(B("cc"), [[0, EQ[MS]]], 1, 0)
-    for k in range(MS):
-        sel(B("cc", EQ[k] + 16 * k, EQ[k] + 16 * k + 16), B("amp"), [[0, 16]], OP.is_ge, 0, 0)
-    iota(B("cc", 0, EQ[6], 96), [[0, 6]], 0, 0)
-    iota(B("cc", EQ[6], EQ[MS], 192), [[0, 6]], 0, 0)
     iota(B("eqo"), [[0, EQ[MS]]], 0, 0)
-    iota(B("kv"), [[1, M]], 0, 0)
+    iota(B("kv", 0, DENSE), [[1, DENSE]], C - 256, 0)
+    iota(B("kv", DENSE, M), [[2, M - DENSE]], C + DENSE + 1 - 256, 0)
 
     X = ["xa", "xb"]
     for t in range(R):
@@ -337,71 +336,93 @@ def rank_program(g, core, T, topo):
                 quant("e%d" % b, 128, "et", shift=3 - b)
                 mm("pd%d" % b, C, "e%d" % b, "x")
 
-        mm("psr", H, "ux", "x")
-        mm("psa", H, "ux", "x", ra=H)
+        mm("pd0", H, "ux", "x")
+        mm("pd1", H, "ux", "x", ra=H)
         mm("pss", C, "ux", "x")
         mm("psm", C, "ux", "x")
         if not first:
-            for b in range(4):
+            for b in (2, 3):
                 mm("pd%d" % b, C, "e%d" % b, "x")
-        mask_psum("sm", "psr", 0, H)
-        mask_psum("sm", "psa", H, H)
-        if first:
-            quant("fs", 128, "fst")
-        hold("swf", "sm", C + 16)
-        if first:
-            quant("sg", 128, "sgt")
-        iota(B("st", 0, C), [[0, C]], -512, 0)
+        iota(B("st", 0, C), [[1, C]], -256, 0)
 
         def signs(q):
             for k in reversed(TILES[q][1]):
                 if k in BYSIGN:
                     act(B("sgn%d" % k), B("psm", 0, 16 * k), AF.Sign, scale=-1.0, bias=B("swf", 16 * k + 15, 16 * k + 16))
 
-        def compare(k, c):
+        def compare(q, e, k):
+            c = B("ct%d" % q, e, 64 * k, 4)
             if k in BYSIGN:
                 sc(c, B("sgn%d" % k), 0.0, OP.is_le, -0.5, OP.add)
             else:
-                sc(c, B("pss", 0, 16 * k), B("swf", 16 * k + 15, 16 * k + 16), OP.is_ge, -0.5, OP.add)
+                sc(c, B("pd0" if q > LATE else "pss", 0, 16 * k), B("swf", 16 * k + 15, 16 * k + 16), OP.is_ge, -0.5, OP.add)
             row_sum(B("rs", k, k + 1), c, 16 * k)
 
         def summed(q):
-            if q < LAST - 1:
-                quant("c%d" % q, TILES[q][0], "ct%d" % q)
-                mm("psa", TILES[q][0], "sg" if q else "fs", "c%d" % q, q == 0, q == LAST - 2)
-            elif q < LAST:
-                quant("c%d" % q, LOW, "ct%d" % q)
-                mm("psr", LOW, "sg", "c%d" % q, True, False)
-            else:
-                quant("c%d" % q, LOW, "ct%d" % q)
-                mm("psr", 128, "sg", "c%d" % q, False, False)
-                mm("psr", 128, "sg", "c%d" % q, False, True, ra=128)
+            w = TILES[q][0]
+            quant("c%d" % q, w, "ct%d" % q)
+            if q == LATE:
+                mm("psr", w, "sg", "c%d" % q)
+                return
+            mm("psa", w, "sg" if q else "fs", "c%d" % q, q == 0, q == LATE - 1)
+            if q == 0:
+                for n in (LAST - 1, LAST):
+                    mm("psa", 128, "sg", "c%d" % n, False, False)
+                if not first:
+                    for b in (0, 1):
+                        mm("pd%d" % b, C, "e%d" % b, "x")
 
+        mask_psum("sm", "pd0", 0, H)
+        hold("swf", "sm", H)
+        mask_psum("sm", "pd1", H, H)
+        for e in (3, 2):
+            compare(LAST - 1, e, 5 + e)
+        scan(B("swf", H), B("nmk", H), B("sm", H), OP.mult, OP.add)
+        for e in (1, 0):
+            compare(LAST - 1, e, 5 + e)
         signs(0)
-        for q, (w, slots) in enumerate(TILES):
-            ct = "ct%d" % q
+        for e in (3, 2, 1, 0):
+            compare(LAST, e, 1 + e)
+        quant("c%d" % (LAST - 1), 128, "ct%d" % (LAST - 1))
+        if first:
+            quant("fs", 128, "fst")
+            quant("sg", 128, "sgt")
+        quant("c%d" % LAST, 128, "ct%d" % LAST)
+        for q, (w, slots) in enumerate(TILES[:LATE + 1]):
             order = [e for e in (3, 2, 1, 0) if slots[e] not in BYSIGN] + [e for e in (3, 2, 1, 0) if slots[e] in BYSIGN]
-            if q < LAST:
-                signs(q + 1)
+            signs(q + 1)
             for e in order:
                 k = slots[e]
                 if k == "d":
-                    tt(B(ct, e, 4 * C, 4), B("pss", 0, C), B("swf", 16 * e, 16 * e + C), (OP.is_le, OP.is_lt)[e])
+                    tt(B("ct0", 0, 4 * C, 4), B("pss", 0, C), B("swf"), OP.is_le)
                 else:
-                    compare(k, B(ct, e, 64 * k, 4))
+                    compare(q, e, k)
                 if q and e == order[0]:
                     summed(q - 1)
-        compare(1, B("ct%d" % LAST, 512, 576, 4))
+                if q == 1 and e == order[1]:
+                    scan(B("fsum"), B("nmk"), B("ct0", 0, 4 * C, 4), OP.mult, OP.add)
         mask_psum("em", "psa", 0, C)
-        summed(LAST)
+        summed(LATE)
         hold("ef", "em")
         if first:
             for e in range(4):
-                a = 16 + 48 * (e // 2)
+                a = 64 * (e // 2)
                 act(B("rtt", e, 4 * 176, 4), B("unit", a, a + 176))
         unit_tile(0)
+        if first:
+            mask("farm", B("far"), M)
+            sc(B("jw"), B("k16"), B("pm"), OP.add, -0.5, OP.add)
+        tt(B("zd"), last16("ef"), last16("fsum"), OP.subtract)
         mask_psum("em2", "psr", 0, LOW)
-        tt(B("z"), last16("ef"), B("rs"), OP.add)
+        if first:
+            sc(B("amp"), B("farm"), 1.0, OP.max)
+            sc(B("kc"), B("jw"), -1.0 / 512, OP.mult)
+            for k in range(MS):
+                sel(B("cc", EQ[k] + 16 * k, EQ[k] + 16 * k + 16), B("amp", 16 * k, 16 * k + 16), [[0, 16]], OP.is_ge, 0, 0)
+            iota(B("cc", 0, EQ[6], 96), [[0, 6]], 0, 0)
+            iota(B("cc", EQ[6], EQ[MS], 192), [[0, 6]], 0, 0)
+            dma("g", T["vt"][:, :], T.v[:, :], [B("vt")], [])
+        tt(B("z"), B("zd"), B("rs"), OP.add)
         hold("ef2", "em2", LOW)
         unit_tile(1)
         tt(B("z", 0, LOW // 16), last16("ef2", LOW), B("z", 0, LOW // 16), OP.add)
@@ -411,13 +432,13 @@ def rank_program(g, core, T, topo):
             quant("rt", 176, "rtt")
         sc(B("dg", 0, 112, 4), B("z"), ROUND16, OP.add, -ROUND16, OP.add)
         sc(B("dg", 114, 224, 4), B("z"), ROUND16, OP.add, -ROUND16, OP.add)
-        sc(B("offq"), B("z"), 216.0, OP.add)
+        sc(B("offq"), B("z"), B("base"), OP.add)
         tt(B("dg", 1, 112, 4), B("z"), B("dg", 0, 112, 4), OP.subtract)
         tt(B("dg", 115, 224, 4), B("z"), B("dg", 0, 112, 4), OP.subtract)
         if first:
             quant("on", 128, "ont")
         quant("dg", 128, "dg")
-        for n, bank in ((1, "psm"), (2, "psr"), (0, "pss"), (3, "psa")):
+        for n, bank in ((2, "psm"), (3, "psr"), (1, "pss"), (0, "psa")):
             mm(bank, 128, "rt", "dg", la=16 * n)
 
         def by_place(h):
@@ -426,29 +447,25 @@ def rank_program(g, core, T, topo):
         by_place(0)
         act(B("qs"), B("psm", 0, 56))
         act(B("l2"), B("psr", 0, 56))
-        act(lo("h2"), lo("psr"))
         tt(B("lo"), B("pss", 0, 56), B("qs"), OP.min)
         tt(B("hi"), B("pss", 0, 56), B("qs"), OP.max)
-        tt(hi("h2"), hi("psa"), hi("l2"), OP.max)
-        tt(B("l3"), hi("psa"), hi("l2"), OP.min)
+        tt(B("l3"), B("psa", 0, 56), B("l2"), OP.min)
+        tt(B("h2"), B("psa", 0, 56), B("l2"), OP.max)
         unit_tile(2)
+        tt(B("s1"), B("lo"), B("l3"), OP.min)
         tt(B("s4"), B("hi"), B("h2"), OP.max)
-        tt(lo("s1"), lo("lo"), lo("l2"), OP.min)
-        tt(hi("s1"), hi("lo"), B("l3"), OP.min)
-        tt(B("n2"), lo("s4"), hi("s4"), OP.max)
+        tt(lo("gy"), lo("hi"), lo("l2"), OP.min)
         unit_tile(3)
-        tt(B("n1"), lo("s1"), hi("s1"), OP.min)
-        tt(B("mxv"), B("n2"), B("z"), OP.max)
-        tt(B("gy"), B("hi"), B("h2"), OP.min)
-        tt(B("mn"), B("n1"), B("z"), OP.min)
-        tt(B("gx"), hi("lo"), B("l3"), OP.max)
-        tt(B("m1"), lo("s4"), hi("s1"), OP.max)
+        tt(B("mn"), lo("s1"), hi("s1"), OP.min)
+        tt(B("mxv"), lo("s4"), hi("s4"), OP.max)
+        tt(hi("gy"), hi("hi"), hi("h2"), OP.min)
+        tt(B("gx"), hi("lo"), hi("l3"), OP.max)
         tt(B("spr"), B("mxv"), B("mn"), OP.subtract)
-        tt(lo("s3"), lo("lo"), lo("gy"), OP.max)
-        tt(hi("s3"), B("gx"), hi("gy"), OP.max)
+        tt(B("n1"), lo("lo"), lo("l2"), OP.min)
+        tt(B("n2"), lo("hi"), lo("l2"), OP.max)
         sc(B("offs"), B("spr"), 0.0, OP.add)
         tt(B("kw"), B("spr"), B("kc"), OP.add)
-        tt(B("b2"), B("gx"), hi("gy"), OP.min)
+        tt(lo("s3"), lo("lo"), lo("gy"), OP.max)
         for b in (2, 3):
             act(B("t%d" % b), B("pd%d" % b, 0, C))
         for h in range(2):
@@ -457,7 +474,10 @@ def rank_program(g, core, T, topo):
         for h in range(2):
             for e in range(4):
                 act(B("cr", 4 * H * h + e, 4 * H * (h + 1), 4), B("ka", H * h, H * h + H), AF.Sign, scale=-1.0, bias=B("kf", e, e + 1))
-        tt(B("m3"), lo("s1"), hi("s3"), OP.max)
+        tt(hi("s3"), B("gx"), hi("gy"), OP.max)
+        tt(B("b2"), B("gx"), hi("gy"), OP.min)
+        tt(B("m1"), B("n2"), hi("s1"), OP.max)
+        tt(B("m3"), B("n1"), hi("s3"), OP.max)
         tt(B("m2"), lo("s3"), B("b2"), OP.max)
         tt(B("m4"), B("m1"), hi("s4"), OP.min)
         tt(B("m5"), B("m2"), B("m3"), OP.min)
@@ -465,8 +485,10 @@ def rank_program(g, core, T, topo):
         tt(B("med"), B("m4"), B("m5"), OP.min)
         quant("cr", H, "cr")
         mm("psr", H, "on", "cr")
-        sc(B("offt"), B("med"), 216.0, OP.add)
+        sc(B("offt"), B("med"), B("base"), OP.add)
         act(B("la"), I(B("ot"), B("offt")))
+        if t < 2:
+            zeros(x, 4 * (C + DENSE), 4 * WIDE)
         quant("cr", H, "cr", H)
         mm("psa", H, "on", "cr", ra=H)
         mask_psum("rm", "psr", 0, H)
@@ -491,14 +513,23 @@ def rank_program(g, core, T, topo):
         mask("lkm", B("lk", 0, M), M)
         hold("lkf", "lkm", M)
         sc(B("offk"), last16("lkf", M), 224.0, OP.add)
-        sc(B("lk2"), last16("lkf", M), 226.0, OP.add)
         n_z, n_a = "z%d" % t, "a%d" % t
-        for b in range(4):
+
+        def same(k0, k1):
+            for k in range(k0, k1):
+                sc(B("eqo", EQ[k], EQ[k] + 16 * k + 16), B("lk", 0, 16 * k + 16), B("lkf", 16 * k + 15, 16 * k + 16), OP.is_equal)
+
+        def seen(k0, k1):
+            scan(B("df", EQ[k0], EQ[k1]), B("cc", EQ[k0], EQ[k1]), B("eqo", EQ[k0], EQ[k1]), OP.mult, OP.max)
+
+        same(6, 8)
+        vcopy(B("zt", 0, 4 * M, 4), I(B("t0"), B("offk")))
+        for b in (1, 2, 3):
             act(B("zt", b, 4 * M, 4), I(B("t%d" % b), B("offk")))
+        act(B("lk2"), last16("lkf", M), AF.Identity, bias=226.0)
         picked(EARLY, NS)
-        for k in range(MS):
-            sc(B("eqo", EQ[k], EQ[k] + 16 * k + 16), B("lk", 0, 16 * k + 16), B("lkf", 16 * k + 15, 16 * k + 16), OP.is_equal)
-        scan(B("df", 0, EQ[6]), B("cc", 0, EQ[6]), B("eqo", 0, EQ[6]), OP.mult, OP.max)
+        same(8, MS)
+        same(0, 2)
         quant(n_z, M, "zt")
         to = T.cores[(rank + 1 + t) % len(T.cores)]
         rid, pid, _se = topo.addr(to)
@@ -509,31 +540,32 @@ def rank_program(g, core, T, topo):
         for view, es in ((lambda n: T["q" + n][:, 0:M].bitcast(dt.uint8), wide), (lambda n: T["s" + n][:, 0:M], thin)):
             g.remote_dma(view(n_a), view(n_z), T.sem["arr%d" % t], T.sem["snd%d" % t], pid, rid, sum(1 << e for e in es))
         add(EARLY, NS)
-        scan(B("df", EQ[6]), B("cc", EQ[6]), B("eqo", EQ[6]), OP.mult, OP.max)
+        same(2, 6)
+        seen(6, MS)
+        seen(0, 6)
         if t == R - 1:
             act(B("olf"), B("la"), AF.Identity, bias=224.0)
             dma("y", T.ol[:, :], T["olf"][0:128:16, :], [], [B("olf")])
-        tt(B("d1", 0, 6), B("df", 95, EQ[6], 96), B("lk2", 0, 6), OP.max)
         tt(B("d1", 6, MS), B("df", EQ[6] + 191, EQ[MS], 192), B("lk2", 6, MS), OP.max)
+        tt(B("d1", 0, 6), B("df", 95, EQ[6], 96), B("lk2", 0, 6), OP.max)
         if first:
             quant("v", 128, "vt")
-        tt(B("d3"), B("d1"), B("nt"), OP.min)
-        sc(B("offd"), B("d3"), -2.0, OP.add)
+        sc(B("offd"), B("d1"), -2.0, OP.add)
         vcopy(I(B("st"), B("offd")), B("kv"))
         mask("stm", B("st", 0, C))
         hold("stf", "stm")
-        tt(B("sxw"), last16("stf"), B("j448"), OP.max)
         for b in (1, 0, 3, 2):
-            sc(B("offx", NS * b, NS * b + NS), B("sxw"), 4.0, OP.mult, 4.0 * C + b, OP.add)
+            sc(B("offx", NS * b, NS * b + NS), last16("stf"), 4.0, OP.mult, 1024.0 + b, OP.add)
         wait("t", "arr%d" % t, got)
         for b in range(4):
             mm("pd%d" % b, M, "w", n_a, la=128 * b)
         for b in range(4):
-            h, pd = B(x, 4 * C + b, 4 * (C + M), 4), B("pd%d" % b, 0, M)
-            if b % 2 == 0:
-                act(h, pd, scale=0.0625)
-            else:
-                sc(h, pd, 0.0625, OP.mult)
+            for o, i in ((B(x, 4 * C + b, 4 * (C + DENSE), 4), B("pd%d" % b, 0, DENSE)),
+                         (B(x, 4 * (C + DENSE + 1) + b, 4 * WIDE, 8), B("pd%d" % b, DENSE, M))):
+                if b < HS_:
+                    act(o, i, scale=0.0625)
+                else:
+                    sc(o, i, 0.0625, OP.mult)
 
         def pick(b, h):
             o, w = B(xn, 4 * H * h + b, 4 * H * (h + 1), 4), I(B(x), B("offx", NS * b + HS * h, NS * b + HS * h + HS))
@@ -547,12 +579,12 @@ def rank_program(g, core, T, topo):
         quant("x", H, xn)
         pick(2, 1)
         quant("x", H, xn, H)
-    mm("pss", H, "v", "x")
-    mm("psm", H, "v", "x", ra=H)
-    dma("y", T.oc[:, :], T["qx"][:, 0:C].bitcast(dt.uint8), [], [B("qx")])
-    act(B("yo", 0, H), B("pss", 0, H))
-    vcopy(B("yo", H, C), B("psm", 0, H))
-    dma("s", T.y[:, :], T["yo"][:, :], [], [B("yo")])
+    for h, bank in enumerate(("pss", "psm")):
+        a, b = H * h, H * h + H
+        mm(bank, H, "v", "x", ra=a)
+        dma("y", T.oc[:, 4 * a:4 * b], T["qx"][:, a:b].bitcast(dt.uint8), [], [B("qx", a, b)])
+        act(B("yo", a, b), B(bank, 0, H))
+        dma("s", T.y[:, a:b], T["yo"][:, a:b], [], [B("yo", a, b)])
     for k in range(4):
         dma("y", T.osc[4 * k:4 * k + 4, :], T["sx"][32 * k:32 * k + 4, 0:C], [], [B("sx")])
     for t in range(R):

@@ -1,15 +1,19 @@
+import math
 from concourse.mybir import dt, AluOpType, ActivationFunctionType
 
 C, M, R, NS, MS = 448, 192, 3, 28, 12
 H, HS = C // 2, NS // 2
 ROUND16 = 201326592.0
-TILES = [(448, ("d", 25, 26, 27)), (384, (21, 22, 23, 24)), (320, (17, 18, 19, 20)), (256, (13, 14, 15, 16)),
+TILES = [(448, (25, 26, 27, "d")), (384, (21, 22, 23, 24)), (320, (17, 18, 19, 20)), (256, (13, 14, 15, 16)),
          (192, (9, 10, 11, 12)), (128, (5, 6, 7, 8)), (128, (1, 2, 3, 4))]
 LAST = len(TILES) - 1
-LATE, LOW = 4, 192
+ORDER = (4, 5, 0, 1, 2, 3, 6)
+FOLD = [(224, 2), (128, 3), (160, 2), (128, 2), (192, 1), (128, 1)]
+ROUND512 = 6442450944.0
+LATE, LOW = 6, 256
 DENSE = 65
 WIDE = C + DENSE + 2 * (M - DENSE)
-BYSIGN = (27, 26, 23, 21, 17)
+BYSIGN = (27, 26, 25, 24, 23, 22, 21, 19, 18, 17, 15, 14, 13)
 EQ = [96 * k for k in range(6)] + [576 + 192 * k for k in range(7)]
 HS_ = 3
 EARLY = 18
@@ -50,13 +54,15 @@ for _n in ("xa", "xb"):
     _sb(_n, 4 * WIDE, "bfloat16")
 for _n, _w in (("cr", 4 * C), ("tl", 4 * C), ("zt", 4 * M), ("ut", 512), ("vt", 512), ("dg", 512)):
     _sb(_n, _w, "bfloat16")
-_pack("kt", "bfloat16", [("ones", 528), ("grp", 128), ("grp0", 128), ("unit", 256), ("sgt", 512), ("fst", 512), ("rtt", 4 * 176), ("ont", 512), ("et", 528)])
+_pack("kt", "bfloat16", [("ones", 528), ("grp", 128), ("grp0", 128), ("unit", 256), ("sgt", 512), ("fst", 512), ("rtt", 4 * 176), ("ont", 512), ("et", 528), ("wt", 528)])
 _pack("tb", "bfloat16", [("t%d" % b, C) for b in range(4)])
-_pack("ctb", "bfloat16", [("ct%d" % q, 4 * TILES[q][0]) for q in range(len(TILES))])
-_pack("kb", "bfloat16", [("mk", C), ("nmk", C), ("i16", C), ("iotaj", C), ("far", M), ("farm", M), ("amp", M), ("cc", EQ[MS]), ("kv", M)])
+ROOM = [LOW if q == ORDER[0] else TILES[q][0] for q in range(len(TILES))]
+_pack("ctb", "bfloat16", [("ct%d" % q, 4 * ROOM[q]) for q in range(len(TILES))])
+_pack("kb", "bfloat16", [("mk", C), ("nmk", C), ("i16", C), ("iotaj", C), ("far", M), ("farm", M), ("amp", M), ("cc", EQ[MS]), ("kv", M),
+                         ("big", 112), ("up", 112), ("down", 112)])
 _pack("sgn", "bfloat16", [("sgn%d" % k, 16 * k) for k in BYSIGN])
-_packmx("k", [("e0", 128), ("e1", 128), ("e2", 128), ("e3", 128), ("sg", 128), ("fs", 128), ("on", 128), ("rt", 176)])
-_packmx("c", [("c%d" % q, TILES[q][0]) for q in range(len(TILES))])
+_packmx("k", [("e0", 128), ("e1", 128), ("e2", 128), ("e3", 128), ("sg", 128), ("fs", 128), ("on", 128), ("rt", 176), ("w0", 128), ("w1", 128)])
+_packmx("c", [("c%d" % q, ROOM[q]) for q in range(len(TILES))])
 for _n, _w in (("u", 128), ("ux", 128), ("v", 128), ("w", 512), ("x", C), ("dg", 128), ("cr", C)):
     _mx(_n, _w)
 for _t in range(R):
@@ -65,19 +71,19 @@ for _t in range(R):
 for _n, _w in (("junk0", C), ("junk1", C), ("junk2", C), ("ot", C), ("la", C), ("lm", C), ("lf", C), ("lk", C), ("lkm", M), ("lkf", M),
                ("df", EQ[MS]), ("eqo", EQ[MS]), ("st", 2048), ("stm", C), ("stf", C), ("em", C), ("fsum", C), ("ef", C), ("em2", LOW), ("ef2", LOW), ("rm", C), ("rf", C)):
     _sb(_n, _w, "bfloat16")
-for _n, _w in (("sm", C), ("swf", C), ("iot512", C), ("kca", C), ("ka", C), ("yo", C), ("olf", C)):
+for _n, _w in (("sm", C), ("swf", C), ("iot512", C), ("kca", C), ("ka", C), ("yo", C), ("olf", C), ("junkf", C)):
     _sb(_n, _w, "float32")
 _pack("fk", "float32", [("pm", 1), ("pg", 1), ("p3", 1), ("base", 1), ("k16", NS), ("kc", NS), ("jw", NS)])
-_pack("fw", "float32", [("rs", NS), ("z", NS), ("zd", NS), ("kw", NS), ("kf", 16), ("qs", 56), ("lo", 56), ("hi", 56), ("l2", 56), ("h2", 56), ("s1", 56), ("s4", 56),
-                        ("gy", 56), ("s3", 56), ("l3", 56), ("gx", NS), ("b2", NS), ("n1", NS), ("n2", NS), ("mn", NS), ("mxv", NS), ("spr", NS),
-                        ("m1", NS), ("m2", NS), ("m3", NS), ("m4", NS), ("m5", NS), ("med", NS), ("lk2", MS), ("d1", MS)])
+_pack("fw", "float32", [("rs", 32), ("z", NS), ("zd", NS), ("rp", 16), ("rph", 16), ("kw", NS), ("kf", 16), ("qs", 56), ("l2", 56),
+                        ("spr", NS), ("lk2", MS), ("d1", MS)] + [(n, NS) for n in ("gya", "gyb", "gx", "n1", "n2", "a2", "b1", "b2", "b3")])
+_pack("bw", "bfloat16", [(n, 112) for n in ("lo", "hi", "mn", "mxv", "mm", "med")])
 _pack("ki", "int32", [("ip", 1), ("ia", 1), ("ib", 1), ("ic", 1), ("if2", 8)])
 for _n, _w in (("offu", 8), ("offe", 2), ("offq", NS), ("offt", NS), ("offs", NS), ("offr", NS), ("offk", MS), ("offl", NS), ("offd", MS), ("offx", 4 * NS)):
     _sb(_n, _w, "uint16")
 for _n in ("pss", "psa", "psm", "psr", "pd0", "pd1", "pd2", "pd3"):
     SCRATCH[_n] = ("psum", [128, 512], "float32")
 
-SEMAPHORES = ["sv", "ss", "sg", "st"] + ["arr%d" % t for t in range(R)] + ["snd%d" % t for t in range(R)] + ["d%d" % i for i in range(24)]
+SEMAPHORES = ["sv", "ss", "sg", "st"] + ["arr%d" % t for t in range(R)] + ["snd%d" % t for t in range(R)] + ["d%d" % i for i in range(32)]
 
 
 def make_queues(g, T):
@@ -98,7 +104,7 @@ def make_queues(g, T):
     def hit(p, q):
         if p[0] >= q[1] or q[0] >= p[1]:
             return False
-        return not (p[2] == q[2] and p[2] > 1 and (p[0] - q[0]) % p[2])
+        return (p[0] - q[0]) % math.gcd(p[2], q[2]) == 0
 
     def wait(e, src, n):
         if known[e].get(src, 0) >= n:
@@ -263,11 +269,8 @@ def rank_program(g, core, T, topo):
         for c in range(a, b, 512):
             act(B(n, c, min(c + 512, b)), B("ones", 0, min(512, b - c)), scale=0.0)
 
-    def lo(n):
-        return B(n, 0, NS)
-
-    def hi(n):
-        return B(n, NS, 2 * NS)
+    def four(n, a):
+        return B(n, a, 112, 4)
 
     dma("s", T["ut"][:, :], T.u[:, :], [B("ut")], [])
     for h in range(2):
@@ -281,14 +284,14 @@ def rank_program(g, core, T, topo):
     iota(B("ip"), [[0, 1]], 0, 1)
     fill(B("ones"), 1.0)
     iota(B("i16"), [[0, NS], [1, 16]], 0, 0)
-    iota(B("ct5", 320, 512), [[0, 192]], 0, 0)
-    one = B("ones", 0, 128)
-    sel(B("grp0"), one, [[-16, 8], [0, 16]], OP.is_ge, 0, 1)
+    sel(B("unit"), B("ones", 0, 256), [[0, 2], [-1, 128]], OP.is_equal, 0, 1)
+    sel(B("grp0"), B("ones", 0, 128), [[-16, 8], [0, 16]], OP.is_ge, 0, 1)
     sel(B("grp"), B("grp0"), [[16, 8], [0, 16]], OP.is_ge, 15, -1)
-    sel(B("fst", 0, 512, 4), B("grp"), [[1, 128]], OP.is_gt, 0, -1)
-    zeros("ct%d" % LAST, 0, 512)
-    zeros("dg", 0, 512)
-    for q in range(5):
+    sel(B("fst", 3, 512, 4), B("grp"), [[1, 128]], OP.is_gt, 0, -1)
+    zeros("ct4", 512, 1024)
+    zeros("ct5", 320, 512)
+    zeros("wt", 0, 516)
+    for q in range(4):
         w = TILES[q][0]
         iota(B("ct%d" % q, 4 * w - 192, 4 * w), [[0, 192]], 0, 0)
     fill(B("rs", 0, 1), 0.0)
@@ -300,29 +303,39 @@ def rank_program(g, core, T, topo):
     vcopy(B("pg"), B("ib"))
     sc(B("p3"), B("ic"), 8.0, OP.mult)
     sc(B("offe", 0, 1), B("p3"), B("pg"), OP.add, float(NS - 1), OP.min)
+    sc(B("base"), B("pm"), -1.0, OP.mult, 232.0, OP.add)
     sc(B("mk"), B("i16"), B("pm"), OP.is_equal)
     quant("u", 128, "ut")
     sc(B("nmk"), B("i16"), B("pm"), OP.not_equal)
     vcopy(I(B("qux"), None, "codes"), I(B("qu"), B("offu"), "codes"))
     act(B("sux"), I(B("su"), B("offu")))
-    for e in (1, 2, 3):
-        act(B("fst", e, 512, 4), B("grp"), scale=-1.0)
+    act(B("wt", 2, 514, 4), B("unit", 0, 128))
+    act(B("wt", 3, 515, 4), B("unit", 0, 128), scale=512.0)
     for e in range(4):
         act(B("sgt", e, 512, 4), B("grp"), scale=-1.0)
+    for e in range(3):
+        act(B("fst", e, 512, 4), B("grp"), scale=-1.0)
     for h in range(2):
         quant("x", H, "xa", H * h)
-    sc(B("base"), B("pm"), -1.0, OP.mult, 232.0, OP.add)
+    for h in range(2):
+        quant("w%d" % h, 128, "wt", shift=2 - 2 * h)
     iota(B("k16"), [[16, NS]], 0, 0)
     iota(B("far"), [[8, M]], 512, 0)
 
-    sel(B("unit"), B("ones", 0, 256), [[0, 2], [-1, 128]], OP.is_equal, 0, 1)
+    iota(B("ct%d" % LAST), [[0, 512]], 0, 0)
     sel(B("et", 0, 516), B("ones", 0, 516), [[-1, 516]], OP.is_equal, 3, 4)
+    iota(B("dg"), [[0, 512]], 0, 0)
+    for n, c in (("up", 1024), ("down", -1024)):
+        iota(B("big"), [[0, 112]], c, 0)
+        sel(B(n), B("big"), [[0, NS], [1, 4]], OP.is_equal, 0, 0)
     iota(B("iotaj"), [[1, C]], -224, 0)
     iota(B("iot512"), [[512, C]], 0, 0)
     iota(B("kca"), [[-1, C]], 0, 0)
     sel(B("ont"), B("ones", 0, 512), [[0, 128], [-1000, 4]], OP.is_gt, 3064, -1)
-    iota(B("cc"), [[0, EQ[MS]]], 1, 0)
-    iota(B("eqo"), [[0, EQ[MS]]], 0, 0)
+    for a in range(0, EQ[MS], 432):
+        for n, src in (("cc", "ones"), ("eqo", "ct%d" % LAST)):
+            o, i = B(n, a, a + 432), B(src, 0, 432)
+            dma("y", ap(o), ap(i), [o], [i])
     iota(B("kv", 0, DENSE), [[1, DENSE]], C - 256, 0)
     iota(B("kv", DENSE, M), [[2, M - DENSE]], C + DENSE + 1 - 256, 0)
 
@@ -334,15 +347,12 @@ def rank_program(g, core, T, topo):
         def unit_tile(b):
             if first:
                 quant("e%d" % b, 128, "et", shift=3 - b)
-                mm("pd%d" % b, C, "e%d" % b, "x")
+            mm("pd%d" % b, C, "e%d" % b, "x")
 
         mm("pd0", H, "ux", "x")
         mm("pd1", H, "ux", "x", ra=H)
         mm("pss", C, "ux", "x")
         mm("psm", C, "ux", "x")
-        if not first:
-            for b in (2, 3):
-                mm("pd%d" % b, C, "e%d" % b, "x")
         iota(B("st", 0, C), [[1, C]], -256, 0)
 
         def signs(q):
@@ -355,89 +365,103 @@ def rank_program(g, core, T, topo):
             if k in BYSIGN:
                 sc(c, B("sgn%d" % k), 0.0, OP.is_le, -0.5, OP.add)
             else:
-                sc(c, B("pd0" if q > LATE else "pss", 0, 16 * k), B("swf", 16 * k + 15, 16 * k + 16), OP.is_ge, -0.5, OP.add)
-            row_sum(B("rs", k, k + 1), c, 16 * k)
+                sc(c, B("pd0" if q in ORDER[:2] else "pss", 0, 16 * k), B("swf", 16 * k + 15, 16 * k + 16), OP.is_ge, -0.5, OP.add)
+            if q == LATE:
+                row_sum(B("rs", k, k + 1), c, 16 * k)
+
+        def bank(q, h):
+            return ("pd2", "pd3", "pd1", "pd0")[(2 * ORDER.index(q) + h) % 4]
+
+        def rows(q):
+            n = FOLD[q][0]
+            for h in range(2):
+                k = TILES[q][1][2 * h] // 2
+                act(B("junkf", H * h, H * h + n), B(bank(q, h), 0, n), acc=B("rp", k, k + 1))
 
         def summed(q):
             w = TILES[q][0]
             quant("c%d" % q, w, "ct%d" % q)
-            if q == LATE:
-                mm("psr", w, "sg", "c%d" % q)
-                return
-            mm("psa", w, "sg" if q else "fs", "c%d" % q, q == 0, q == LATE - 1)
-            if q == 0:
-                for n in (LAST - 1, LAST):
-                    mm("psa", 128, "sg", "c%d" % n, False, False)
-                if not first:
-                    for b in (0, 1):
-                        mm("pd%d" % b, C, "e%d" % b, "x")
+            if q > 2:
+                mm("psr", LOW if q == ORDER[0] else w, "sg", "c%d" % q, q == ORDER[0], q == LATE)
+            else:
+                mm("psa", w, "sg" if q else "fs", "c%d" % q, q == 0, q == 2)
+            if q != LATE:
+                n, pieces = FOLD[q]
+                for h in range(2):
+                    for i in range(pieces):
+                        mm(bank(q, h), n, "w%d" % h, "c%d" % q, i == 0, i == pieces - 1, ra=n * i)
 
         mask_psum("sm", "pd0", 0, H)
+        if first:
+            quant("c4", 128, "ct4", 128)
         hold("swf", "sm", H)
         mask_psum("sm", "pd1", H, H)
-        for e in (3, 2):
-            compare(LAST - 1, e, 5 + e)
+        compare(4, 3, 12)
         scan(B("swf", H), B("nmk", H), B("sm", H), OP.mult, OP.add)
-        for e in (1, 0):
-            compare(LAST - 1, e, 5 + e)
         signs(0)
-        for e in (3, 2, 1, 0):
-            compare(LAST, e, 1 + e)
-        quant("c%d" % (LAST - 1), 128, "ct%d" % (LAST - 1))
-        if first:
-            quant("fs", 128, "fst")
-            quant("sg", 128, "sgt")
-        quant("c%d" % LAST, 128, "ct%d" % LAST)
-        for q, (w, slots) in enumerate(TILES[:LATE + 1]):
+        for e in (2, 1, 0):
+            compare(4, e, 9 + e)
+        for n in range(1, len(ORDER)):
+            q = ORDER[n]
+            slots = TILES[q][1]
             order = [e for e in (3, 2, 1, 0) if slots[e] not in BYSIGN] + [e for e in (3, 2, 1, 0) if slots[e] in BYSIGN]
-            signs(q + 1)
+            if q < 3:
+                signs(q + 1)
+            if n > 1:
+                rows(ORDER[n - 2])
             for e in order:
                 k = slots[e]
                 if k == "d":
-                    tt(B("ct0", 0, 4 * C, 4), B("pss", 0, C), B("swf"), OP.is_le)
+                    tt(B("ct0", e, 4 * C, 4), B("pss", 0, C), B("swf"), OP.is_le)
                 else:
                     compare(q, e, k)
-                if q and e == order[0]:
-                    summed(q - 1)
+                if e == order[0]:
+                    if first and n == 1:
+                        quant("sg", 128, "sgt")
+                    if first and q == 1:
+                        quant("fs", 128, "fst")
+                    summed(ORDER[n - 1])
                 if q == 1 and e == order[1]:
-                    scan(B("fsum"), B("nmk"), B("ct0", 0, 4 * C, 4), OP.mult, OP.add)
+                    scan(B("fsum"), B("nmk"), B("ct0", 3, 4 * C, 4), OP.mult, OP.add)
         mask_psum("em", "psa", 0, C)
         summed(LATE)
+        rows(ORDER[-2])
         hold("ef", "em")
         if first:
             for e in range(4):
                 a = 64 * (e // 2)
                 act(B("rtt", e, 4 * 176, 4), B("unit", a, a + 176))
         unit_tile(0)
-        if first:
-            mask("farm", B("far"), M)
-            sc(B("jw"), B("k16"), B("pm"), OP.add, -0.5, OP.add)
         tt(B("zd"), last16("ef"), last16("fsum"), OP.subtract)
         mask_psum("em2", "psr", 0, LOW)
+        sc(B("rph", 2, 14), B("rp", 2, 14), ROUND512, OP.add, -ROUND512, OP.add)
         if first:
+            mask("farm", B("far"), M)
+        hold("ef2", "em2", LOW)
+        act(B("rs", 6, 29, 2), B("rph", 2, 14), scale=1.0 / 512)
+        tt(B("rs", 5, 28, 2), B("rp", 2, 14), B("rph", 2, 14), OP.subtract)
+        tt(B("zd", 0, LOW // 16), last16("ef2", LOW), B("zd", 0, LOW // 16), OP.add)
+        unit_tile(1)
+        tt(B("z"), B("zd"), B("rs", 0, NS), OP.add)
+        for b in (0, 1):
+            act(B("t%d" % b), B("pd%d" % b, 0, C))
+        if first:
+            quant("rt", 176, "rtt")
+        sc(B("dg", 0, 224, 8), B("z"), ROUND16, OP.add, -ROUND16, OP.add)
+        sc(B("dg", 6, 224, 8), B("z"), ROUND16, OP.add, -ROUND16, OP.add)
+        sc(B("offq"), B("z"), B("base"), OP.add)
+        tt(B("dg", 1, 224, 8), B("z"), B("dg", 0, 224, 8), OP.subtract)
+        tt(B("dg", 7, 224, 8), B("z"), B("dg", 0, 224, 8), OP.subtract)
+        if first:
+            sc(B("jw"), B("k16"), B("pm"), OP.add, -0.5, OP.add)
             sc(B("amp"), B("farm"), 1.0, OP.max)
-            sc(B("kc"), B("jw"), -1.0 / 512, OP.mult)
+        quant("dg", 128, "dg")
+        if first:
             for k in range(MS):
                 sel(B("cc", EQ[k] + 16 * k, EQ[k] + 16 * k + 16), B("amp", 16 * k, 16 * k + 16), [[0, 16]], OP.is_ge, 0, 0)
             iota(B("cc", 0, EQ[6], 96), [[0, 6]], 0, 0)
             iota(B("cc", EQ[6], EQ[MS], 192), [[0, 6]], 0, 0)
             dma("g", T["vt"][:, :], T.v[:, :], [B("vt")], [])
-        tt(B("z"), B("zd"), B("rs"), OP.add)
-        hold("ef2", "em2", LOW)
-        unit_tile(1)
-        tt(B("z", 0, LOW // 16), last16("ef2", LOW), B("z", 0, LOW // 16), OP.add)
-        for b in (0, 1):
-            act(B("t%d" % b), B("pd%d" % b, 0, C))
-        if first:
-            quant("rt", 176, "rtt")
-        sc(B("dg", 0, 112, 4), B("z"), ROUND16, OP.add, -ROUND16, OP.add)
-        sc(B("dg", 114, 224, 4), B("z"), ROUND16, OP.add, -ROUND16, OP.add)
-        sc(B("offq"), B("z"), B("base"), OP.add)
-        tt(B("dg", 1, 112, 4), B("z"), B("dg", 0, 112, 4), OP.subtract)
-        tt(B("dg", 115, 224, 4), B("z"), B("dg", 0, 112, 4), OP.subtract)
-        if first:
-            quant("on", 128, "ont")
-        quant("dg", 128, "dg")
         for n, bank in ((2, "psm"), (3, "psr"), (1, "pss"), (0, "psa")):
             mm(bank, 128, "rt", "dg", la=16 * n)
 
@@ -447,51 +471,58 @@ def rank_program(g, core, T, topo):
         by_place(0)
         act(B("qs"), B("psm", 0, 56))
         act(B("l2"), B("psr", 0, 56))
-        tt(B("lo"), B("pss", 0, 56), B("qs"), OP.min)
-        tt(B("hi"), B("pss", 0, 56), B("qs"), OP.max)
-        tt(B("l3"), B("psa", 0, 56), B("l2"), OP.min)
-        tt(B("h2"), B("psa", 0, 56), B("l2"), OP.max)
-        unit_tile(2)
-        tt(B("s1"), B("lo"), B("l3"), OP.min)
-        tt(B("s4"), B("hi"), B("h2"), OP.max)
-        tt(lo("gy"), lo("hi"), lo("l2"), OP.min)
-        unit_tile(3)
-        tt(B("mn"), lo("s1"), hi("s1"), OP.min)
-        tt(B("mxv"), lo("s4"), hi("s4"), OP.max)
-        tt(hi("gy"), hi("hi"), hi("h2"), OP.min)
-        tt(B("gx"), hi("lo"), hi("l3"), OP.max)
-        tt(B("spr"), B("mxv"), B("mn"), OP.subtract)
-        tt(B("n1"), lo("lo"), lo("l2"), OP.min)
-        tt(B("n2"), lo("hi"), lo("l2"), OP.max)
+        tt(B("lo", 0, 112, 2), B("pss", 0, 56), B("qs"), OP.min)
+        tt(B("hi", 0, 112, 2), B("pss", 0, 56), B("qs"), OP.max)
+        tt(B("lo", 1, 112, 2), B("psa", 0, 56), B("l2"), OP.min)
+        tt(B("hi", 1, 112, 2), B("psa", 0, 56), B("l2"), OP.max)
+        if first:
+            sc(B("kc"), B("jw"), -1.0 / 512, OP.mult)
+        a3 = B("l2", 0, 56, 2)
+        tt(B("gya"), four("hi", 0), a3, OP.min)
+        scan(B("mn"), B("up"), B("lo"), OP.add, OP.min)
+        scan(B("mxv"), B("down"), B("hi"), OP.add, OP.max)
+        tt(B("gyb"), four("hi", 2), four("hi", 3), OP.min)
+        tt(B("gx"), four("lo", 2), four("lo", 3), OP.max)
+        tt(B("spr"), four("mxv", 3), four("mn", 3), OP.subtract)
+        tt(B("n1"), four("lo", 0), a3, OP.min)
+        tt(B("n2"), four("hi", 0), a3, OP.max)
         sc(B("offs"), B("spr"), 0.0, OP.add)
         tt(B("kw"), B("spr"), B("kc"), OP.add)
-        tt(lo("s3"), lo("lo"), lo("gy"), OP.max)
-        for b in (2, 3):
-            act(B("t%d" % b), B("pd%d" % b, 0, C))
+        tt(B("b1"), four("lo", 2), four("lo", 3), OP.min)
+        if not first:
+            for b in (2, 3):
+                unit_tile(b)
+                act(B("t%d" % b), B("pd%d" % b, 0, C))
         for h in range(2):
             tt(B("ka", H * h, H * h + H), I(B("iot512"), B("offs", HS * h, HS * h + HS)), B("kca", H * h, H * h + H), OP.add)
         act(B("kf"), I(B("kw"), B("offe", 0, 1)), scale=512.0)
         for h in range(2):
             for e in range(4):
                 act(B("cr", 4 * H * h + e, 4 * H * (h + 1), 4), B("ka", H * h, H * h + H), AF.Sign, scale=-1.0, bias=B("kf", e, e + 1))
-        tt(hi("s3"), B("gx"), hi("gy"), OP.max)
-        tt(B("b2"), B("gx"), hi("gy"), OP.min)
-        tt(B("m1"), B("n2"), hi("s1"), OP.max)
-        tt(B("m3"), B("n1"), hi("s3"), OP.max)
-        tt(B("m2"), lo("s3"), B("b2"), OP.max)
-        tt(B("m4"), B("m1"), hi("s4"), OP.min)
-        tt(B("m5"), B("m2"), B("m3"), OP.min)
+        tt(B("b3"), B("gx"), B("gyb"), OP.max)
+        tt(B("a2"), four("lo", 0), B("gya"), OP.max)
+        tt(B("b2"), B("gx"), B("gyb"), OP.min)
+        tt(four("mm", 0), B("n2"), B("b1"), OP.max)
+        tt(four("mm", 3), four("hi", 2), four("hi", 3), OP.max)
+        tt(four("mm", 2), B("n1"), B("b3"), OP.max)
+        tt(four("mm", 1), B("a2"), B("b2"), OP.max)
+        if first:
+            quant("on", 128, "ont")
         by_place(1)
-        tt(B("med"), B("m4"), B("m5"), OP.min)
+        scan(B("med"), B("up"), B("mm"), OP.add, OP.min)
         quant("cr", H, "cr")
         mm("psr", H, "on", "cr")
-        sc(B("offt"), B("med"), B("base"), OP.add)
+        sc(B("offt"), four("med", 3), B("base"), OP.add)
         act(B("la"), I(B("ot"), B("offt")))
-        if t < 2:
-            zeros(x, 4 * (C + DENSE), 4 * WIDE)
+        if first:
+            unit_tile(2)
+            act(B("t2"), B("pd2", 0, C))
         quant("cr", H, "cr", H)
         mm("psa", H, "on", "cr", ra=H)
         mask_psum("rm", "psr", 0, H)
+        if first:
+            unit_tile(3)
+            act(B("t3"), B("pd3", 0, C))
         mask_psum("rm", "psa", H, H)
         mask("lm", B("la"))
         hold("rf", "rm")
@@ -523,13 +554,13 @@ def rank_program(g, core, T, topo):
             scan(B("df", EQ[k0], EQ[k1]), B("cc", EQ[k0], EQ[k1]), B("eqo", EQ[k0], EQ[k1]), OP.mult, OP.max)
 
         same(6, 8)
-        vcopy(B("zt", 0, 4 * M, 4), I(B("t0"), B("offk")))
-        for b in (1, 2, 3):
-            act(B("zt", b, 4 * M, 4), I(B("t%d" % b), B("offk")))
+        for b in range(4):
+            (act if b % 2 else vcopy)(B("zt", b, 4 * M, 4), I(B("t%d" % b), B("offk")))
         act(B("lk2"), last16("lkf", M), AF.Identity, bias=226.0)
         picked(EARLY, NS)
-        same(8, MS)
-        same(0, 2)
+        if t < 2:
+            zeros(x, 4 * (C + DENSE), 4 * WIDE)
+        same(8, 10)
         quant(n_z, M, "zt")
         to = T.cores[(rank + 1 + t) % len(T.cores)]
         rid, pid, _se = topo.addr(to)
@@ -540,7 +571,8 @@ def rank_program(g, core, T, topo):
         for view, es in ((lambda n: T["q" + n][:, 0:M].bitcast(dt.uint8), wide), (lambda n: T["s" + n][:, 0:M], thin)):
             g.remote_dma(view(n_a), view(n_z), T.sem["arr%d" % t], T.sem["snd%d" % t], pid, rid, sum(1 << e for e in es))
         add(EARLY, NS)
-        same(2, 6)
+        same(10, MS)
+        same(0, 6)
         seen(6, MS)
         seen(0, 6)
         if t == R - 1:
@@ -552,8 +584,10 @@ def rank_program(g, core, T, topo):
             quant("v", 128, "vt")
         sc(B("offd"), B("d1"), -2.0, OP.add)
         vcopy(I(B("st"), B("offd")), B("kv"))
-        mask("stm", B("st", 0, C))
-        hold("stf", "stm")
+        for a in (0, H):
+            scan(B("stm", a, a + H), B("st", a, a + H), B("mk", 0, H), OP.add, OP.mult)
+        for a in (0, H):
+            scan(B("stf", a, a + H), B("nmk", 0, H), B("stm", a, a + H), OP.mult, OP.add)
         for b in (1, 0, 3, 2):
             sc(B("offx", NS * b, NS * b + NS), last16("stf"), 4.0, OP.mult, 1024.0 + b, OP.add)
         wait("t", "arr%d" % t, got)

import math
from concourse.mybir import dt, AluOpType, ActivationFunctionType

C, M, R, NS, MS = 448, 192, 3, 28, 12
H, HS = C // 2, NS // 2
ROUND16 = 201326592.0
TILES = [(448, (25, 26, 27, "d")), (384, (21, 22, 23, 24)), (320, (17, 18, 19, 20)), (256, (13, 14, 15, 16)),
         (192, (9, 10, 11, 12)), (128, (5, 6, 7, 8)), (128, (1, 2, 3, 4))]
LAST = len(TILES) - 1
ORDER = (4, 5, 0, 1, 2, 3, 6)
FOLD = [(224, 2), (128, 3), (160, 2), (128, 2), (192, 1), (128, 1)]
ROUND512 = 6442450944.0
LATE, LOW = 6, 256
DENSE = 65
WIDE = C + DENSE + 2 * (M - DENSE)
BYSIGN = (27, 26, 25, 24, 23, 22, 21, 19, 18, 17, 15, 14, 13)
EQ = [96 * k for k in range(6)] + [576 + 192 * k for k in range(7)]
HS_ = 3
EARLY = 18
OP = AluOpType
AF = ActivationFunctionType

SCRATCH = {}
ALIAS = {}


def _sb(name, n, d):
    SCRATCH[name] = ("sbuf", [128, n], d)


def _mx(name, n):
    _sb("q" + name, n, "float8_e4m3fn_x4")
    _sb("s" + name, n, "uint8")


def _pack(buf, d, parts):
    at = 0
    for n, w in parts:
        ALIAS[n] = (buf, at, w)
        at += (w + 15) // 16 * 16
    _sb(buf, at, d)


def _packmx(buf, parts):
    at = 0
    for n, w in parts:
        ALIAS["q" + n] = ("q" + buf, at, w)
        ALIAS["s" + n] = ("s" + buf, at, w)
        at += w
    _mx(buf, at)


for _n in ("xa", "xb"):
    _sb(_n, 4 * WIDE, "bfloat16")
for _n, _w in (("cr", 4 * C), ("tl", 4 * C), ("zt", 4 * M), ("ut", 512), ("vt", 512), ("dg", 512)):
    _sb(_n, _w, "bfloat16")
_pack("kt", "bfloat16", [("ones", 528), ("grp", 128), ("grp0", 128), ("unit", 256), ("sgt", 512), ("fst", 512), ("rtt", 4 * 176), ("ont", 512), ("et", 528), ("wt", 528)])
_pack("tb", "bfloat16", [("t%d" % b, C) for b in range(4)])
ROOM = [LOW if q == ORDER[0] else TILES[q][0] for q in range(len(TILES))]
_pack("ctb", "bfloat16", [("ct%d" % q, 4 * ROOM[q]) for q in range(len(TILES))])
_pack("kb", "bfloat16", [("mk", C), ("nmk", C), ("i16", C), ("iotaj", C), ("far", M), ("farm", M), ("amp", M), ("cc", EQ[MS]), ("kv", M),
                         ("big", 112), ("up", 112), ("down", 112)])
_pack("sgn", "bfloat16", [("sgn%d" % k, 16 * k) for k in BYSIGN])
_packmx("k", [("e0", 128), ("e1", 128), ("e2", 128), ("e3", 128), ("sg", 128), ("fs", 128), ("on", 128), ("rt", 176), ("w0", 128), ("w1", 128)])
_packmx("c", [("c%d" % q, ROOM[q]) for q in range(len(TILES))])
for _n, _w in (("u", 128), ("ux", 128), ("v", 128), ("w", 512), ("x", C), ("dg", 128), ("cr", C)):
    _mx(_n, _w)
for _t in range(R):
    _mx("z%d" % _t, M)
    _mx("a%d" % _t, M)
for _n, _w in (("junk0", C), ("junk1", C), ("junk2", C), ("ot", C), ("la", C), ("lm", C), ("lf", C), ("lk", C), ("lkm", M), ("lkf", M),
               ("df", EQ[MS]), ("eqo", EQ[MS]), ("st", 2048), ("stm", C), ("stf", C), ("em", C), ("fsum", C), ("ef", C), ("em2", LOW), ("ef2", LOW), ("rm", C), ("rf", C)):
    _sb(_n, _w, "bfloat16")
for _n, _w in (("sm", C), ("swf", C), ("iot512", C), ("kca", C), ("ka", C), ("yo", C), ("olf", C), ("junkf", C)):
    _sb(_n, _w, "float32")
_pack("fk", "float32", [("pm", 1), ("pg", 1), ("p3", 1), ("base", 1), ("k16", NS), ("kc", NS), ("jw", NS)])
_pack("fw", "float32", [("rs", 32), ("z", NS), ("zd", NS), ("rp", 16), ("rph", 16), ("kw", NS), ("kf", 16), ("qs", 56), ("l2", 56),
                        ("spr", NS), ("lk2", MS), ("d1", MS)] + [(n, NS) for n in ("gya", "gyb", "gx", "n1", "n2", "a2", "b1", "b2", "b3")])
_pack("bw", "bfloat16", [(n, 112) for n in ("lo", "hi", "mn", "mxv", "mm", "med")])
_pack("ki", "int32", [("ip", 1), ("ia", 1), ("ib", 1), ("ic", 1), ("if2", 8)])
for _n, _w in (("offu", 8), ("offe", 2), ("offq", NS), ("offt", NS), ("offs", NS), ("offr", NS), ("offk", MS), ("offl", NS), ("offd", MS), ("offx", 4 * NS)):
    _sb(_n, _w, "uint16")
for _n in ("pss", "psa", "psm", "psr", "pd0", "pd1", "pd2", "pd3"):
    SCRATCH[_n] = ("psum", [128, 512], "float32")

SEMAPHORES = ["sv", "ss", "sg", "st"] + ["arr%d" % t for t in range(R)] + ["snd%d" % t for t in range(R)] + ["d%d" % i for i in range(32)]


def make_queues(g, T):
    eng = {"v": g.vector, "s": g.scalar, "g": g, "t": g.tensor, "y": g.sync}
    sem = {"v": "sv", "s": "ss", "g": "sg", "t": "st"}
    count = {k: 0 for k in sem}
    known = {k: {} for k in eng}
    snap = {}
    log = {}
    ndma = [0]

    def psum(v):
        return SCRATCH[v[0]][0] == "psum"

    def region(v):
        return (0, 512, 1) if psum(v) else (v[1], v[2], v[3])

    def hit(p, q):
        if p[0] >= q[1] or q[0] >= p[1]:
            return False
        return (p[0] - q[0]) % math.gcd(p[2], q[2]) == 0

    def wait(e, src, n):
        if known[e].get(src, 0) >= n:
            return
        eng[e].wait_ge(T.sem[sem.get(src, src)], n)
        known[e][src] = n
        for k, m in snap.get((src, n), {}).items():
            if known[e].get(k, 0) < m:
                known[e][k] = m

    def deps(e, outs, ins):
        need = {}
        for write, vs in ((True, outs), (False, ins)):
            for v in vs:
                r = region(v)
                for w2, r2, src, n in log.get(v[0], []):
                    if not hit(r, r2) or (e == "t" and src == "t"):
                        continue
                    if write or w2 or (psum(v) and src != e):
                        need[src] = max(need.get(src, 0), n)
        for src in sorted(need):
            wait(e, src, need[src])

    def record(outs, ins, src, n):
        for write, vs in ((True, outs), (False, ins)):
            for v in vs:
                r = region(v)
                L = log.setdefault(v[0], [])
                if write and not psum(v) and r[2] == 1:
                    L[:] = [x for x in L if not (r[0] <= x[1][0] and x[1][1] <= r[1])]
                L[:] = [x for x in L if not (x[0] == write and x[1] == r and x[2] == src)]
                L.append((write, r, src, n))

    def ap(v):
        x = T[v[0]][:, v[1]:v[2]:v[3]] if v[3] > 1 else T[v[0]][:, v[1]:v[2]]
        if len(v) > 4:
            if v[5] == "codes":
                x = x.bitcast(dt.uint32)
            if v[4] is not None:
                o = v[4]
                x = x.indirect(T[o[0]][:, o[1]:o[2]])
        return x

    def issue(e, outs, ins, call):
        deps(e, outs, ins)
        count[e] += 1
        call().then_inc(T.sem[sem[e]], 1)
        snap[(e, count[e])] = dict(known[e])
        record(outs, ins, e, count[e])

    def dma(e, out, in_, outs, ins, **kw):
        deps(e, outs, ins)
        name = "d%d" % ndma[0]
        ndma[0] += 1
        snap[(name, 16)] = dict(known[e])
        eng[e].dma_start(out, in_, **kw).then_inc(T.sem[name], 16)
        record(outs, ins, name, 16)

    def finish():
        for i in range(ndma[0]):
            wait("g", "d%d" % i, 16)
        for k in ("v", "s", "t", "g"):
            wait("g", k, count[k])

    return issue, dma, ap, wait, deps, finish


def rank_program(g, core, T, topo):
    rank = T.rank_of(core)
    if rank is None:
        return
    issue, dma, ap, wait, deps, finish = make_queues(g, T)

    def B(name, a=0, b=None, s=1):
        if name in ALIAS:
            buf, at, w = ALIAS[name]
        else:
            buf, at, w = name, 0, SCRATCH[name][1][1]
        return (buf, at + a, at + (w if b is None else b), s)

    def I(v, off, kind=""):
        return v + (off, kind)

    def srcs(*vs):
        r = []
        for v in vs:
            r.append(v)
            if len(v) > 4 and v[4] is not None:
                r.append(v[4])
        return r

    def tt(out, a, b, op):
        issue("v", [out], srcs(a, b), lambda: g.vector.tensor_tensor(ap(out), ap(a), ap(b), op))

    def sc(out, a, s1, op0, s2=None, op1=None):
        ins = srcs(a) + ([s1] if isinstance(s1, tuple) else [])
        x1 = ap(s1) if isinstance(s1, tuple) else s1
        if op1 is None:
            issue("v", [out], ins, lambda: g.vector.tensor_scalar(ap(out), ap(a), x1, None, op0))
        else:
            issue("v", [out], ins, lambda: g.vector.tensor_scalar(ap(out), ap(a), x1, s2, op0, op1))

    def scan(out, d0, d1, op0, op1, init=None):
        issue("v", [out], [d0, d1] + ([init] if init else []),
              lambda: g.vector.tensor_tensor_scan(ap(out), ap(d0), ap(d1), ap(init) if init else 0.0, op0, op1))

    def vcopy(out, a):
        ins = srcs(a) + ([out[4]] if len(out) > 4 and out[4] is not None else [])
        issue("v", [out], ins, lambda: g.vector.tensor_copy(ap(out), ap(a)))

    def act(out, a, func=AF.Copy, scale=None, bias=None, acc=None):
        kw = {}
        ins, outs = srcs(a), [out]
        for k, v in (("scale", scale), ("bias", bias)):
            if v is not None:
                kw[k] = ap(v) if isinstance(v, tuple) else v
                if isinstance(v, tuple):
                    ins.append(v)
        if acc is not None:
            kw["accum_out"] = ap(acc)
            outs.append(acc)
        issue("s", outs, ins, lambda: g.scalar.activation(ap(out), ap(a), func, **kw))

    nj = [0]

    def row_sum(acc, v, n):
        nj[0] = (nj[0] + 1) % 3
        act(B("junk%d" % nj[0], 0, n), v, acc=acc)

    def fill(v, c):
        issue("v", [v], [], lambda: g.vector.memset(ap(v), c))

    def quant(name, n, tile, a=0, shift=0):
        src, o, s = B(tile, 4 * a + shift, 4 * (a + n) + shift), B("q" + name, a, a + n), B("s" + name, a, a + n)
        issue("v", [o, s], [src], lambda: g.vector.quantize_mx(ap(o), ap(s), ap(src)))

    def mm(out, n, l, r, start=True, stop=True, la=0, ra=0):
        o = B(out, 0, n)
        a, asc, b, bsc = B("q" + l, la, la + 128), B("s" + l, la, la + 128), B("q" + r, ra, ra + n), B("s" + r, ra, ra + n)
        issue("t", [o], [a, asc, b, bsc], lambda: g.tensor.matmul_mx(ap(o), ap(a), ap(asc), ap(b), ap(bsc), start, stop))

    def iota(v, pattern, base, cm):
        kw = {} if SCRATCH[v[0]][2] == "int32" else {"allow_small_or_imprecise_dtypes": True}
        issue("g", [v], [], lambda: g.iota(ap(v), pattern, base, cm, **kw))

    def sel(out, in_, pattern, op, base, cm):
        issue("g", [out], [in_], lambda: g.affine_select(ap(out), ap(in_), pattern, op, 0.0, base, cm))

    def last16(name, n=C):
        return B(name, 15, n, 16)

    def mask(out, v, n=C):
        scan(B(out, 0, n), v, B("mk", 0, n), OP.add, OP.mult)

    def mask_psum(out, bank, a, n):
        tt(B(out, a, a + n), B(bank, 0, n), B("mk", 0, n), OP.mult)

    def hold(out, m, n=C):
        scan(B(out, 0, n), B("nmk", 0, n), B(m, 0, n), OP.mult, OP.add)

    def zeros(n, a, b):
        for c in range(a, b, 512):
            act(B(n, c, min(c + 512, b)), B("ones", 0, min(512, b - c)), scale=0.0)

    def four(n, a):
        return B(n, a, 112, 4)

    dma("s", T["ut"][:, :], T.u[:, :], [B("ut")], [])
    for h in range(2):
        a, b = 4 * H * h, 4 * H * (h + 1)
        dma("y", T["xa"][:, a:b], T.x[:, a:b], [B("xa", a, b)], [])
    deps("y", [], [B("xa", 0, 4 * C)])
    dma("y", T["qw"][:, 0:512].bitcast(dt.uint8), T.wc[:, :], [B("qw")], [])
    dma("y", T["sw"][:, :], T.ws[:, :], [B("sw")], [])

    iota(B("if2"), [[16, 8]], 0, 0)
    iota(B("ip"), [[0, 1]], 0, 1)
    fill(B("ones"), 1.0)
    iota(B("i16"), [[0, NS], [1, 16]], 0, 0)
    sel(B("unit"), B("ones", 0, 256), [[0, 2], [-1, 128]], OP.is_equal, 0, 1)
    sel(B("grp0"), B("ones", 0, 128), [[-16, 8], [0, 16]], OP.is_ge, 0, 1)
    sel(B("grp"), B("grp0"), [[16, 8], [0, 16]], OP.is_ge, 15, -1)
    sel(B("fst", 3, 512, 4), B("grp"), [[1, 128]], OP.is_gt, 0, -1)
    zeros("ct4", 512, 1024)
    zeros("ct5", 320, 512)
    zeros("wt", 0, 516)
    for q in range(4):
        w = TILES[q][0]
        iota(B("ct%d" % q, 4 * w - 192, 4 * w), [[0, 192]], 0, 0)
    fill(B("rs", 0, 1), 0.0)
    vcopy(B("offu"), B("if2"))
    sc(B("ia"), B("ip"), 15, OP.bitwise_and)
    sc(B("ib"), B("ip"), 4, OP.arith_shift_right)
    sc(B("ic"), B("ip"), 3, OP.bitwise_and)
    vcopy(B("pm"), B("ia"))
    vcopy(B("pg"), B("ib"))
    sc(B("p3"), B("ic"), 8.0, OP.mult)
    sc(B("offe", 0, 1), B("p3"), B("pg"), OP.add, float(NS - 1), OP.min)
    sc(B("base"), B("pm"), -1.0, OP.mult, 232.0, OP.add)
    sc(B("mk"), B("i16"), B("pm"), OP.is_equal)
    quant("u", 128, "ut")
    sc(B("nmk"), B("i16"), B("pm"), OP.not_equal)
    vcopy(I(B("qux"), None, "codes"), I(B("qu"), B("offu"), "codes"))
    act(B("sux"), I(B("su"), B("offu")))
    act(B("wt", 2, 514, 4), B("unit", 0, 128))
    act(B("wt", 3, 515, 4), B("unit", 0, 128), scale=512.0)
    for e in range(4):
        act(B("sgt", e, 512, 4), B("grp"), scale=-1.0)
    for e in range(3):
        act(B("fst", e, 512, 4), B("grp"), scale=-1.0)
    for h in range(2):
        quant("x", H, "xa", H * h)
    for h in range(2):
        quant("w%d" % h, 128, "wt", shift=2 - 2 * h)
    iota(B("k16"), [[16, NS]], 0, 0)
    iota(B("far"), [[8, M]], 512, 0)

    iota(B("ct%d" % LAST), [[0, 512]], 0, 0)
    sel(B("et", 0, 516), B("ones", 0, 516), [[-1, 516]], OP.is_equal, 3, 4)
    iota(B("dg"), [[0, 512]], 0, 0)
    for n, c in (("up", 1024), ("down", -1024)):
        iota(B("big"), [[0, 112]], c, 0)
        sel(B(n), B("big"), [[0, NS], [1, 4]], OP.is_equal, 0, 0)
    iota(B("iotaj"), [[1, C]], -224, 0)
    iota(B("iot512"), [[512, C]], 0, 0)
    iota(B("kca"), [[-1, C]], 0, 0)
    sel(B("ont"), B("ones", 0, 512), [[0, 128], [-1000, 4]], OP.is_gt, 3064, -1)
    for a in range(0, EQ[MS], 432):
        for n, src in (("cc", "ones"), ("eqo", "ct%d" % LAST)):
            o, i = B(n, a, a + 432), B(src, 0, 432)
            dma("y", ap(o), ap(i), [o], [i])
    iota(B("kv", 0, DENSE), [[1, DENSE]], C - 256, 0)
    iota(B("kv", DENSE, M), [[2, M - DENSE]], C + DENSE + 1 - 256, 0)

    X = ["xa", "xb"]
    for t in range(R):
        x, xn = X[t % 2], X[(t + 1) % 2]
        first = t == 0

        def unit_tile(b):
            if first:
                quant("e%d" % b, 128, "et", shift=3 - b)
            mm("pd%d" % b, C, "e%d" % b, "x")

        mm("pd0", H, "ux", "x")
        mm("pd1", H, "ux", "x", ra=H)
        mm("pss", C, "ux", "x")
        mm("psm", C, "ux", "x")
        iota(B("st", 0, C), [[1, C]], -256, 0)

        def signs(q):
            for k in reversed(TILES[q][1]):
                if k in BYSIGN:
                    act(B("sgn%d" % k), B("psm", 0, 16 * k), AF.Sign, scale=-1.0, bias=B("swf", 16 * k + 15, 16 * k + 16))

        def compare(q, e, k):
            c = B("ct%d" % q, e, 64 * k, 4)
            if k in BYSIGN:
                sc(c, B("sgn%d" % k), 0.0, OP.is_le, -0.5, OP.add)
            else:
                sc(c, B("pd0" if q in ORDER[:2] else "pss", 0, 16 * k), B("swf", 16 * k + 15, 16 * k + 16), OP.is_ge, -0.5, OP.add)
            if q == LATE:
                row_sum(B("rs", k, k + 1), c, 16 * k)

        def bank(q, h):
            return ("pd2", "pd3", "pd1", "pd0")[(2 * ORDER.index(q) + h) % 4]

        def rows(q):
            n = FOLD[q][0]
            for h in range(2):
                k = TILES[q][1][2 * h] // 2
                act(B("junkf", H * h, H * h + n), B(bank(q, h), 0, n), acc=B("rp", k, k + 1))

        def summed(q):
            w = TILES[q][0]
            quant("c%d" % q, w, "ct%d" % q)
            if q > 2:
                mm("psr", LOW if q == ORDER[0] else w, "sg", "c%d" % q, q == ORDER[0], q == LATE)
            else:
                mm("psa", w, "sg" if q else "fs", "c%d" % q, q == 0, q == 2)
            if q != LATE:
                n, pieces = FOLD[q]
                for h in range(2):
                    for i in range(pieces):
                        mm(bank(q, h), n, "w%d" % h, "c%d" % q, i == 0, i == pieces - 1, ra=n * i)

        mask_psum("sm", "pd0", 0, H)
        if first:
            quant("c4", 128, "ct4", 128)
        hold("swf", "sm", H)
        mask_psum("sm", "pd1", H, H)
        compare(4, 3, 12)
        scan(B("swf", H), B("nmk", H), B("sm", H), OP.mult, OP.add)
        signs(0)
        for e in (2, 1, 0):
            compare(4, e, 9 + e)
        for n in range(1, len(ORDER)):
            q = ORDER[n]
            slots = TILES[q][1]
            order = [e for e in (3, 2, 1, 0) if slots[e] not in BYSIGN] + [e for e in (3, 2, 1, 0) if slots[e] in BYSIGN]
            if q < 3:
                signs(q + 1)
            if n > 1:
                rows(ORDER[n - 2])
            for e in order:
                k = slots[e]
                if k == "d":
                    tt(B("ct0", e, 4 * C, 4), B("pss", 0, C), B("swf"), OP.is_le)
                else:
                    compare(q, e, k)
                if e == order[0]:
                    if first and n == 1:
                        quant("sg", 128, "sgt")
                    if first and q == 1:
                        quant("fs", 128, "fst")
                    summed(ORDER[n - 1])
                if q == 1 and e == order[1]:
                    scan(B("fsum"), B("nmk"), B("ct0", 3, 4 * C, 4), OP.mult, OP.add)
        mask_psum("em", "psa", 0, C)
        summed(LATE)
        rows(ORDER[-2])
        hold("ef", "em")
        if first:
            for e in range(4):
                a = 64 * (e // 2)
                act(B("rtt", e, 4 * 176, 4), B("unit", a, a + 176))
        unit_tile(0)
        tt(B("zd"), last16("ef"), last16("fsum"), OP.subtract)
        mask_psum("em2", "psr", 0, LOW)
        sc(B("rph", 2, 14), B("rp", 2, 14), ROUND512, OP.add, -ROUND512, OP.add)
        if first:
            mask("farm", B("far"), M)
        hold("ef2", "em2", LOW)
        act(B("rs", 6, 29, 2), B("rph", 2, 14), scale=1.0 / 512)
        tt(B("rs", 5, 28, 2), B("rp", 2, 14), B("rph", 2, 14), OP.subtract)
        tt(B("zd", 0, LOW // 16), last16("ef2", LOW), B("zd", 0, LOW // 16), OP.add)
        unit_tile(1)
        tt(B("z"), B("zd"), B("rs", 0, NS), OP.add)
        for b in (0, 1):
            act(B("t%d" % b), B("pd%d" % b, 0, C))
        if first:
            quant("rt", 176, "rtt")
        sc(B("dg", 0, 224, 8), B("z"), ROUND16, OP.add, -ROUND16, OP.add)
        sc(B("dg", 6, 224, 8), B("z"), ROUND16, OP.add, -ROUND16, OP.add)
        sc(B("offq"), B("z"), B("base"), OP.add)
        tt(B("dg", 1, 224, 8), B("z"), B("dg", 0, 224, 8), OP.subtract)
        tt(B("dg", 7, 224, 8), B("z"), B("dg", 0, 224, 8), OP.subtract)
        if first:
            sc(B("jw"), B("k16"), B("pm"), OP.add, -0.5, OP.add)
            sc(B("amp"), B("farm"), 1.0, OP.max)
        quant("dg", 128, "dg")
        if first:
            for k in range(MS):
                sel(B("cc", EQ[k] + 16 * k, EQ[k] + 16 * k + 16), B("amp", 16 * k, 16 * k + 16), [[0, 16]], OP.is_ge, 0, 0)
            iota(B("cc", 0, EQ[6], 96), [[0, 6]], 0, 0)
            iota(B("cc", EQ[6], EQ[MS], 192), [[0, 6]], 0, 0)
            dma("g", T["vt"][:, :], T.v[:, :], [B("vt")], [])
        for n, bank in ((2, "psm"), (3, "psr"), (1, "pss"), (0, "psa")):
            mm(bank, 128, "rt", "dg", la=16 * n)

        def by_place(h):
            vcopy(I(B("ot"), B("offq", HS * h, HS * h + HS)), B("iotaj", H * h, H * h + H))

        by_place(0)
        act(B("qs"), B("psm", 0, 56))
        act(B("l2"), B("psr", 0, 56))
        tt(B("lo", 0, 112, 2), B("pss", 0, 56), B("qs"), OP.min)
        tt(B("hi", 0, 112, 2), B("pss", 0, 56), B("qs"), OP.max)
        tt(B("lo", 1, 112, 2), B("psa", 0, 56), B("l2"), OP.min)
        tt(B("hi", 1, 112, 2), B("psa", 0, 56), B("l2"), OP.max)
        if first:
            sc(B("kc"), B("jw"), -1.0 / 512, OP.mult)
        a3 = B("l2", 0, 56, 2)
        tt(B("gya"), four("hi", 0), a3, OP.min)
        scan(B("mn"), B("up"), B("lo"), OP.add, OP.min)
        scan(B("mxv"), B("down"), B("hi"), OP.add, OP.max)
        tt(B("gyb"), four("hi", 2), four("hi", 3), OP.min)
        tt(B("gx"), four("lo", 2), four("lo", 3), OP.max)
        tt(B("spr"), four("mxv", 3), four("mn", 3), OP.subtract)
        tt(B("n1"), four("lo", 0), a3, OP.min)
        tt(B("n2"), four("hi", 0), a3, OP.max)
        sc(B("offs"), B("spr"), 0.0, OP.add)
        tt(B("kw"), B("spr"), B("kc"), OP.add)
        tt(B("b1"), four("lo", 2), four("lo", 3), OP.min)
        if not first:
            for b in (2, 3):
                unit_tile(b)
                act(B("t%d" % b), B("pd%d" % b, 0, C))
        for h in range(2):
            tt(B("ka", H * h, H * h + H), I(B("iot512"), B("offs", HS * h, HS * h + HS)), B("kca", H * h, H * h + H), OP.add)
        act(B("kf"), I(B("kw"), B("offe", 0, 1)), scale=512.0)
        for h in range(2):
            for e in range(4):
                act(B("cr", 4 * H * h + e, 4 * H * (h + 1), 4), B("ka", H * h, H * h + H), AF.Sign, scale=-1.0, bias=B("kf", e, e + 1))
        tt(B("b3"), B("gx"), B("gyb"), OP.max)
        tt(B("a2"), four("lo", 0), B("gya"), OP.max)
        tt(B("b2"), B("gx"), B("gyb"), OP.min)
        tt(four("mm", 0), B("n2"), B("b1"), OP.max)
        tt(four("mm", 3), four("hi", 2), four("hi", 3), OP.max)
        tt(four("mm", 2), B("n1"), B("b3"), OP.max)
        tt(four("mm", 1), B("a2"), B("b2"), OP.max)
        if first:
            quant("on", 128, "ont")
        by_place(1)
        scan(B("med"), B("up"), B("mm"), OP.add, OP.min)
        quant("cr", H, "cr")
        mm("psr", H, "on", "cr")
        sc(B("offt"), four("med", 3), B("base"), OP.add)
        act(B("la"), I(B("ot"), B("offt")))
        if first:
            unit_tile(2)
            act(B("t2"), B("pd2", 0, C))
        quant("cr", H, "cr", H)
        mm("psa", H, "on", "cr", ra=H)
        mask_psum("rm", "psr", 0, H)
        if first:
            unit_tile(3)
            act(B("t3"), B("pd3", 0, C))
        mask_psum("rm", "psa", H, H)
        mask("lm", B("la"))
        hold("rf", "rm")
        hold("lf", "lm")
        sc(B("offr"), last16("rf"), 0.5, OP.mult, 223.0, OP.add)
        sc(B("offl"), last16("lf"), 224.0, OP.add)

        def picked(k0, k1):
            for b in range(4):
                act(B("tl", 64 * k0 + b, 64 * k1, 4), I(B("t%d" % b), B("offl", k0, k1)))

        def add(k0, k1):
            o, i = B(x, 64 * k0, 64 * k1), B("tl", 64 * k0, 64 * k1)
            dma("g", ap(o), ap(i), [o], [i], accum_op=OP.add)

        picked(0, EARLY)
        add(0, EARLY)
        vcopy(I(B("lk"), B("offr")), B("la"))
        mask("lkm", B("lk", 0, M), M)
        hold("lkf", "lkm", M)
        sc(B("offk"), last16("lkf", M), 224.0, OP.add)
        n_z, n_a = "z%d" % t, "a%d" % t

        def same(k0, k1):
            for k in range(k0, k1):
                sc(B("eqo", EQ[k], EQ[k] + 16 * k + 16), B("lk", 0, 16 * k + 16), B("lkf", 16 * k + 15, 16 * k + 16), OP.is_equal)

        def seen(k0, k1):
            scan(B("df", EQ[k0], EQ[k1]), B("cc", EQ[k0], EQ[k1]), B("eqo", EQ[k0], EQ[k1]), OP.mult, OP.max)

        same(6, 8)
        for b in range(4):
            (act if b % 2 else vcopy)(B("zt", b, 4 * M, 4), I(B("t%d" % b), B("offk")))
        act(B("lk2"), last16("lkf", M), AF.Identity, bias=226.0)
        picked(EARLY, NS)
        if t < 2:
            zeros(x, 4 * (C + DENSE), 4 * WIDE)
        same(8, 10)
        quant(n_z, M, "zt")
        to = T.cores[(rank + 1 + t) % len(T.cores)]
        rid, pid, _se = topo.addr(to)
        en = topo.engines(core, to)
        wide, thin = en[0::2], en[1::4]
        got = len(wide) + len(thin)
        deps("g", [], [B("q" + n_z), B("s" + n_z)])
        for view, es in ((lambda n: T["q" + n][:, 0:M].bitcast(dt.uint8), wide), (lambda n: T["s" + n][:, 0:M], thin)):
            g.remote_dma(view(n_a), view(n_z), T.sem["arr%d" % t], T.sem["snd%d" % t], pid, rid, sum(1 << e for e in es))
        add(EARLY, NS)
        same(10, MS)
        same(0, 6)
        seen(6, MS)
        seen(0, 6)
        if t == R - 1:
            act(B("olf"), B("la"), AF.Identity, bias=224.0)
            dma("y", T.ol[:, :], T["olf"][0:128:16, :], [], [B("olf")])
        tt(B("d1", 6, MS), B("df", EQ[6] + 191, EQ[MS], 192), B("lk2", 6, MS), OP.max)
        tt(B("d1", 0, 6), B("df", 95, EQ[6], 96), B("lk2", 0, 6), OP.max)
        if first:
            quant("v", 128, "vt")
        sc(B("offd"), B("d1"), -2.0, OP.add)
        vcopy(I(B("st"), B("offd")), B("kv"))
        for a in (0, H):
            scan(B("stm", a, a + H), B("st", a, a + H), B("mk", 0, H), OP.add, OP.mult)
        for a in (0, H):
            scan(B("stf", a, a + H), B("nmk", 0, H), B("stm", a, a + H), OP.mult, OP.add)
        for b in (1, 0, 3, 2):
            sc(B("offx", NS * b, NS * b + NS), last16("stf"), 4.0, OP.mult, 1024.0 + b, OP.add)
        wait("t", "arr%d" % t, got)
        for b in range(4):
            mm("pd%d" % b, M, "w", n_a, la=128 * b)
        for b in range(4):
            for o, i in ((B(x, 4 * C + b, 4 * (C + DENSE), 4), B("pd%d" % b, 0, DENSE)),
                         (B(x, 4 * (C + DENSE + 1) + b, 4 * WIDE, 8), B("pd%d" % b, DENSE, M))):
                if b < HS_:
                    act(o, i, scale=0.0625)
                else:
                    sc(o, i, 0.0625, OP.mult)

        def pick(b, h):
            o, w = B(xn, 4 * H * h + b, 4 * H * (h + 1), 4), I(B(x), B("offx", NS * b + HS * h, NS * b + HS * h + HS))
            if b % 2:
                act(o, w, scale=0.5)
            else:
                sc(o, w, 0.5, OP.mult)

        for b, h in ((0, 0), (1, 0), (2, 0), (3, 0), (0, 1), (1, 1), (3, 1)):
            pick(b, h)
        quant("x", H, xn)
        pick(2, 1)
        quant("x", H, xn, H)
    for h, bank in enumerate(("pss", "psm")):
        a, b = H * h, H * h + H
        mm(bank, H, "v", "x", ra=a)
        dma("y", T.oc[:, 4 * a:4 * b], T["qx"][:, a:b].bitcast(dt.uint8), [], [B("qx", a, b)])
        act(B("yo", a, b), B(bank, 0, H))
        dma("s", T.y[:, a:b], T["yo"][:, a:b], [], [B("yo", a, b)])
    for k in range(4):
        dma("y", T.osc[4 * k:4 * k + 4, :], T["sx"][32 * k:32 * k + 4, 0:C], [], [B("sx")])
    for t in range(R):
        wait("g", "arr%d" % t, got)
        wait("g", "snd%d" % t, got)
    finish()
